import numpy as np
import ml_dtypes


def mxq(x, axis, fmt="e4m3"):
    dtype, down = {"e4m3": (ml_dtypes.float8_e4m3fn, 7), "e5m2": (ml_dtypes.float8_e5m2, 14)}[fmt]
    v = np.moveaxis(np.asarray(x, np.float32).astype(ml_dtypes.bfloat16).astype(np.float64), axis, -1)
    blocks = v.reshape(v.shape[:-1] + (-1, 32))
    amax = np.abs(blocks).max(-1, keepdims=True)
    byte = np.maximum(np.where(amax > 0, np.frexp(amax)[1] - 1 + 127, 0) - down, 1)
    scale = np.exp2(byte - 127.0)
    codes = (blocks / scale).astype(np.float32).astype(dtype).astype(np.float64)
    return np.moveaxis((codes * scale).reshape(v.shape), -1, axis)


WIDE = False


def mx_kscale(k):
    if not WIDE:
        return np.ones(k)
    levels = np.array([10, -10, 5, -5, 0])
    if k % 512:
        return np.exp2(np.random.permutation(np.resize(levels, k // 32))).repeat(32)
    a = np.empty((k // 512, 16))
    for p in range(k // 512):
        a[p, :8] = np.random.permutation(np.resize(levels, 8))
        for g in range(8):
            far = levels[np.abs(levels - a[p, g]) >= 10]
            a[p, g + 8] = far[np.random.randint(len(far))]
    return np.exp2(a.ravel()).repeat(32)


def f64(x):
    return np.asarray(x).astype(np.float64)


def striped(idx):
    return np.tile(idx.reshape(-1, 16).T, (8, 1)).astype(np.uint16)


def unstriped(offs):
    return offs[:16].T.reshape(-1).astype(np.int64)


def striped8(idx):
    return np.concatenate([x.reshape(-1, 16).T for x in idx]).astype(np.uint16)


def runs(offs, k):
    lists = np.stack([offs[16 * r : 16 * r + 16].T.reshape(-1) for r in range(8)]).astype(np.int64)
    return lists[np.arange(k) % 512 // 64]


def pack_weight(w):
    k, n = w.shape
    w = f64(np.asarray(w, np.float32).astype(ml_dtypes.bfloat16)).reshape(k // 32, 32, n)
    amax = np.abs(w).max(1)
    byte = np.clip(np.where(amax > 0, np.frexp(amax)[1] - 1 + 127 - 7, 1), 1, 254)
    scaled = (w * np.exp2(127.0 - byte)[:, None, :]).reshape(k, n).astype(np.float32)
    words = np.ascontiguousarray(scaled.reshape(k // 512, 128, 4, n).transpose(0, 1, 3, 2)).astype(ml_dtypes.float8_e4m3fn).view(np.uint8)
    return words, np.ascontiguousarray(byte.astype(np.uint8).reshape(k // 512, 16, n))


def unpack_weight(words, scales):
    g, p, n, _ = words.shape
    vals = np.ascontiguousarray(words).view(ml_dtypes.float8_e4m3fn).astype(np.float64) * np.repeat(np.exp2(scales.astype(np.float64) - 127.0), 8, axis=1)[..., None]
    return vals.transpose(0, 1, 3, 2).reshape(g * 512, n)


def silu(v):
    return v / (1.0 + np.exp(-np.maximum(v, -700.0)))

def planes(y):
    n, m = y.shape
    v = y.astype(np.float32).astype(ml_dtypes.bfloat16).astype(np.float64).reshape(n // 32, 32, m)
    top = np.abs(v).max(1)
    byte = np.clip(np.where(top > 0, np.frexp(top)[1] - 1 + 127 - 7, 1), 1, 254)
    codes = (v * np.exp2(127.0 - byte)[:, None, :]).reshape(n, m).astype(np.float32).astype(ml_dtypes.float8_e4m3fn).view(np.uint8)
    words = codes.reshape(n // 512, 128, 4, m).transpose(0, 1, 3, 2)
    return np.ascontiguousarray(words), np.ascontiguousarray(byte.astype(np.uint8).reshape(n // 512, 16, m))


K, T, S, V, N, H = 512, 2048, 1024, 512, 512, 512


def setup_inputs():
    n = np.random.standard_normal
    s = mx_kscale(K)[:, None]
    u = mx_kscale(H)
    packed_xT = pack_weight(n((K, T)) * s)
    packed_w2 = pack_weight(n((H, N)) / np.sqrt(H) / u[:, None])
    return {
        "x_words": packed_xT[0],
        "x_scales": packed_xT[1],
        "w1": (n((K, H)) / np.sqrt(K) / s * u).astype(np.float32),
        "wa": np.repeat(np.random.uniform(0.2, 0.8, (8, V)), 64, axis=0).astype(np.float32),
        "w2_words": packed_w2[0],
        "w2_scales": packed_w2[1],
        "offs": striped(np.random.permutation(T)[:S]),
        "a1": striped8(np.stack([np.random.permutation(S)[:V] for _ in range(8)])),
        "a2": striped8(np.stack([np.random.permutation(S)[:V] for _ in range(8)])),
        "back": striped8(np.random.randint(0, V, (8, S))),
    }


def reference(x_words, x_scales, w1, wa, w2_words, w2_scales, offs, a1, a2, back):
    xq = unpack_weight(x_words, x_scales)[:, unstriped(offs)]
    y = mxq(f64(w1), 0, "e4m3").T @ xq
    q = y[np.arange(H)[:, None], runs(a2, H)]
    mg = silu(q + f64(wa) * (y[np.arange(H)[:, None], runs(a1, H)] - q))
    z = y + mg[np.arange(H)[:, None], runs(back, H)]
    out_0 = unpack_weight(w2_words, w2_scales).T @ mxq(z, 0, "e4m3")
    return (out_0,) + planes(out_0)

@@ -1,0 +1,264 @@
+from contextlib import ExitStack
+
+import concourse.mybir as mybir
+from concourse.masks import make_identity
+
+K, T, S, V, H, N = 512, 2048, 1024, 512, 512, 512
+FLOPS = 2 * K * H * S + 2 * H * N * S
+
+F32 = mybir.dt.float32
+BF16 = mybir.dt.bfloat16
+I32 = mybir.dt.int32
+U32 = mybir.dt.uint32
+U16 = mybir.dt.uint16
+U8 = mybir.dt.uint8
+FP8X4 = mybir.dt.float8_e4m3fn_x4
+ALU = mybir.AluOpType
+ACT = mybir.ActivationFunctionType
+
+P = 128
+PACK = 4
+BANK = 512
+STRIP = 128
+W1_PIECES = (256, 256)
+W1_VECTOR_COLS = 160
+FIRST_PIECES = (512, 256, 256)
+CHUNKS = (256, 256, 256, 256)
+VECTOR_ROUNDS = (2, 3, 4, 5, 6)
+FINE_STORES = 2
+VECTOR_WEAVES = (3,)
+Z_SLOTS = 3
+TENSOR_MIXES = 3
+
+
+def tile_picked_tome8_silu_po_kernel(
+    tc, x_words, x_scales, w1, wa, w2_words, w2_scales, offs, a1, a2, back, out_0, out_1, out_2
+):
+    nc = tc.nc
+    with ExitStack() as ctx:
+        keep = ctx.enter_context(tc.tile_pool(name="keep", bufs=1))
+        ring = ctx.enter_context(tc.tile_pool(name="ring", bufs=4))
+        psum = ctx.enter_context(tc.psum_pool(name="psum", bufs=6))
+        psum_mix = ctx.enter_context(tc.psum_pool(name="psum_mix", bufs=1))
+
+        def load_scale_rows(plane, rows, queue):
+            for q in range(4):
+                queue.dma_start(
+                    out=plane[32 * q : 32 * q + 4, :].bitcast(I32), in_=rows[0, 4 * q : 4 * q + 4, :].bitcast(I32)
+                )
+
+        offs_sb = keep.tile([P, S // 16], U16)
+        a1_sb = keep.tile([P, V // 16], U16)
+        a2_sb = keep.tile([P, V // 16], U16)
+        back_sb = keep.tile([P, S // 16], U16)
+
+        xs_all = keep.tile([P, T], U8, align_bytes=64)
+        nc.vector.memset(xs_all[:].bitcast(I32), 0)
+        w2s_raw = keep.tile([P, N], U8, align_bytes=64)
+        nc.vector.memset(w2s_raw[:].bitcast(I32), 0)
+        warm = keep.tile([P, 2], F32)
+        nc.gpsimd.memset(warm[:, 0:1], 0.0)
+        nc.scalar.activation(warm[:, 1:2], warm[:, 0:1], ACT.Silu)
+
+        ident = keep.tile([P, P], F32)
+        make_identity(nc, ident[:])
+
+        nc.sync.dma_start(offs_sb[:], offs)
+        nc.sync.dma_start(a1_sb[:], a1)
+        nc.sync.dma_start(a2_sb[:], a2)
+        load_scale_rows(xs_all, x_scales, nc.sync)
+        xw_all = keep.tile([P, T], I32, align_bytes=64)
+        nc.sync.dma_start(out=xw_all[:], in_=x_words[0].rearrange("p c r -> p (c r)").bitcast(I32))
+
+        w1_rows = w1.rearrange("(p j) c -> p j c", j=PACK)
+        w1_bf = keep.tile([P, H * PACK], BF16, align_bytes=64)
+        w1_dealt = w1_bf[:].rearrange("p (t m j) -> p m j t", t=PACK, j=PACK)
+        c0 = 0
+        for i, width in enumerate(W1_PIECES):
+            raw = keep.tile([P, PACK, width], F32, name="w1_raw%d" % i)
+            nc.sync.dma_start(out=raw[:], in_=w1_rows[:, :, c0 : c0 + width])
+            split = width if i == 0 else width - W1_VECTOR_COLS
+            nc.scalar.copy(
+                out=w1_dealt[:, c0 // PACK : (c0 + split) // PACK, :, :],
+                in_=raw[:, :, 0:split].rearrange("p j (m t) -> p m j t", t=PACK),
+            )
+            if split < width:
+                w1_late = (
+                    w1_dealt[:, (c0 + split) // PACK : (c0 + width) // PACK, :, :],
+                    raw[:, :, split:width].rearrange("p j (m t) -> p m j t", t=PACK),
+                )
+            c0 = c0 + width
+
+        wa_sb = keep.tile([P, V], F32)
+        nc.sync.dma_start(out=wa_sb[:], in_=wa.rearrange("(p j) v -> p j v", j=PACK)[:, 0, :])
+        nc.sync.dma_start(back_sb[:], back)
+        w2w_raw = keep.tile([P, N], I32, align_bytes=64)
+        nc.sync.dma_start(out=w2w_raw[:], in_=w2_words[0].rearrange("p c r -> p (c r)").bitcast(I32))
+        load_scale_rows(w2s_raw, w2_scales, nc.sync)
+
+        xs = keep.tile([P, S], U8, align_bytes=64)
+        nc.vector.tensor_copy(xs[:], xs_all[:].indirect(offs_sb[:]))
+        xw = keep.tile([P, S], U32, align_bytes=64)
+        nc.vector.tensor_copy(xw[:], xw_all[:].bitcast(U32).indirect(offs_sb[:]))
+
+        nc.vector.tensor_copy(out=w1_late[0], in_=w1_late[1])
+        wb_sb = keep.tile([P, V], F32)
+        nc.scalar.activation(wb_sb[:], wa_sb[:], ACT.Copy, bias=1.0, scale=-1.0)
+
+        w1_codes = keep.tile([P, H], U32, align_bytes=64)
+        w1_scales = keep.tile([P, H], U8, align_bytes=64)
+        for t0, t1 in ((0, 1), (1, 2), (2, 4)):
+            nc.vector.quantize_mx(
+                out=w1_codes[:, t0 * P : t1 * P].bitcast(FP8X4),
+                scales=w1_scales[:, t0 * P : t1 * P],
+                in_=w1_bf[:, t0 * P * PACK : t1 * P * PACK],
+            )
+        y = [keep.tile([P, S], F32, name="y%d" % t) for t in range(PACK)]
+        for t in range(PACK):
+            cols = slice(t * P, (t + 1) * P)
+            j0 = 0
+            for width in FIRST_PIECES if t == 0 else (BANK, BANK):
+                picked = slice(j0, j0 + width)
+                acc = psum.tile([P, BANK], F32, name="acc")
+                nc.tensor.matmul_mx(
+                    out=acc[:, 0:width],
+                    lhsT=w1_codes[:, cols].bitcast(FP8X4),
+                    lhsT_scale=w1_scales[:, cols],
+                    rhs=xw[:, picked].bitcast(FP8X4),
+                    rhs_scale=xs[:, picked],
+                    start=True,
+                    stop=True,
+                )
+                if t == 0 and j0 == 0:
+                    nc.vector.tensor_copy(out=y[t][:, picked], in_=acc[:, 0:width])
+                else:
+                    nc.scalar.copy(out=y[t][:, picked], in_=acc[:, 0:width])
+                j0 = j0 + width
+
+        w2_codes = keep.tile([P, N], U32, align_bytes=64)
+        nc.vector.tensor_copy(
+            out=w2_codes[:].rearrange("p (t m) -> p m t", t=PACK),
+            in_=w2w_raw[:].bitcast(U32).rearrange("p (m t) -> p m t", t=PACK),
+        )
+        w2_sc = keep.tile([P, N], U8, align_bytes=64)
+        nc.vector.tensor_copy(
+            out=w2_sc[:].rearrange("p (t m) -> p m t", t=PACK),
+            in_=w2s_raw[:].rearrange("p (m t) -> p m t", t=PACK),
+        )
+
+        mg = [keep.tile([P, V], F32, name="mg%d" % t) for t in range(PACK)]
+        first = [keep.tile([P, V], F32, name="first%d" % t) for t in range(PACK)]
+        second = [keep.tile([P, V], F32, name="second%d" % t) for t in range(PACK)]
+
+        def mix(t):
+            mixed = keep.tile([P, V], F32, name="mixed", tag="z%d" % (2 - t % 2))
+            if t >= TENSOR_MIXES:
+                nc.vector.tensor_tensor(mixed[:], first[t][:], second[t][:], ALU.add)
+                nc.scalar.activation(mg[t][:], mixed[:], ACT.Silu)
+                return
+            summed = psum_mix.tile([P, BANK], F32, name="summed")
+            for v0 in range(0, V, P):
+                for k, part in enumerate((first[t], second[t])):
+                    nc.tensor.matmul(
+                        summed[:, v0 : v0 + P],
+                        part[:, v0 : v0 + P],
+                        ident[:],
+                        start=(k == 0),
+                        stop=(k == 1),
+                        is_transpose=True,
+                    )
+            nc.scalar.activation(mixed[:], summed[:], ACT.Silu)
+            turned = psum_mix.tile([P, BANK], F32, name="turned")
+            for v0 in range(0, V, P):
+                nc.tensor.transpose(turned[:, v0 : v0 + P], mixed[:, v0 : v0 + P], ident[:])
+            nc.scalar.copy(out=mg[t][:], in_=turned[:])
+
+        for t in range(PACK):
+            nc.vector.tensor_tensor(first[t][:], y[t][:].indirect(a1_sb[:]), wa_sb[:], ALU.mult)
+            if t > 0:
+                mix(t - 1)
+            nc.vector.tensor_tensor(second[t][:], y[t][:].indirect(a2_sb[:]), wb_sb[:], ALU.mult)
+
+        z_codes = keep.tile([P, S], U32, align_bytes=64)
+        z_scales = keep.tile([P, S], U8, align_bytes=64)
+        o_codes = keep.tile([P, S], I32, align_bytes=64)
+        o_scales = keep.tile([P, S], U8, align_bytes=64)
+        out_rows = out_0.rearrange("(p t) j -> p t j", t=PACK)
+        out_words = out_1[0].rearrange("p c r -> p (c r)").bitcast(I32)
+        starts = [sum(CHUNKS[:c]) for c in range(len(CHUNKS))]
+        z_bf = {}
+        o_bf = {}
+
+        def woven(tile_bf):
+            return tile_bf.rearrange("p (c i t) -> p c t i", i=4, t=PACK)
+
+        def planes(tile_f32):
+            return tile_f32.rearrange("p t (c i) -> p c t i", i=4)
+
+        def unmerge(c):
+            j0, width = starts[c], CHUNKS[c]
+            z = keep.tile([P, PACK, width], F32, name="z", tag="z%d" % (c % Z_SLOTS))
+            for t in range(PACK):
+                if c == 0 and t == 1:
+                    mix(PACK - 1)
+                nc.vector.tensor_tensor(
+                    z[:, t, :],
+                    mg[t][:].indirect(back_sb[:, j0 // 16 : (j0 + width) // 16]),
+                    y[t][:, j0 : j0 + width],
+                    ALU.add,
+                )
+            z_bf[c] = ring.tile([P, width * PACK], BF16, name="z_bf", align_bytes=64)
+            if c in VECTOR_WEAVES:
+                nc.vector.tensor_copy(out=woven(z_bf[c][:]), in_=planes(z[:]))
+            else:
+                nc.scalar.copy(out=woven(z_bf[c][:]), in_=planes(z[:]))
+
+        def multiply(c):
+            j0, width = starts[c], CHUNKS[c]
+            cols = slice(j0, j0 + width)
+            nc.vector.quantize_mx(out=z_codes[:, cols].bitcast(FP8X4), scales=z_scales[:, cols], in_=z_bf[c][:])
+            res = ring.tile([P, PACK, width], F32, name="res")
+            o_bf[c] = ring.tile([P, width * PACK], BF16, name="o_bf", align_bytes=64)
+            for s0 in range(0, width, STRIP):
+                acc = psum.tile([P, BANK], F32, name="acc")
+                strip = slice(j0 + s0, j0 + s0 + STRIP)
+                for t in range(PACK):
+                    nc.tensor.matmul_mx(
+                        out=acc[:, t * STRIP : (t + 1) * STRIP],
+                        lhsT=w2_codes[:, t * P : (t + 1) * P].bitcast(FP8X4),
+                        lhsT_scale=w2_sc[:, t * P : (t + 1) * P],
+                        rhs=z_codes[:, strip].bitcast(FP8X4),
+                        rhs_scale=z_scales[:, strip],
+                        start=True,
+                        stop=True,
+                    )
+                acc_planes = acc[:].rearrange("p (t n) -> p t n", t=PACK)
+                rounded = woven(o_bf[c][:, s0 * PACK : (s0 + STRIP) * PACK])
+                if (j0 + s0) // STRIP not in VECTOR_ROUNDS:
+                    nc.scalar.copy(out=rounded, in_=planes(acc_planes))
+                    nc.scalar.copy(out=res[:, :, s0 : s0 + STRIP], in_=acc_planes)
+                else:
+                    nc.scalar.copy(out=res[:, :, s0 : s0 + STRIP], in_=acc_planes)
+                    nc.vector.tensor_copy(out=rounded, in_=planes(res[:, :, s0 : s0 + STRIP]))
+                if c >= FINE_STORES:
+                    nc.sync.dma_start(out=out_rows[:, :, strip], in_=res[:, :, s0 : s0 + STRIP])
+            if c < FINE_STORES:
+                nc.sync.dma_start(out=out_rows[:, :, cols], in_=res[:])
+
+        def hand_on(c):
+            cols = slice(starts[c], starts[c] + CHUNKS[c])
+            nc.vector.quantize_mx(out=o_codes[:, cols].bitcast(FP8X4), scales=o_scales[:, cols], in_=o_bf[c][:])
+            nc.sync.dma_start(out=out_words[:, cols], in_=o_codes[:, cols])
+
+        for step in range(len(CHUNKS) + 2):
+            if step < len(CHUNKS):
+                unmerge(step)
+            if 0 <= step - 1 < len(CHUNKS):
+                multiply(step - 1)
+            if 0 <= step - 2 < len(CHUNKS):
+                hand_on(step - 2)
+
+        for q in range(4):
+            (nc.scalar if q < 3 else nc.sync).dma_start(
+                out=out_2[0, 4 * q : 4 * q + 4, :].bitcast(I32), in_=o_scales[32 * q : 32 * q + 4, :].bitcast(I32)
+            )

@@ -24,10 +24,10 @@ W1_PIECES = (256, 256)
 W1_VECTOR_COLS = 160
 FIRST_PIECES = (512, 256, 256)
 CHUNKS = (256, 256, 256, 256)
-VECTOR_ROUNDS = (2, 3, 4, 5, 6)
-FINE_STORES = 2
-VECTOR_WEAVES = (3,)
-Z_SLOTS = 3
+VECTOR_ROUNDS = (2, 3, 4, 5, 6, 7)
+FINE_STORES = 4
+VECTOR_WEAVES = ()
+Z_SLOTS = 2
 TENSOR_MIXES = 3
 
 
@@ -151,7 +151,7 @@ def tile_picked_tome8_silu_po_kernel(
         second = [keep.tile([P, V], F32, name="second%d" % t) for t in range(PACK)]
 
         def mix(t):
-            mixed = keep.tile([P, V], F32, name="mixed", tag="z%d" % (2 - t % 2))
+            mixed = keep.tile([P, V], F32, name="mixed", tag="mixed" if t == 1 else "z1")
             if t >= TENSOR_MIXES:
                 nc.vector.tensor_tensor(mixed[:], first[t][:], second[t][:], ALU.add)
                 nc.scalar.activation(mg[t][:], mixed[:], ACT.Silu)

@@ -28,7 +28,7 @@ VECTOR_ROUNDS = (2, 3, 4, 5, 6, 7)
 FINE_STORES = 4
 VECTOR_WEAVES = ()
 Z_SLOTS = 2
-TENSOR_MIXES = 3
+TENSOR_MIXES = 2
 
 
 def tile_picked_tome8_silu_po_kernel(
@@ -57,11 +57,12 @@ def tile_picked_tome8_silu_po_kernel(
         w2s_raw = keep.tile([P, N], U8, align_bytes=64)
         nc.vector.memset(w2s_raw[:].bitcast(I32), 0)
         warm = keep.tile([P, 2], F32)
-        nc.gpsimd.memset(warm[:, 0:1], 0.0)
+        nc.vector.memset(warm[:, 0:1], 0.0)
         nc.scalar.activation(warm[:, 1:2], warm[:, 0:1], ACT.Silu)
 
         ident = keep.tile([P, P], F32)
-        make_identity(nc, ident[:])
+        nc.vector.memset(ident[:], 0.0)
+        make_identity(nc, ident[:], nomemset=True)
 
         nc.sync.dma_start(offs_sb[:], offs)
         nc.sync.dma_start(a1_sb[:], a1)
@@ -150,28 +151,36 @@ def tile_picked_tome8_silu_po_kernel(
         first = [keep.tile([P, V], F32, name="first%d" % t) for t in range(PACK)]
         second = [keep.tile([P, V], F32, name="second%d" % t) for t in range(PACK)]
 
-        def mix(t):
-            mixed = keep.tile([P, V], F32, name="mixed", tag="mixed" if t == 1 else "z1")
-            if t >= TENSOR_MIXES:
-                nc.vector.tensor_tensor(mixed[:], first[t][:], second[t][:], ALU.add)
-                nc.scalar.activation(mg[t][:], mixed[:], ACT.Silu)
-                return
-            summed = psum_mix.tile([P, BANK], F32, name="summed")
-            for v0 in range(0, V, P):
-                for k, part in enumerate((first[t], second[t])):
-                    nc.tensor.matmul(
-                        summed[:, v0 : v0 + P],
-                        part[:, v0 : v0 + P],
-                        ident[:],
-                        start=(k == 0),
-                        stop=(k == 1),
-                        is_transpose=True,
-                    )
-            nc.scalar.activation(mixed[:], summed[:], ACT.Silu)
+        mixed = {}
+
+        def turn_back(t):
             turned = psum_mix.tile([P, BANK], F32, name="turned")
             for v0 in range(0, V, P):
-                nc.tensor.transpose(turned[:, v0 : v0 + P], mixed[:, v0 : v0 + P], ident[:])
+                nc.tensor.transpose(turned[:, v0 : v0 + P], mixed[t][:, v0 : v0 + P], ident[:])
             nc.scalar.copy(out=mg[t][:], in_=turned[:])
+
+        def mix(t):
+            mixed[t] = keep.tile([P, V], F32, name="mixed", tag="z1" if t % 2 else "mixed")
+            if t < TENSOR_MIXES:
+                summed = psum_mix.tile([P, BANK], F32, name="summed")
+                for v0 in range(0, V, P):
+                    for k, part in enumerate((first[t], second[t])):
+                        nc.tensor.matmul(
+                            summed[:, v0 : v0 + P],
+                            part[:, v0 : v0 + P],
+                            ident[:],
+                            start=(k == 0),
+                            stop=(k == 1),
+                            is_transpose=True,
+                        )
+                nc.scalar.activation(mixed[t][:], summed[:], ACT.Silu)
+                if t > 0:
+                    turn_back(t - 1)
+                if t == TENSOR_MIXES - 1:
+                    turn_back(t)
+            else:
+                nc.vector.tensor_tensor(mixed[t][:], first[t][:], second[t][:], ALU.add)
+                nc.scalar.activation(mg[t][:], mixed[t][:], ACT.Silu)
 
         for t in range(PACK):
             nc.vector.tensor_tensor(first[t][:], y[t][:].indirect(a1_sb[:]), wa_sb[:], ALU.mult)
@@ -187,13 +196,20 @@ def tile_picked_tome8_silu_po_kernel(
         out_words = out_1[0].rearrange("p c r -> p (c r)").bitcast(I32)
         starts = [sum(CHUNKS[:c]) for c in range(len(CHUNKS))]
         z_bf = {}
-        o_bf = {}
 
         def woven(tile_bf):
             return tile_bf.rearrange("p (c i t) -> p c t i", i=4, t=PACK)
 
         def planes(tile_f32):
             return tile_f32.rearrange("p t (c i) -> p c t i", i=4)
+
+        res = {}
+        o_bf = keep.tile([P, S * PACK], BF16, align_bytes=64)
+        last = len(CHUNKS) - 1
+
+        def pieces(c):
+            step = STRIP if c in (0, last) else CHUNKS[c]
+            return [(s0, step) for s0 in range(0, CHUNKS[c], step)]
 
         def unmerge(c):
             j0, width = starts[c], CHUNKS[c]
@@ -207,56 +223,71 @@ def tile_picked_tome8_silu_po_kernel(
                     y[t][:, j0 : j0 + width],
                     ALU.add,
                 )
-            z_bf[c] = ring.tile([P, width * PACK], BF16, name="z_bf", align_bytes=64)
-            if c in VECTOR_WEAVES:
-                nc.vector.tensor_copy(out=woven(z_bf[c][:]), in_=planes(z[:]))
-            else:
-                nc.scalar.copy(out=woven(z_bf[c][:]), in_=planes(z[:]))
+            z_bf[c] = keep.tile([P, width * PACK], BF16, name="z_bf", tag="bf%d" % (c % 2), align_bytes=64)
+            for s0, step in pieces(c) if c == last else [(0, width)]:
+                nc.scalar.copy(
+                    out=woven(z_bf[c][:, s0 * PACK : (s0 + step) * PACK]), in_=planes(z[:, :, s0 : s0 + step])
+                )
 
         def multiply(c):
             j0, width = starts[c], CHUNKS[c]
-            cols = slice(j0, j0 + width)
-            nc.vector.quantize_mx(out=z_codes[:, cols].bitcast(FP8X4), scales=z_scales[:, cols], in_=z_bf[c][:])
-            res = ring.tile([P, PACK, width], F32, name="res")
-            o_bf[c] = ring.tile([P, width * PACK], BF16, name="o_bf", align_bytes=64)
-            for s0 in range(0, width, STRIP):
-                acc = psum.tile([P, BANK], F32, name="acc")
-                strip = slice(j0 + s0, j0 + s0 + STRIP)
-                for t in range(PACK):
-                    nc.tensor.matmul_mx(
-                        out=acc[:, t * STRIP : (t + 1) * STRIP],
-                        lhsT=w2_codes[:, t * P : (t + 1) * P].bitcast(FP8X4),
-                        lhsT_scale=w2_sc[:, t * P : (t + 1) * P],
-                        rhs=z_codes[:, strip].bitcast(FP8X4),
-                        rhs_scale=z_scales[:, strip],
-                        start=True,
-                        stop=True,
+            res[c] = ring.tile([P, PACK, width], F32, name="res")
+            for s0, step in pieces(c):
+                cols = slice(j0 + s0, j0 + s0 + step)
+                if c > 0 or s0 == 0:
+                    span = width if c == 0 else step
+                    nc.vector.quantize_mx(
+                        out=z_codes[:, j0 + s0 : j0 + s0 + span].bitcast(FP8X4),
+                        scales=z_scales[:, j0 + s0 : j0 + s0 + span],
+                        in_=z_bf[c][:, s0 * PACK : (s0 + span) * PACK],
                     )
-                acc_planes = acc[:].rearrange("p (t n) -> p t n", t=PACK)
-                rounded = woven(o_bf[c][:, s0 * PACK : (s0 + STRIP) * PACK])
-                if (j0 + s0) // STRIP not in VECTOR_ROUNDS:
-                    nc.scalar.copy(out=rounded, in_=planes(acc_planes))
-                    nc.scalar.copy(out=res[:, :, s0 : s0 + STRIP], in_=acc_planes)
-                else:
-                    nc.scalar.copy(out=res[:, :, s0 : s0 + STRIP], in_=acc_planes)
-                    nc.vector.tensor_copy(out=rounded, in_=planes(res[:, :, s0 : s0 + STRIP]))
-                if c >= FINE_STORES:
-                    nc.sync.dma_start(out=out_rows[:, :, strip], in_=res[:, :, s0 : s0 + STRIP])
-            if c < FINE_STORES:
-                nc.sync.dma_start(out=out_rows[:, :, cols], in_=res[:])
+                per_bank = BANK // step
+                for t0 in range(0, PACK, per_bank):
+                    acc = psum.tile([P, BANK], F32, name="acc")
+                    for i in range(per_bank):
+                        rows = slice((t0 + i) * P, (t0 + i + 1) * P)
+                        nc.tensor.matmul_mx(
+                            out=acc[:, i * step : (i + 1) * step],
+                            lhsT=w2_codes[:, rows].bitcast(FP8X4),
+                            lhsT_scale=w2_sc[:, rows],
+                            rhs=z_codes[:, cols].bitcast(FP8X4),
+                            rhs_scale=z_scales[:, cols],
+                            start=True,
+                            stop=True,
+                        )
+                    held = res[c][:, t0 : t0 + per_bank, s0 : s0 + step]
+                    sums = acc[:].rearrange("p (t n) -> p t n", t=per_bank)
+                    if c == 0:
+                        nc.scalar.copy(out=woven(o_bf[:, s0 * PACK : (s0 + step) * PACK]), in_=planes(sums))
+                    nc.scalar.copy(out=held, in_=sums)
+                    if 0 < c < last:
+                        nc.sync.dma_start(out=out_rows[:, t0 : t0 + per_bank, cols], in_=held)
+            if c in (0, last):
+                nc.sync.dma_start(out=out_rows[:, :, j0 : j0 + width], in_=res[c][:])
 
         def hand_on(c):
-            cols = slice(starts[c], starts[c] + CHUNKS[c])
-            nc.vector.quantize_mx(out=o_codes[:, cols].bitcast(FP8X4), scales=o_scales[:, cols], in_=o_bf[c][:])
+            j0, width = starts[c], CHUNKS[c]
+            for s0, step in pieces(c):
+                nc.vector.tensor_copy(
+                    out=woven(o_bf[:, (j0 + s0) * PACK : (j0 + s0 + step) * PACK]),
+                    in_=planes(res[c][:, :, s0 : s0 + step]),
+                )
+            c0 = 0 if c == 1 else j0
+            cols = slice(c0, j0 + width)
+            nc.vector.quantize_mx(
+                out=o_codes[:, cols].bitcast(FP8X4),
+                scales=o_scales[:, cols],
+                in_=o_bf[:, c0 * PACK : (j0 + width) * PACK],
+            )
             nc.sync.dma_start(out=out_words[:, cols], in_=o_codes[:, cols])
 
-        for step in range(len(CHUNKS) + 2):
+        for step in range(len(CHUNKS) + 3):
             if step < len(CHUNKS):
                 unmerge(step)
             if 0 <= step - 1 < len(CHUNKS):
                 multiply(step - 1)
-            if 0 <= step - 2 < len(CHUNKS):
-                hand_on(step - 2)
+            if 1 <= step - 3 < len(CHUNKS):
+                hand_on(step - 3)
 
         for q in range(4):
             (nc.scalar if q < 3 else nc.sync).dma_start(

@@ -27,7 +27,8 @@ CHUNKS = (256, 256, 256, 256)
 VECTOR_ROUNDS = (2, 3, 4, 5, 6, 7)
 FINE_STORES = 4
 VECTOR_WEAVES = ()
-Z_SLOTS = 2
+Z_SLOTS = 3
+HALF = V // 2
 TENSOR_MIXES = 2
 
 
@@ -38,7 +39,7 @@ def tile_picked_tome8_silu_po_kernel(
     with ExitStack() as ctx:
         keep = ctx.enter_context(tc.tile_pool(name="keep", bufs=1))
         ring = ctx.enter_context(tc.tile_pool(name="ring", bufs=4))
-        psum = ctx.enter_context(tc.psum_pool(name="psum", bufs=6))
+        psum = ctx.enter_context(tc.psum_pool(name="psum", bufs=4))
         psum_mix = ctx.enter_context(tc.psum_pool(name="psum_mix", bufs=1))
 
         def load_scale_rows(plane, rows, queue):
@@ -151,36 +152,27 @@ def tile_picked_tome8_silu_po_kernel(
         first = [keep.tile([P, V], F32, name="first%d" % t) for t in range(PACK)]
         second = [keep.tile([P, V], F32, name="second%d" % t) for t in range(PACK)]
 
-        mixed = {}
-
-        def turn_back(t):
-            turned = psum_mix.tile([P, BANK], F32, name="turned")
-            for v0 in range(0, V, P):
-                nc.tensor.transpose(turned[:, v0 : v0 + P], mixed[t][:, v0 : v0 + P], ident[:])
-            nc.scalar.copy(out=mg[t][:], in_=turned[:])
-
         def mix(t):
-            mixed[t] = keep.tile([P, V], F32, name="mixed", tag="z1" if t % 2 else "mixed")
-            if t < TENSOR_MIXES:
-                summed = psum_mix.tile([P, BANK], F32, name="summed")
-                for v0 in range(0, V, P):
+            mixed = keep.tile([P, V], F32, name="mixed", tag="z2" if t % 2 else "mixed")
+            halves = [range(h * HALF, (h + 1) * HALF, P) for h in range(2)]
+            for h, blocks in enumerate(halves):
+                summed = psum_mix.tile([P, HALF], F32, name="summed%d" % h)
+                for i, v0 in enumerate(blocks):
                     for k, part in enumerate((first[t], second[t])):
                         nc.tensor.matmul(
-                            summed[:, v0 : v0 + P],
+                            summed[:, i * P : (i + 1) * P],
                             part[:, v0 : v0 + P],
                             ident[:],
                             start=(k == 0),
                             stop=(k == 1),
                             is_transpose=True,
                         )
-                nc.scalar.activation(mixed[t][:], summed[:], ACT.Silu)
-                if t > 0:
-                    turn_back(t - 1)
-                if t == TENSOR_MIXES - 1:
-                    turn_back(t)
-            else:
-                nc.vector.tensor_tensor(mixed[t][:], first[t][:], second[t][:], ALU.add)
-                nc.scalar.activation(mg[t][:], mixed[t][:], ACT.Silu)
+                nc.scalar.activation(mixed[:, h * HALF : (h + 1) * HALF], summed[:], ACT.Silu)
+            for h, blocks in enumerate(halves):
+                turned = psum_mix.tile([P, HALF], F32, name="turned%d" % h)
+                for i, v0 in enumerate(blocks):
+                    nc.tensor.transpose(turned[:, i * P : (i + 1) * P], mixed[:, v0 : v0 + P], ident[:])
+                nc.scalar.copy(out=mg[t][:, h * HALF : (h + 1) * HALF], in_=turned[:])
 
         for t in range(PACK):
             nc.vector.tensor_tensor(first[t][:], y[t][:].indirect(a1_sb[:]), wa_sb[:], ALU.mult)
@@ -207,10 +199,6 @@ def tile_picked_tome8_silu_po_kernel(
         o_bf = keep.tile([P, S * PACK], BF16, align_bytes=64)
         last = len(CHUNKS) - 1
 
-        def pieces(c):
-            step = STRIP if c in (0, last) else CHUNKS[c]
-            return [(s0, step) for s0 in range(0, CHUNKS[c], step)]
-
         def unmerge(c):
             j0, width = starts[c], CHUNKS[c]
             z = keep.tile([P, PACK, width], F32, name="z", tag="z%d" % (c % Z_SLOTS))
@@ -223,55 +211,40 @@ def tile_picked_tome8_silu_po_kernel(
                     y[t][:, j0 : j0 + width],
                     ALU.add,
                 )
-            z_bf[c] = keep.tile([P, width * PACK], BF16, name="z_bf", tag="bf%d" % (c % 2), align_bytes=64)
-            for s0, step in pieces(c) if c == last else [(0, width)]:
-                nc.scalar.copy(
-                    out=woven(z_bf[c][:, s0 * PACK : (s0 + step) * PACK]), in_=planes(z[:, :, s0 : s0 + step])
-                )
+            z_bf[c] = ring.tile([P, width * PACK], BF16, name="z_bf", align_bytes=64)
+            if c == last:
+                nc.vector.tensor_copy(out=woven(z_bf[c][:]), in_=planes(z[:]))
+            else:
+                nc.scalar.copy(out=woven(z_bf[c][:]), in_=planes(z[:]))
 
         def multiply(c):
             j0, width = starts[c], CHUNKS[c]
+            cols = slice(j0, j0 + width)
             res[c] = ring.tile([P, PACK, width], F32, name="res")
-            for s0, step in pieces(c):
-                cols = slice(j0 + s0, j0 + s0 + step)
-                if c > 0 or s0 == 0:
-                    span = width if c == 0 else step
-                    nc.vector.quantize_mx(
-                        out=z_codes[:, j0 + s0 : j0 + s0 + span].bitcast(FP8X4),
-                        scales=z_scales[:, j0 + s0 : j0 + s0 + span],
-                        in_=z_bf[c][:, s0 * PACK : (s0 + span) * PACK],
+            nc.vector.quantize_mx(out=z_codes[:, cols].bitcast(FP8X4), scales=z_scales[:, cols], in_=z_bf[c][:])
+            per_bank = BANK // width
+            for t0 in range(0, PACK, per_bank):
+                acc = psum.tile([P, BANK], F32, name="acc")
+                for i in range(per_bank):
+                    rows = slice((t0 + i) * P, (t0 + i + 1) * P)
+                    nc.tensor.matmul_mx(
+                        out=acc[:, i * width : (i + 1) * width],
+                        lhsT=w2_codes[:, rows].bitcast(FP8X4),
+                        lhsT_scale=w2_sc[:, rows],
+                        rhs=z_codes[:, cols].bitcast(FP8X4),
+                        rhs_scale=z_scales[:, cols],
+                        start=True,
+                        stop=True,
                     )
-                per_bank = BANK // step
-                for t0 in range(0, PACK, per_bank):
-                    acc = psum.tile([P, BANK], F32, name="acc")
-                    for i in range(per_bank):
-                        rows = slice((t0 + i) * P, (t0 + i + 1) * P)
-                        nc.tensor.matmul_mx(
-                            out=acc[:, i * step : (i + 1) * step],
-                            lhsT=w2_codes[:, rows].bitcast(FP8X4),
-                            lhsT_scale=w2_sc[:, rows],
-                            rhs=z_codes[:, cols].bitcast(FP8X4),
-                            rhs_scale=z_scales[:, cols],
-                            start=True,
-                            stop=True,
-                        )
-                    held = res[c][:, t0 : t0 + per_bank, s0 : s0 + step]
-                    sums = acc[:].rearrange("p (t n) -> p t n", t=per_bank)
-                    if c == 0:
-                        nc.scalar.copy(out=woven(o_bf[:, s0 * PACK : (s0 + step) * PACK]), in_=planes(sums))
-                    nc.scalar.copy(out=held, in_=sums)
-                    if 0 < c < last:
-                        nc.sync.dma_start(out=out_rows[:, t0 : t0 + per_bank, cols], in_=held)
-            if c in (0, last):
-                nc.sync.dma_start(out=out_rows[:, :, j0 : j0 + width], in_=res[c][:])
+                held = res[c][:, t0 : t0 + per_bank, :]
+                nc.scalar.copy(out=held, in_=acc[:].rearrange("p (t n) -> p t n", t=per_bank))
+                nc.sync.dma_start(out=out_rows[:, t0 : t0 + per_bank, cols], in_=held)
 
         def hand_on(c):
             j0, width = starts[c], CHUNKS[c]
-            for s0, step in pieces(c):
-                nc.vector.tensor_copy(
-                    out=woven(o_bf[:, (j0 + s0) * PACK : (j0 + s0 + step) * PACK]),
-                    in_=planes(res[c][:, :, s0 : s0 + step]),
-                )
+            nc.vector.tensor_copy(out=woven(o_bf[:, j0 * PACK : (j0 + width) * PACK]), in_=planes(res[c][:]))
+            if c == 0:
+                return
             c0 = 0 if c == 1 else j0
             cols = slice(c0, j0 + width)
             nc.vector.quantize_mx(
@@ -286,7 +259,7 @@ def tile_picked_tome8_silu_po_kernel(
                 unmerge(step)
             if 0 <= step - 1 < len(CHUNKS):
                 multiply(step - 1)
-            if 1 <= step - 3 < len(CHUNKS):
+            if 0 <= step - 3 < len(CHUNKS):
                 hand_on(step - 3)
 
         for q in range(4):

@@ -19,17 +19,9 @@ ACT = mybir.ActivationFunctionType
 P = 128
 PACK = 4
 BANK = 512
-STRIP = 128
-W1_PIECES = (256, 256)
-W1_VECTOR_COLS = 160
-FIRST_PIECES = (512, 256, 256)
-CHUNKS = (256, 256, 256, 256)
-VECTOR_ROUNDS = (2, 3, 4, 5, 6, 7)
-FINE_STORES = 4
-VECTOR_WEAVES = ()
-Z_SLOTS = 3
+WORD_PIECES = (256, 256, 256, 256)
+SLOT = 256
 HALF = V // 2
-TENSOR_MIXES = 2
 
 
 def tile_picked_tome8_silu_po_kernel(
@@ -38,7 +30,6 @@ def tile_picked_tome8_silu_po_kernel(
     nc = tc.nc
     with ExitStack() as ctx:
         keep = ctx.enter_context(tc.tile_pool(name="keep", bufs=1))
-        ring = ctx.enter_context(tc.tile_pool(name="ring", bufs=4))
         psum = ctx.enter_context(tc.psum_pool(name="psum", bufs=4))
         psum_mix = ctx.enter_context(tc.psum_pool(name="psum_mix", bufs=1))
 
@@ -65,61 +56,51 @@ def tile_picked_tome8_silu_po_kernel(
         nc.vector.memset(ident[:], 0.0)
         make_identity(nc, ident[:], nomemset=True)
 
-        nc.sync.dma_start(offs_sb[:], offs)
-        nc.sync.dma_start(a1_sb[:], a1)
-        nc.sync.dma_start(a2_sb[:], a2)
-        load_scale_rows(xs_all, x_scales, nc.sync)
-        xw_all = keep.tile([P, T], I32, align_bytes=64)
-        nc.sync.dma_start(out=xw_all[:], in_=x_words[0].rearrange("p c r -> p (c r)").bitcast(I32))
-
         w1_rows = w1.rearrange("(p j) c -> p j c", j=PACK)
-        w1_bf = keep.tile([P, H * PACK], BF16, align_bytes=64)
-        w1_dealt = w1_bf[:].rearrange("p (t m j) -> p m j t", t=PACK, j=PACK)
-        c0 = 0
-        for i, width in enumerate(W1_PIECES):
-            raw = keep.tile([P, PACK, width], F32, name="w1_raw%d" % i)
-            nc.sync.dma_start(out=raw[:], in_=w1_rows[:, :, c0 : c0 + width])
-            split = width if i == 0 else width - W1_VECTOR_COLS
-            nc.scalar.copy(
-                out=w1_dealt[:, c0 // PACK : (c0 + split) // PACK, :, :],
-                in_=raw[:, :, 0:split].rearrange("p j (m t) -> p m j t", t=PACK),
-            )
-            if split < width:
-                w1_late = (
-                    w1_dealt[:, (c0 + split) // PACK : (c0 + width) // PACK, :, :],
-                    raw[:, :, split:width].rearrange("p j (m t) -> p m j t", t=PACK),
-                )
-            c0 = c0 + width
-
+        w1_raw = keep.tile([P, PACK, H], F32)
+        xw_all = keep.tile([P, T], I32, align_bytes=64)
         wa_sb = keep.tile([P, V], F32)
-        nc.sync.dma_start(out=wa_sb[:], in_=wa.rearrange("(p j) v -> p j v", j=PACK)[:, 0, :])
-        nc.sync.dma_start(back_sb[:], back)
         w2w_raw = keep.tile([P, N], I32, align_bytes=64)
+        nc.sync.dma_start(offs_sb[:], offs)
+        nc.sync.dma_start(out=w1_raw[:, 0, :], in_=w1_rows[:, 0, :])
+        nc.sync.dma_start(a1_sb[:], a1)
+        load_scale_rows(xs_all, x_scales, nc.sync)
+        nc.sync.dma_start(out=w1_raw[:, 1:PACK, :], in_=w1_rows[:, 1:PACK, :])
+        nc.sync.dma_start(out=xw_all[:], in_=x_words[0].rearrange("p c r -> p (c r)").bitcast(I32))
+        nc.sync.dma_start(out=wa_sb[:], in_=wa.rearrange("(p j) v -> p j v", j=PACK)[:, 0, :])
         nc.sync.dma_start(out=w2w_raw[:], in_=w2_words[0].rearrange("p c r -> p (c r)").bitcast(I32))
         load_scale_rows(w2s_raw, w2_scales, nc.sync)
+        nc.sync.dma_start(a2_sb[:], a2)
+        nc.sync.dma_start(back_sb[:], back)
 
         xs = keep.tile([P, S], U8, align_bytes=64)
         nc.vector.tensor_copy(xs[:], xs_all[:].indirect(offs_sb[:]))
-        xw = keep.tile([P, S], U32, align_bytes=64)
-        nc.vector.tensor_copy(xw[:], xw_all[:].bitcast(U32).indirect(offs_sb[:]))
 
-        nc.vector.tensor_copy(out=w1_late[0], in_=w1_late[1])
+        w1_bf = keep.tile([P, H * PACK], BF16, align_bytes=64)
+        w1_dealt = w1_bf[:].rearrange("p (t m j) -> p m j t", t=PACK, j=PACK)
+        w1_cols = w1_raw[:].rearrange("p j (m t) -> p m j t", t=PACK)
+        w1_codes = keep.tile([P, H], U32, align_bytes=64)
+        w1_scales = keep.tile([P, H], U8, align_bytes=64)
+        nc.scalar.copy(out=w1_dealt[:, 0:64, :, :], in_=w1_cols[:, 0:64, :, :])
+        nc.vector.tensor_copy(out=w1_dealt[:, 64:P, :, :], in_=w1_cols[:, 64:P, :, :])
+        nc.vector.quantize_mx(out=w1_codes[:].bitcast(FP8X4), scales=w1_scales[:], in_=w1_bf[:])
+
+        xw = keep.tile([P, S], U32, align_bytes=64)
+        j0 = 0
+        for width in WORD_PIECES:
+            nc.vector.tensor_copy(
+                xw[:, j0 : j0 + width], xw_all[:].bitcast(U32).indirect(offs_sb[:, j0 // 16 : (j0 + width) // 16])
+            )
+            j0 = j0 + width
+
         wb_sb = keep.tile([P, V], F32)
         nc.scalar.activation(wb_sb[:], wa_sb[:], ACT.Copy, bias=1.0, scale=-1.0)
 
-        w1_codes = keep.tile([P, H], U32, align_bytes=64)
-        w1_scales = keep.tile([P, H], U8, align_bytes=64)
-        for t0, t1 in ((0, 1), (1, 2), (2, 4)):
-            nc.vector.quantize_mx(
-                out=w1_codes[:, t0 * P : t1 * P].bitcast(FP8X4),
-                scales=w1_scales[:, t0 * P : t1 * P],
-                in_=w1_bf[:, t0 * P * PACK : t1 * P * PACK],
-            )
         y = [keep.tile([P, S], F32, name="y%d" % t) for t in range(PACK)]
         for t in range(PACK):
             cols = slice(t * P, (t + 1) * P)
             j0 = 0
-            for width in FIRST_PIECES if t == 0 else (BANK, BANK):
+            for width in WORD_PIECES if t == 0 else (BANK, BANK):
                 picked = slice(j0, j0 + width)
                 acc = psum.tile([P, BANK], F32, name="acc")
                 nc.tensor.matmul_mx(
@@ -131,10 +112,7 @@ def tile_picked_tome8_silu_po_kernel(
                     start=True,
                     stop=True,
                 )
-                if t == 0 and j0 == 0:
-                    nc.vector.tensor_copy(out=y[t][:, picked], in_=acc[:, 0:width])
-                else:
-                    nc.scalar.copy(out=y[t][:, picked], in_=acc[:, 0:width])
+                nc.scalar.copy(out=y[t][:, picked], in_=acc[:, 0:width])
                 j0 = j0 + width
 
         w2_codes = keep.tile([P, N], U32, align_bytes=64)
@@ -148,46 +126,73 @@ def tile_picked_tome8_silu_po_kernel(
             in_=w2s_raw[:].rearrange("p (m t) -> p m t", t=PACK),
         )
 
-        mg = [keep.tile([P, V], F32, name="mg%d" % t) for t in range(PACK)]
-        first = [keep.tile([P, V], F32, name="first%d" % t) for t in range(PACK)]
-        second = [keep.tile([P, V], F32, name="second%d" % t) for t in range(PACK)]
+        mg = [keep.tile([P, V], F32, name="mg%d" % t, align_bytes=64) for t in range(PACK)]
+        first = {}
+        second = {}
 
-        def mix(t):
-            mixed = keep.tile([P, V], F32, name="mixed", tag="z2" if t % 2 else "mixed")
-            halves = [range(h * HALF, (h + 1) * HALF, P) for h in range(2)]
-            for h, blocks in enumerate(halves):
-                summed = psum_mix.tile([P, HALF], F32, name="summed%d" % h)
-                for i, v0 in enumerate(blocks):
+        def take_first(t, v0, v1, tag):
+            if v0 == 0:
+                first[t] = keep.tile([P, V], F32, name="first", tag=tag)
+            nc.vector.tensor_tensor(
+                first[t][:, v0:v1], y[t][:].indirect(a1_sb[:, v0 // 16 : v1 // 16]), wa_sb[:, v0:v1], ALU.mult
+            )
+
+        def take_second(t, v0, v1, tag):
+            if v0 == 0:
+                second[t] = keep.tile([P, V], F32, name="second", tag=tag)
+            nc.vector.tensor_tensor(
+                second[t][:, v0:v1], y[t][:].indirect(a2_sb[:, v0 // 16 : v1 // 16]), wb_sb[:, v0:v1], ALU.mult
+            )
+
+        def mix(t, spans, sum_tags, turn_tags, homes):
+            for (v0, v1), tag, home in zip(spans, sum_tags, homes):
+                summed = psum_mix.tile([P, v1 - v0], F32, name="summed", tag=tag)
+                for v in range(v0, v1, P):
                     for k, part in enumerate((first[t], second[t])):
                         nc.tensor.matmul(
-                            summed[:, i * P : (i + 1) * P],
-                            part[:, v0 : v0 + P],
+                            summed[:, v - v0 : v - v0 + P],
+                            part[:, v : v + P],
                             ident[:],
                             start=(k == 0),
                             stop=(k == 1),
                             is_transpose=True,
                         )
-                nc.scalar.activation(mixed[:, h * HALF : (h + 1) * HALF], summed[:], ACT.Silu)
-            for h, blocks in enumerate(halves):
-                turned = psum_mix.tile([P, HALF], F32, name="turned%d" % h)
-                for i, v0 in enumerate(blocks):
-                    nc.tensor.transpose(turned[:, i * P : (i + 1) * P], mixed[:, v0 : v0 + P], ident[:])
-                nc.scalar.copy(out=mg[t][:, h * HALF : (h + 1) * HALF], in_=turned[:])
+                nc.scalar.activation(home, summed[:].rearrange("p (b v) -> p b v", v=P), ACT.Silu)
+            for (v0, v1), tag, home in zip(spans, turn_tags, homes):
+                turned = psum_mix.tile([P, v1 - v0], F32, name="turned", tag=tag)
+                for b in reversed(range((v1 - v0) // P)):
+                    nc.tensor.transpose(turned[:, b * P : (b + 1) * P], home[:, b, :], ident[:])
+                nc.scalar.copy(out=mg[t][:, v0:v1], in_=turned[:])
 
-        for t in range(PACK):
-            nc.vector.tensor_tensor(first[t][:], y[t][:].indirect(a1_sb[:]), wa_sb[:], ALU.mult)
-            if t > 0:
-                mix(t - 1)
-            nc.vector.tensor_tensor(second[t][:], y[t][:].indirect(a2_sb[:]), wb_sb[:], ALU.mult)
+        def mix_on_vector(t, v0, v1, summed):
+            nc.vector.tensor_tensor(summed, first[t][:, v0:v1], second[t][:, v0:v1], ALU.add)
+            nc.scalar.activation(mg[t][:, v0:v1], summed, ACT.Silu)
 
         z_codes = keep.tile([P, S], U32, align_bytes=64)
         z_scales = keep.tile([P, S], U8, align_bytes=64)
-        o_codes = keep.tile([P, S], I32, align_bytes=64)
         o_scales = keep.tile([P, S], U8, align_bytes=64)
         out_rows = out_0.rearrange("(p t) j -> p t j", t=PACK)
         out_words = out_1[0].rearrange("p c r -> p (c r)").bitcast(I32)
-        starts = [sum(CHUNKS[:c]) for c in range(len(CHUNKS))]
-        z_bf = {}
+        res = {}
+        banks = {}
+
+        halves = ((0, HALF), (HALF, V))
+        z_ring = keep.tile([P, 8 * SLOT], F32)
+        bank = ["m%d" % b for b in range(4)]
+        for t in range(PACK - 1):
+            take_first(t, 0, V, "first%d" % (t % 2))
+            take_second(t, 0, V, "second%d" % t)
+            mixed = keep.tile([P, 2, 2, P], F32, name="mixed", tag="mixed%d" % (t % 2))
+            homes = [mixed[:, 0, :, :], mixed[:, 1, :, :]]
+            if t == 1:
+                homes[1] = z_ring[:, 0:SLOT].rearrange("p (b v) -> p b v", b=2)
+            if t == 2:
+                homes[1] = z_ring[:, SLOT : 7 * SLOT].rearrange("p (b v) -> p b v", b=2)[:, :, 0:P]
+            mix(t, halves, (bank[t], bank[t + 1]), (bank[(t + 2) % 4], bank[(t + 3) % 4]), homes)
+        take_first(PACK - 1, 0, V, "first1")
+        take_second(PACK - 1, 0, V, "mixed1")
+        mix_on_vector(PACK - 1, 0, V, z_ring[:, 4 * SLOT : 6 * SLOT])
+
 
         def woven(tile_bf):
             return tile_bf.rearrange("p (c i t) -> p c t i", i=4, t=PACK)
@@ -195,74 +200,119 @@ def tile_picked_tome8_silu_po_kernel(
         def planes(tile_f32):
             return tile_f32.rearrange("p t (c i) -> p c t i", i=4)
 
-        res = {}
-        o_bf = keep.tile([P, S * PACK], BF16, align_bytes=64)
-        last = len(CHUNKS) - 1
+        def z_home(col0, width, step=SLOT):
+            rows = z_ring[:, col0 : col0 + PACK * step].rearrange("p (t j) -> p t j", t=PACK)
+            return rows[:, :, 0:width]
 
-        def unmerge(c):
-            j0, width = starts[c], CHUNKS[c]
-            z = keep.tile([P, PACK, width], F32, name="z", tag="z%d" % (c % Z_SLOTS))
-            for t in range(PACK):
-                if c == 0 and t == 1:
-                    mix(PACK - 1)
+        def unmerge(home, j0, ts):
+            width = home.shape[2]
+            for t in ts:
                 nc.vector.tensor_tensor(
-                    z[:, t, :],
+                    home[:, t, :],
                     mg[t][:].indirect(back_sb[:, j0 // 16 : (j0 + width) // 16]),
                     y[t][:, j0 : j0 + width],
                     ALU.add,
                 )
-            z_bf[c] = ring.tile([P, width * PACK], BF16, name="z_bf", align_bytes=64)
-            if c == last:
-                nc.vector.tensor_copy(out=woven(z_bf[c][:]), in_=planes(z[:]))
-            else:
-                nc.scalar.copy(out=woven(z_bf[c][:]), in_=planes(z[:]))
 
-        def multiply(c):
-            j0, width = starts[c], CHUNKS[c]
+        def weave(engine_copy, source, target):
+            engine_copy(out=woven(target), in_=planes(source))
+
+        def bf_tile(width, tag):
+            return keep.tile([P, width * PACK], BF16, name="bf", tag=tag, align_bytes=64)
+
+        def multiply(z_bf, j0, width, per_bank=2):
             cols = slice(j0, j0 + width)
-            res[c] = ring.tile([P, PACK, width], F32, name="res")
-            nc.vector.quantize_mx(out=z_codes[:, cols].bitcast(FP8X4), scales=z_scales[:, cols], in_=z_bf[c][:])
-            per_bank = BANK // width
-            for t0 in range(0, PACK, per_bank):
-                acc = psum.tile([P, BANK], F32, name="acc")
-                for i in range(per_bank):
-                    rows = slice((t0 + i) * P, (t0 + i + 1) * P)
-                    nc.tensor.matmul_mx(
-                        out=acc[:, i * width : (i + 1) * width],
-                        lhsT=w2_codes[:, rows].bitcast(FP8X4),
-                        lhsT_scale=w2_sc[:, rows],
-                        rhs=z_codes[:, cols].bitcast(FP8X4),
-                        rhs_scale=z_scales[:, cols],
-                        start=True,
-                        stop=True,
-                    )
-                held = res[c][:, t0 : t0 + per_bank, :]
-                nc.scalar.copy(out=held, in_=acc[:].rearrange("p (t n) -> p t n", t=per_bank))
-                nc.sync.dma_start(out=out_rows[:, t0 : t0 + per_bank, cols], in_=held)
+            nc.vector.quantize_mx(out=z_codes[:, cols].bitcast(FP8X4), scales=z_scales[:, cols], in_=z_bf)
+            span = min(width, BANK // per_bank)
+            for s0 in range(j0, j0 + width, span):
+                for t0 in range(0, PACK, per_bank):
+                    acc = psum.tile([P, per_bank, span], F32, name="acc")
+                    banks[s0, t0] = acc
+                    for i in range(per_bank):
+                        rows = slice((t0 + i) * P, (t0 + i + 1) * P)
+                        nc.tensor.matmul_mx(
+                            out=acc[:, i, :],
+                            lhsT=w2_codes[:, rows].bitcast(FP8X4),
+                            lhsT_scale=w2_sc[:, rows],
+                            rhs=z_codes[:, s0 : s0 + span].bitcast(FP8X4),
+                            rhs_scale=z_scales[:, s0 : s0 + span],
+                            start=True,
+                            stop=True,
+                        )
 
-        def hand_on(c):
-            j0, width = starts[c], CHUNKS[c]
-            nc.vector.tensor_copy(out=woven(o_bf[:, j0 * PACK : (j0 + width) * PACK]), in_=planes(res[c][:]))
-            if c == 0:
-                return
-            c0 = 0 if c == 1 else j0
-            cols = slice(c0, j0 + width)
-            nc.vector.quantize_mx(
-                out=o_codes[:, cols].bitcast(FP8X4),
-                scales=o_scales[:, cols],
-                in_=o_bf[:, c0 * PACK : (j0 + width) * PACK],
-            )
-            nc.sync.dma_start(out=out_words[:, cols], in_=o_codes[:, cols])
+        def store(j0, width, per_bank=2, copies=None, joined=False):
+            res[j0] = keep.tile([P, PACK, width], F32, name="res%d" % j0)
+            span = min(width, BANK // per_bank)
+            parts = [(s0, t0) for s0 in range(0, width, span) for t0 in range(0, PACK, per_bank)]
+            for (s0, t0), engine_copy in zip(parts, copies or (on_scalar, on_scalar)):
+                held = res[j0][:, t0 : t0 + per_bank, s0 : s0 + span]
+                engine_copy(out=held, in_=banks[j0 + s0, t0][:])
+                if not joined:
+                    nc.sync.dma_start(out=out_rows[:, t0 : t0 + per_bank, j0 + s0 : j0 + s0 + span], in_=held)
+            if joined:
+                nc.sync.dma_start(out=out_rows[:, :, j0 : j0 + width], in_=res[j0][:])
 
-        for step in range(len(CHUNKS) + 3):
-            if step < len(CHUNKS):
-                unmerge(step)
-            if 0 <= step - 1 < len(CHUNKS):
-                multiply(step - 1)
-            if 0 <= step - 3 < len(CHUNKS):
-                hand_on(step - 3)
+        def code_tile(width, tag):
+            return keep.tile([P, width], I32, name="o_codes", tag=tag, align_bytes=64)
+
+        def hand_on(codes, piece, j0, width):
+            nc.vector.quantize_mx(out=codes.bitcast(FP8X4), scales=o_scales[:, j0 : j0 + width], in_=piece)
+
+        def store_words(codes, j0, width):
+            nc.sync.dma_start(out=out_words[:, j0 : j0 + width], in_=codes)
+
+        on_scalar, on_vector = nc.scalar.copy, nc.vector.tensor_copy
+        homes = [z_home(0, SLOT), z_home(3 * SLOT, SLOT), z_home(0, SLOT)]
+        home_a, home_b = z_home(3 * SLOT, P), z_home(SLOT + P, P)
+        zb = [bf_tile(SLOT, "zb%d" % c) for c in range(3)]
+        zb_a, zb_b = bf_tile(P, "zb_a"), bf_tile(P, "zb_b")
+        unmerge(homes[0], 0, (0, 1, 2, 3))
+        weave(on_scalar, homes[0], zb[0][:])
+        unmerge(homes[1], 256, (1, 2, 3))
+        multiply(zb[0][:], 0, 256, PACK)
+        unmerge(homes[1], 256, (0,))
+        weave(on_scalar, homes[1], zb[1][:])
+        store(0, 256, PACK, joined=True)
+        unmerge(homes[2], 512, (0, 1, 2))
+        multiply(zb[1][:], 256, 256)
+        unmerge(homes[2], 512, (3,))
+        o0 = bf_tile(256, "zb1")
+        weave(on_scalar, res[0][:, :, 0:P], o0[:, 0:512])
+        weave(on_scalar, homes[2], zb[2][:])
+        store(256, 256)
+        unmerge(home_a, 768, (1, 2, 3))
+        unmerge(home_b, 896, (3,))
+        weave(on_vector, res[0][:, :, P:256], o0[:, 512:1024])
+        multiply(zb[2][:], 512, 256)
+        unmerge(home_a, 768, (0,))
+        weave(on_scalar, home_a, zb_a[:])
+        unmerge(home_b, 896, (0, 1, 2))
+        multiply(zb_a[:], 768, P)
+        weave(on_vector, home_b, zb_b[:])
+        codes0 = code_tile(256, "mg0")
+        hand_on(codes0[:], o0[:], 0, 256)
+        store_words(codes0[:], 0, 256)
+        store(512, 256)
+        multiply(zb_b[:], 896, P)
+        o1 = bf_tile(256, "zb_a")
+        weave(on_scalar, res[256][:, :, 0:P], o1[:, 0:512])
+        weave(on_vector, res[256][:, :, P:256], o1[:, 512:1024])
+        store(768, P)
+        o2 = bf_tile(256, "o2")
+        weave(on_vector, res[512][:], o2[:])
+        codes12 = code_tile(512, "codes12")
+        hand_on(codes12[:, 0:256], o1[:], 256, 256)
+        hand_on(codes12[:, 256:512], o2[:], 512, 256)
+        store_words(codes12[:], 256, 512)
+        store(896, P, joined=True)
+        o3 = bf_tile(256, "o3")
+        weave(on_vector, res[768][:], o3[:, 0:512])
+        weave(on_vector, res[896][:], o3[:, 512:1024])
+        codes3 = code_tile(256, "codes3")
+        hand_on(codes3[:], o3[:], 768, 256)
+        store_words(codes3[:], 768, 256)
 
         for q in range(4):
-            (nc.scalar if q < 3 else nc.sync).dma_start(
+            (nc.scalar if q % 2 else nc.sync).dma_start(
                 out=out_2[0, 4 * q : 4 * q + 4, :].bitcast(I32), in_=o_scales[32 * q : 32 * q + 4, :].bitcast(I32)
             )

@@ -19,7 +19,7 @@ ACT = mybir.ActivationFunctionType
 P = 128
 PACK = 4
 BANK = 512
-WORD_PIECES = (256, 256, 256, 256)
+WORD_PIECES = (512, 256, 128, 128)
 SLOT = 256
 HALF = V // 2
 
@@ -30,7 +30,7 @@ def tile_picked_tome8_silu_po_kernel(
     nc = tc.nc
     with ExitStack() as ctx:
         keep = ctx.enter_context(tc.tile_pool(name="keep", bufs=1))
-        psum = ctx.enter_context(tc.psum_pool(name="psum", bufs=4))
+        psum = ctx.enter_context(tc.psum_pool(name="psum", bufs=1))
         psum_mix = ctx.enter_context(tc.psum_pool(name="psum_mix", bufs=1))
 
         def load_scale_rows(plane, rows, queue):
@@ -62,47 +62,58 @@ def tile_picked_tome8_silu_po_kernel(
         wa_sb = keep.tile([P, V], F32)
         w2w_raw = keep.tile([P, N], I32, align_bytes=64)
         nc.sync.dma_start(offs_sb[:], offs)
-        nc.sync.dma_start(out=w1_raw[:, 0, :], in_=w1_rows[:, 0, :])
         nc.sync.dma_start(a1_sb[:], a1)
+        nc.sync.dma_start(a2_sb[:], a2)
         load_scale_rows(xs_all, x_scales, nc.sync)
-        nc.sync.dma_start(out=w1_raw[:, 1:PACK, :], in_=w1_rows[:, 1:PACK, :])
         nc.sync.dma_start(out=xw_all[:], in_=x_words[0].rearrange("p c r -> p (c r)").bitcast(I32))
+        nc.sync.dma_start(out=w1_raw[:], in_=w1_rows)
         nc.sync.dma_start(out=wa_sb[:], in_=wa.rearrange("(p j) v -> p j v", j=PACK)[:, 0, :])
         nc.sync.dma_start(out=w2w_raw[:], in_=w2_words[0].rearrange("p c r -> p (c r)").bitcast(I32))
         load_scale_rows(w2s_raw, w2_scales, nc.sync)
-        nc.sync.dma_start(a2_sb[:], a2)
         nc.sync.dma_start(back_sb[:], back)
 
         xs = keep.tile([P, S], U8, align_bytes=64)
         nc.vector.tensor_copy(xs[:], xs_all[:].indirect(offs_sb[:]))
+        xw = keep.tile([P, S], U32, align_bytes=64)
+        nc.vector.tensor_copy(xw[:], xw_all[:].bitcast(U32).indirect(offs_sb[:]))
 
         w1_bf = keep.tile([P, H * PACK], BF16, align_bytes=64)
         w1_dealt = w1_bf[:].rearrange("p (t m j) -> p m j t", t=PACK, j=PACK)
         w1_cols = w1_raw[:].rearrange("p j (m t) -> p m j t", t=PACK)
         w1_codes = keep.tile([P, H], U32, align_bytes=64)
         w1_scales = keep.tile([P, H], U8, align_bytes=64)
-        nc.scalar.copy(out=w1_dealt[:, 0:64, :, :], in_=w1_cols[:, 0:64, :, :])
-        nc.vector.tensor_copy(out=w1_dealt[:, 64:P, :, :], in_=w1_cols[:, 64:P, :, :])
-        nc.vector.quantize_mx(out=w1_codes[:].bitcast(FP8X4), scales=w1_scales[:], in_=w1_bf[:])
 
-        xw = keep.tile([P, S], U32, align_bytes=64)
-        j0 = 0
-        for width in WORD_PIECES:
-            nc.vector.tensor_copy(
-                xw[:, j0 : j0 + width], xw_all[:].bitcast(U32).indirect(offs_sb[:, j0 // 16 : (j0 + width) // 16])
+        def round_w1(t0, t1, split):
+            nc.scalar.copy(out=w1_dealt[:, 0:split, :, t0:t1], in_=w1_cols[:, 0:split, :, t0:t1])
+            nc.vector.tensor_copy(out=w1_dealt[:, split:P, :, t0:t1], in_=w1_cols[:, split:P, :, t0:t1])
+
+        def quantise_w1(t0, t1):
+            nc.vector.quantize_mx(
+                out=w1_codes[:, t0 * P : t1 * P].bitcast(FP8X4),
+                scales=w1_scales[:, t0 * P : t1 * P],
+                in_=w1_bf[:, t0 * P * PACK : t1 * P * PACK],
             )
-            j0 = j0 + width
+
+        round_w1(0, 2, 48)
+        quantise_w1(0, 1)
+        quantise_w1(1, 2)
+        round_w1(2, 4, 80)
+        quantise_w1(2, 4)
 
         wb_sb = keep.tile([P, V], F32)
         nc.scalar.activation(wb_sb[:], wa_sb[:], ACT.Copy, bias=1.0, scale=-1.0)
 
         y = [keep.tile([P, S], F32, name="y%d" % t) for t in range(PACK)]
-        for t in range(PACK):
+
+        def first_product(t):
             cols = slice(t * P, (t + 1) * P)
             j0 = 0
-            for width in WORD_PIECES if t == 0 else (BANK, BANK):
+            for i, width in enumerate(WORD_PIECES if t == 0 else (BANK, BANK)):
                 picked = slice(j0, j0 + width)
-                acc = psum.tile([P, BANK], F32, name="acc")
+                if t == 0:
+                    acc = psum_mix.tile([P, BANK], F32, name="summed%d" % i)
+                else:
+                    acc = psum.tile([P, BANK], F32, name="acc%d" % (2 * (1 - t % 2) + i))
                 nc.tensor.matmul_mx(
                     out=acc[:, 0:width],
                     lhsT=w1_codes[:, cols].bitcast(FP8X4),
@@ -112,8 +123,14 @@ def tile_picked_tome8_silu_po_kernel(
                     start=True,
                     stop=True,
                 )
-                nc.scalar.copy(out=y[t][:, picked], in_=acc[:, 0:width])
+                if t == 0 and i in (1, 2):
+                    nc.vector.tensor_copy(out=y[t][:, picked], in_=acc[:, 0:width])
+                else:
+                    nc.scalar.copy(out=y[t][:, picked], in_=acc[:, 0:width])
                 j0 = j0 + width
+
+        for t in range(PACK):
+            first_product(t)
 
         w2_codes = keep.tile([P, N], U32, align_bytes=64)
         nc.vector.tensor_copy(
@@ -122,8 +139,8 @@ def tile_picked_tome8_silu_po_kernel(
         )
         w2_sc = keep.tile([P, N], U8, align_bytes=64)
         nc.vector.tensor_copy(
-            out=w2_sc[:].rearrange("p (t m) -> p m t", t=PACK),
-            in_=w2s_raw[:].rearrange("p (m t) -> p m t", t=PACK),
+            out=w2_sc[:].rearrange("p (t m) -> p t m", t=PACK),
+            in_=w2s_raw[:].rearrange("p (m t) -> p t m", t=PACK),
         )
 
         mg = [keep.tile([P, V], F32, name="mg%d" % t, align_bytes=64) for t in range(PACK)]
@@ -144,29 +161,30 @@ def tile_picked_tome8_silu_po_kernel(
                 second[t][:, v0:v1], y[t][:].indirect(a2_sb[:, v0 // 16 : v1 // 16]), wb_sb[:, v0:v1], ALU.mult
             )
 
-        def mix(t, spans, sum_tags, turn_tags, homes):
-            for (v0, v1), tag, home in zip(spans, sum_tags, homes):
-                summed = psum_mix.tile([P, v1 - v0], F32, name="summed", tag=tag)
-                for v in range(v0, v1, P):
-                    for k, part in enumerate((first[t], second[t])):
-                        nc.tensor.matmul(
-                            summed[:, v - v0 : v - v0 + P],
-                            part[:, v : v + P],
-                            ident[:],
-                            start=(k == 0),
-                            stop=(k == 1),
-                            is_transpose=True,
-                        )
-                nc.scalar.activation(home, summed[:].rearrange("p (b v) -> p b v", v=P), ACT.Silu)
-            for (v0, v1), tag, home in zip(spans, turn_tags, homes):
-                turned = psum_mix.tile([P, v1 - v0], F32, name="turned", tag=tag)
-                for b in reversed(range((v1 - v0) // P)):
-                    nc.tensor.transpose(turned[:, b * P : (b + 1) * P], home[:, b, :], ident[:])
-                nc.scalar.copy(out=mg[t][:, v0:v1], in_=turned[:])
+        def open_sums(t):
+            for b in range(V // P):
+                summed[b] = psum_mix.tile([P, P], F32, name="summed%d" % b)
+                nc.tensor.matmul(
+                    summed[b][:], first[t][:, b * P : (b + 1) * P], ident[:], start=True, stop=False, is_transpose=True
+                )
 
-        def mix_on_vector(t, v0, v1, summed):
-            nc.vector.tensor_tensor(summed, first[t][:, v0:v1], second[t][:, v0:v1], ALU.add)
-            nc.scalar.activation(mg[t][:, v0:v1], summed, ACT.Silu)
+        def mix(t, homes):
+            for b in range(V // P):
+                nc.tensor.matmul(
+                    summed[b][:], second[t][:, b * P : (b + 1) * P], ident[:], start=False, stop=True, is_transpose=True
+                )
+                nc.scalar.activation(homes[b], summed[b][:], ACT.Silu)
+            for h in range(2):
+                turned = psum.tile([P, HALF], F32, name="acc%d" % (2 + h))
+                for i in range(2):
+                    nc.tensor.transpose(turned[:, i * P : (i + 1) * P], homes[2 * h + i], ident[:])
+                nc.scalar.copy(out=mg[t][:, h * HALF : (h + 1) * HALF], in_=turned[:])
+
+        summed = {}
+
+        def mix_on_vector(t, v0, v1, total):
+            nc.vector.tensor_tensor(total, first[t][:, v0:v1], second[t][:, v0:v1], ALU.add)
+            nc.scalar.activation(mg[t][:, v0:v1], total, ACT.Silu)
 
         z_codes = keep.tile([P, S], U32, align_bytes=64)
         z_scales = keep.tile([P, S], U8, align_bytes=64)
@@ -176,19 +194,19 @@ def tile_picked_tome8_silu_po_kernel(
         res = {}
         banks = {}
 
-        halves = ((0, HALF), (HALF, V))
         z_ring = keep.tile([P, 8 * SLOT], F32)
-        bank = ["m%d" % b for b in range(4)]
         for t in range(PACK - 1):
             take_first(t, 0, V, "first%d" % (t % 2))
-            take_second(t, 0, V, "second%d" % t)
-            mixed = keep.tile([P, 2, 2, P], F32, name="mixed", tag="mixed%d" % (t % 2))
-            homes = [mixed[:, 0, :, :], mixed[:, 1, :, :]]
+            open_sums(t)
+            take_second(t, 0, V, "second%d" % (t % 2))
+            mixed = keep.tile([P, V], F32, name="mixed", tag="mixed%d" % (t % 2))
+            homes = [mixed[:, b * P : (b + 1) * P] for b in range(V // P)]
             if t == 1:
-                homes[1] = z_ring[:, 0:SLOT].rearrange("p (b v) -> p b v", b=2)
+                homes[3] = z_ring[:, 0:P]
             if t == 2:
-                homes[1] = z_ring[:, SLOT : 7 * SLOT].rearrange("p (b v) -> p b v", b=2)[:, :, 0:P]
-            mix(t, halves, (bank[t], bank[t + 1]), (bank[(t + 2) % 4], bank[(t + 3) % 4]), homes)
+                homes[2] = z_ring[:, 4 * SLOT : 4 * SLOT + P]
+                homes[3] = z_ring[:, SLOT : SLOT + P]
+            mix(t, homes)
         take_first(PACK - 1, 0, V, "first1")
         take_second(PACK - 1, 0, V, "mixed1")
         mix_on_vector(PACK - 1, 0, V, z_ring[:, 4 * SLOT : 6 * SLOT])
@@ -226,7 +244,7 @@ def tile_picked_tome8_silu_po_kernel(
             span = min(width, BANK // per_bank)
             for s0 in range(j0, j0 + width, span):
                 for t0 in range(0, PACK, per_bank):
-                    acc = psum.tile([P, per_bank, span], F32, name="acc")
+                    acc = psum.tile([P, per_bank, span], F32, name="acc%d" % (len(banks) % 4))
                     banks[s0, t0] = acc
                     for i in range(per_bank):
                         rows = slice((t0 + i) * P, (t0 + i + 1) * P)

@@ -22,6 +22,7 @@ BANK = 512
 WORD_PIECES = (512, 256, 128, 128)
 SLOT = 256
 HALF = V // 2
+EARLY = 512
 
 
 def tile_picked_tome8_silu_po_kernel(
@@ -45,7 +46,7 @@ def tile_picked_tome8_silu_po_kernel(
         back_sb = keep.tile([P, S // 16], U16)
 
         xs_all = keep.tile([P, T], U8, align_bytes=64)
-        nc.vector.memset(xs_all[:].bitcast(I32), 0)
+        nc.gpsimd.memset(xs_all[:].bitcast(I32), 0)
         w2s_raw = keep.tile([P, N], U8, align_bytes=64)
         nc.vector.memset(w2s_raw[:].bitcast(I32), 0)
         warm = keep.tile([P, 2], F32)
@@ -61,14 +62,16 @@ def tile_picked_tome8_silu_po_kernel(
         xw_all = keep.tile([P, T], I32, align_bytes=64)
         wa_sb = keep.tile([P, V], F32)
         w2w_raw = keep.tile([P, N], I32, align_bytes=64)
+        x_rows = x_words[0].rearrange("p c r -> p (c r)").bitcast(I32)
+        nc.sync.dma_start(out=xw_all[:, 0:EARLY], in_=x_rows[:, 0:EARLY])
         nc.sync.dma_start(offs_sb[:], offs)
-        nc.sync.dma_start(a1_sb[:], a1)
-        nc.sync.dma_start(a2_sb[:], a2)
         load_scale_rows(xs_all, x_scales, nc.sync)
-        nc.sync.dma_start(out=xw_all[:], in_=x_words[0].rearrange("p c r -> p (c r)").bitcast(I32))
+        nc.sync.dma_start(out=xw_all[:, EARLY:T], in_=x_rows[:, EARLY:T])
         nc.sync.dma_start(out=w1_raw[:], in_=w1_rows)
         nc.sync.dma_start(out=wa_sb[:], in_=wa.rearrange("(p j) v -> p j v", j=PACK)[:, 0, :])
         nc.sync.dma_start(out=w2w_raw[:], in_=w2_words[0].rearrange("p c r -> p (c r)").bitcast(I32))
+        nc.sync.dma_start(a1_sb[:], a1)
+        nc.sync.dma_start(a2_sb[:], a2)
         load_scale_rows(w2s_raw, w2_scales, nc.sync)
         nc.sync.dma_start(back_sb[:], back)
 
@@ -94,7 +97,7 @@ def tile_picked_tome8_silu_po_kernel(
                 in_=w1_bf[:, t0 * P * PACK : t1 * P * PACK],
             )
 
-        round_w1(0, 2, 48)
+        round_w1(0, 2, 96)
         quantise_w1(0, 1)
         quantise_w1(1, 2)
         round_w1(2, 4, 80)

@@ -23,6 +23,7 @@ WORD_PIECES = (512, 256, 128, 128)
 SLOT = 256
 HALF = V // 2
 EARLY = 512
+PART_AT = ((384, 1024), (0, 512), (1408, 0), (512, 1024))
 
 
 def tile_picked_tome8_silu_po_kernel(
@@ -35,10 +36,8 @@ def tile_picked_tome8_silu_po_kernel(
         psum_mix = ctx.enter_context(tc.psum_pool(name="psum_mix", bufs=1))
 
         def load_scale_rows(plane, rows, queue):
-            for q in range(4):
-                queue.dma_start(
-                    out=plane[32 * q : 32 * q + 4, :].bitcast(I32), in_=rows[0, 4 * q : 4 * q + 4, :].bitcast(I32)
-                )
+            for r in range(4):
+                queue.dma_start(out=plane[r:P:32, :].bitcast(I32), in_=rows[0, r:16:4, :].bitcast(I32))
 
         offs_sb = keep.tile([P, S // 16], U16)
         a1_sb = keep.tile([P, V // 16], U16)
@@ -46,7 +45,7 @@ def tile_picked_tome8_silu_po_kernel(
         back_sb = keep.tile([P, S // 16], U16)
 
         xs_all = keep.tile([P, T], U8, align_bytes=64)
-        nc.gpsimd.memset(xs_all[:].bitcast(I32), 0)
+        nc.vector.memset(xs_all[:].bitcast(I32), 0)
         w2s_raw = keep.tile([P, N], U8, align_bytes=64)
         nc.vector.memset(w2s_raw[:].bitcast(I32), 0)
         warm = keep.tile([P, 2], F32)
@@ -70,9 +69,9 @@ def tile_picked_tome8_silu_po_kernel(
         nc.sync.dma_start(out=w1_raw[:], in_=w1_rows)
         nc.sync.dma_start(out=wa_sb[:], in_=wa.rearrange("(p j) v -> p j v", j=PACK)[:, 0, :])
         nc.sync.dma_start(out=w2w_raw[:], in_=w2_words[0].rearrange("p c r -> p (c r)").bitcast(I32))
+        load_scale_rows(w2s_raw, w2_scales, nc.sync)
         nc.sync.dma_start(a1_sb[:], a1)
         nc.sync.dma_start(a2_sb[:], a2)
-        load_scale_rows(w2s_raw, w2_scales, nc.sync)
         nc.sync.dma_start(back_sb[:], back)
 
         xs = keep.tile([P, S], U8, align_bytes=64)
@@ -97,7 +96,7 @@ def tile_picked_tome8_silu_po_kernel(
                 in_=w1_bf[:, t0 * P * PACK : t1 * P * PACK],
             )
 
-        round_w1(0, 2, 96)
+        round_w1(0, 2, 64)
         quantise_w1(0, 1)
         quantise_w1(1, 2)
         round_w1(2, 4, 80)
@@ -150,16 +149,16 @@ def tile_picked_tome8_silu_po_kernel(
         first = {}
         second = {}
 
+        parts = keep.tile([P, 1920], F32)
+
         def take_first(t, v0, v1, tag):
-            if v0 == 0:
-                first[t] = keep.tile([P, V], F32, name="first", tag=tag)
+            first[t] = parts[:, PART_AT[t][0] : PART_AT[t][0] + V]
             nc.vector.tensor_tensor(
                 first[t][:, v0:v1], y[t][:].indirect(a1_sb[:, v0 // 16 : v1 // 16]), wa_sb[:, v0:v1], ALU.mult
             )
 
         def take_second(t, v0, v1, tag):
-            if v0 == 0:
-                second[t] = keep.tile([P, V], F32, name="second", tag=tag)
+            second[t] = parts[:, PART_AT[t][1] : PART_AT[t][1] + V]
             nc.vector.tensor_tensor(
                 second[t][:, v0:v1], y[t][:].indirect(a2_sb[:, v0 // 16 : v1 // 16]), wb_sb[:, v0:v1], ALU.mult
             )
@@ -333,7 +332,7 @@ def tile_picked_tome8_silu_po_kernel(
         hand_on(codes3[:], o3[:], 768, 256)
         store_words(codes3[:], 768, 256)
 
-        for q in range(4):
-            (nc.scalar if q % 2 else nc.sync).dma_start(
-                out=out_2[0, 4 * q : 4 * q + 4, :].bitcast(I32), in_=o_scales[32 * q : 32 * q + 4, :].bitcast(I32)
+        for r in range(4):
+            (nc.scalar if r % 2 else nc.sync).dma_start(
+                out=out_2[0, r:16:4, :].bitcast(I32), in_=o_scales[r:P:32, :].bitcast(I32)
             )

@@ -17,27 +17,37 @@ ALU = mybir.AluOpType
 ACT = mybir.ActivationFunctionType
 
 P = 128
-PACK = 4
+PLANES = 4
+QUADRANT = 32
 BANK = 512
-WORD_PIECES = (512, 256, 128, 128)
-SLOT = 256
-HALF = V // 2
-EARLY = 512
-PART_AT = ((384, 1024), (0, 512), (1408, 0), (512, 1024))
+BLOCKS = V // P
+CHUNK = 256
+STRIP = CHUNK // 2
+LAST = PLANES - 1
+
+EARLY_WORDS = T // 4
+PLANE0_PASSES = (512, 256, 128, 128)
+W1_SCALAR_COLS = (96, 80)
+PART_AT = ((V - P, 2 * V), (0, V), (3 * V - P, 0), (V, 2 * V))
 
 
 def tile_picked_tome8_silu_po_kernel(
     tc, x_words, x_scales, w1, wa, w2_words, w2_scales, offs, a1, a2, back, out_0, out_1, out_2
 ):
     nc = tc.nc
+    on_scalar, on_vector = nc.scalar.copy, nc.vector.tensor_copy
     with ExitStack() as ctx:
         keep = ctx.enter_context(tc.tile_pool(name="keep", bufs=1))
         psum = ctx.enter_context(tc.psum_pool(name="psum", bufs=1))
         psum_mix = ctx.enter_context(tc.psum_pool(name="psum_mix", bufs=1))
 
-        def load_scale_rows(plane, rows, queue):
+        def scale_rows(tile, rows, r):
+            return tile[r:P:QUADRANT, :].bitcast(I32), rows[0, r:16:4, :].bitcast(I32)
+
+        def load_scales(tile, rows):
             for r in range(4):
-                queue.dma_start(out=plane[r:P:32, :].bitcast(I32), in_=rows[0, r:16:4, :].bitcast(I32))
+                in_sbuf, in_hbm = scale_rows(tile, rows, r)
+                nc.sync.dma_start(out=in_sbuf, in_=in_hbm)
 
         offs_sb = keep.tile([P, S // 16], U16)
         a1_sb = keep.tile([P, V // 16], U16)
@@ -56,20 +66,19 @@ def tile_picked_tome8_silu_po_kernel(
         nc.vector.memset(ident[:], 0.0)
         make_identity(nc, ident[:], nomemset=True)
 
-        w1_rows = w1.rearrange("(p j) c -> p j c", j=PACK)
-        w1_raw = keep.tile([P, PACK, H], F32)
+        w1_raw = keep.tile([P, PLANES, H], F32)
         xw_all = keep.tile([P, T], I32, align_bytes=64)
         wa_sb = keep.tile([P, V], F32)
         w2w_raw = keep.tile([P, N], I32, align_bytes=64)
         x_rows = x_words[0].rearrange("p c r -> p (c r)").bitcast(I32)
-        nc.sync.dma_start(out=xw_all[:, 0:EARLY], in_=x_rows[:, 0:EARLY])
+        nc.sync.dma_start(out=xw_all[:, 0:EARLY_WORDS], in_=x_rows[:, 0:EARLY_WORDS])
         nc.sync.dma_start(offs_sb[:], offs)
-        load_scale_rows(xs_all, x_scales, nc.sync)
-        nc.sync.dma_start(out=xw_all[:, EARLY:T], in_=x_rows[:, EARLY:T])
-        nc.sync.dma_start(out=w1_raw[:], in_=w1_rows)
-        nc.sync.dma_start(out=wa_sb[:], in_=wa.rearrange("(p j) v -> p j v", j=PACK)[:, 0, :])
+        load_scales(xs_all, x_scales)
+        nc.sync.dma_start(out=xw_all[:, EARLY_WORDS:T], in_=x_rows[:, EARLY_WORDS:T])
+        nc.sync.dma_start(out=w1_raw[:], in_=w1.rearrange("(p j) c -> p j c", j=PLANES))
+        nc.sync.dma_start(out=wa_sb[:], in_=wa.rearrange("(p j) v -> p j v", j=PLANES)[:, 0, :])
         nc.sync.dma_start(out=w2w_raw[:], in_=w2_words[0].rearrange("p c r -> p (c r)").bitcast(I32))
-        load_scale_rows(w2s_raw, w2_scales, nc.sync)
+        load_scales(w2s_raw, w2_scales)
         nc.sync.dma_start(a1_sb[:], a1)
         nc.sync.dma_start(a2_sb[:], a2)
         nc.sync.dma_start(back_sb[:], back)
@@ -79,38 +88,38 @@ def tile_picked_tome8_silu_po_kernel(
         xw = keep.tile([P, S], U32, align_bytes=64)
         nc.vector.tensor_copy(xw[:], xw_all[:].bitcast(U32).indirect(offs_sb[:]))
 
-        w1_bf = keep.tile([P, H * PACK], BF16, align_bytes=64)
-        w1_dealt = w1_bf[:].rearrange("p (t m j) -> p m j t", t=PACK, j=PACK)
-        w1_cols = w1_raw[:].rearrange("p j (m t) -> p m j t", t=PACK)
+        w1_bf = keep.tile([P, H * PLANES], BF16, align_bytes=64)
+        w1_dealt = w1_bf[:].rearrange("p (t m j) -> p m j t", t=PLANES, j=PLANES)
+        w1_cols = w1_raw[:].rearrange("p j (m t) -> p m j t", t=PLANES)
         w1_codes = keep.tile([P, H], U32, align_bytes=64)
         w1_scales = keep.tile([P, H], U8, align_bytes=64)
 
         def round_w1(t0, t1, split):
-            nc.scalar.copy(out=w1_dealt[:, 0:split, :, t0:t1], in_=w1_cols[:, 0:split, :, t0:t1])
-            nc.vector.tensor_copy(out=w1_dealt[:, split:P, :, t0:t1], in_=w1_cols[:, split:P, :, t0:t1])
+            on_scalar(out=w1_dealt[:, 0:split, :, t0:t1], in_=w1_cols[:, 0:split, :, t0:t1])
+            on_vector(out=w1_dealt[:, split:P, :, t0:t1], in_=w1_cols[:, split:P, :, t0:t1])
 
         def quantise_w1(t0, t1):
             nc.vector.quantize_mx(
                 out=w1_codes[:, t0 * P : t1 * P].bitcast(FP8X4),
                 scales=w1_scales[:, t0 * P : t1 * P],
-                in_=w1_bf[:, t0 * P * PACK : t1 * P * PACK],
+                in_=w1_bf[:, t0 * P * PLANES : t1 * P * PLANES],
             )
 
-        round_w1(0, 2, 64)
+        round_w1(0, 2, W1_SCALAR_COLS[0])
         quantise_w1(0, 1)
         quantise_w1(1, 2)
-        round_w1(2, 4, 80)
+        round_w1(2, 4, W1_SCALAR_COLS[1])
         quantise_w1(2, 4)
 
         wb_sb = keep.tile([P, V], F32)
         nc.scalar.activation(wb_sb[:], wa_sb[:], ACT.Copy, bias=1.0, scale=-1.0)
 
-        y = [keep.tile([P, S], F32, name="y%d" % t) for t in range(PACK)]
-
-        def first_product(t):
+        y = [keep.tile([P, S], F32, name="y%d" % t) for t in range(PLANES)]
+        plane0_copies = (on_scalar, on_vector, on_vector, on_scalar)
+        for t in range(PLANES):
             cols = slice(t * P, (t + 1) * P)
             j0 = 0
-            for i, width in enumerate(WORD_PIECES if t == 0 else (BANK, BANK)):
+            for i, width in enumerate(PLANE0_PASSES if t == 0 else (BANK, BANK)):
                 picked = slice(j0, j0 + width)
                 if t == 0:
                     acc = psum_mix.tile([P, BANK], F32, name="summed%d" % i)
@@ -125,108 +134,78 @@ def tile_picked_tome8_silu_po_kernel(
                     start=True,
                     stop=True,
                 )
-                if t == 0 and i in (1, 2):
-                    nc.vector.tensor_copy(out=y[t][:, picked], in_=acc[:, 0:width])
-                else:
-                    nc.scalar.copy(out=y[t][:, picked], in_=acc[:, 0:width])
+                engine_copy = plane0_copies[i] if t == 0 else on_scalar
+                engine_copy(out=y[t][:, picked], in_=acc[:, 0:width])
                 j0 = j0 + width
 
-        for t in range(PACK):
-            first_product(t)
-
         w2_codes = keep.tile([P, N], U32, align_bytes=64)
-        nc.vector.tensor_copy(
-            out=w2_codes[:].rearrange("p (t m) -> p m t", t=PACK),
-            in_=w2w_raw[:].bitcast(U32).rearrange("p (m t) -> p m t", t=PACK),
+        on_vector(
+            out=w2_codes[:].rearrange("p (t m) -> p m t", t=PLANES),
+            in_=w2w_raw[:].bitcast(U32).rearrange("p (m t) -> p m t", t=PLANES),
         )
         w2_sc = keep.tile([P, N], U8, align_bytes=64)
-        nc.vector.tensor_copy(
-            out=w2_sc[:].rearrange("p (t m) -> p t m", t=PACK),
-            in_=w2s_raw[:].rearrange("p (m t) -> p t m", t=PACK),
+        on_vector(
+            out=w2_sc[:].rearrange("p (t m) -> p t m", t=PLANES),
+            in_=w2s_raw[:].rearrange("p (m t) -> p t m", t=PLANES),
         )
 
-        mg = [keep.tile([P, V], F32, name="mg%d" % t, align_bytes=64) for t in range(PACK)]
-        first = {}
-        second = {}
+        mg = [keep.tile([P, V], F32, name="mg%d" % t, align_bytes=64) for t in range(PLANES)]
+        parts = keep.tile([P, 4 * V - P], F32)
 
-        parts = keep.tile([P, 1920], F32)
-
-        def take_first(t, v0, v1, tag):
-            first[t] = parts[:, PART_AT[t][0] : PART_AT[t][0] + V]
-            nc.vector.tensor_tensor(
-                first[t][:, v0:v1], y[t][:].indirect(a1_sb[:, v0 // 16 : v1 // 16]), wa_sb[:, v0:v1], ALU.mult
-            )
-
-        def take_second(t, v0, v1, tag):
-            second[t] = parts[:, PART_AT[t][1] : PART_AT[t][1] + V]
-            nc.vector.tensor_tensor(
-                second[t][:, v0:v1], y[t][:].indirect(a2_sb[:, v0 // 16 : v1 // 16]), wb_sb[:, v0:v1], ALU.mult
-            )
-
-        def open_sums(t):
-            for b in range(V // P):
-                summed[b] = psum_mix.tile([P, P], F32, name="summed%d" % b)
-                nc.tensor.matmul(
-                    summed[b][:], first[t][:, b * P : (b + 1) * P], ident[:], start=True, stop=False, is_transpose=True
-                )
-
-        def mix(t, homes):
-            for b in range(V // P):
-                nc.tensor.matmul(
-                    summed[b][:], second[t][:, b * P : (b + 1) * P], ident[:], start=False, stop=True, is_transpose=True
-                )
-                nc.scalar.activation(homes[b], summed[b][:], ACT.Silu)
-            for h in range(2):
-                turned = psum.tile([P, HALF], F32, name="acc%d" % (2 + h))
-                for i in range(2):
-                    nc.tensor.transpose(turned[:, i * P : (i + 1) * P], homes[2 * h + i], ident[:])
-                nc.scalar.copy(out=mg[t][:, h * HALF : (h + 1) * HALF], in_=turned[:])
-
-        summed = {}
-
-        def mix_on_vector(t, v0, v1, total):
-            nc.vector.tensor_tensor(total, first[t][:, v0:v1], second[t][:, v0:v1], ALU.add)
-            nc.scalar.activation(mg[t][:, v0:v1], total, ACT.Silu)
+        def take_part(t, which):
+            part = parts[:, PART_AT[t][which] : PART_AT[t][which] + V]
+            offsets, weight = ((a1_sb, wa_sb), (a2_sb, wb_sb))[which]
+            nc.vector.tensor_tensor(part, y[t][:].indirect(offsets[:]), weight[:], ALU.mult)
+            return part
 
         z_codes = keep.tile([P, S], U32, align_bytes=64)
         z_scales = keep.tile([P, S], U8, align_bytes=64)
         o_scales = keep.tile([P, S], U8, align_bytes=64)
-        out_rows = out_0.rearrange("(p t) j -> p t j", t=PACK)
+        z_stage = keep.tile([P, 8 * CHUNK], F32)
+
+        def slot(s, width=CHUNK):
+            return z_stage[:, s * CHUNK : s * CHUNK + width]
+
+        turned_homes = {(1, 3): slot(0, P), (2, 2): slot(4, P), (2, 3): slot(1, P)}
+        for t in range(LAST):
+            first = take_part(t, 0)
+            summed = [psum_mix.tile([P, P], F32, name="summed%d" % b) for b in range(BLOCKS)]
+            for b in range(BLOCKS):
+                nc.tensor.matmul(
+                    summed[b][:], first[:, b * P : (b + 1) * P], ident[:], start=True, stop=False, is_transpose=True
+                )
+            second = take_part(t, 1)
+            mixed = keep.tile([P, V], F32, name="mixed", tag="mixed%d" % (t % 2))
+            silu_t = [turned_homes.get((t, b), mixed[:, b * P : (b + 1) * P]) for b in range(BLOCKS)]
+            for b in range(BLOCKS):
+                nc.tensor.matmul(
+                    summed[b][:], second[:, b * P : (b + 1) * P], ident[:], start=False, stop=True, is_transpose=True
+                )
+                nc.scalar.activation(silu_t[b], summed[b][:], ACT.Silu)
+            for h in range(2):
+                back_turned = psum.tile([P, 2 * P], F32, name="acc%d" % (2 + h))
+                for i in range(2):
+                    nc.tensor.transpose(back_turned[:, i * P : (i + 1) * P], silu_t[2 * h + i], ident[:])
+                on_scalar(out=mg[t][:, 2 * h * P : 2 * (h + 1) * P], in_=back_turned[:])
+
+        first = take_part(LAST, 0)
+        second = take_part(LAST, 1)
+        total = slot(4, V)
+        nc.vector.tensor_tensor(total, first, second, ALU.add)
+        nc.scalar.activation(mg[LAST][:], total, ACT.Silu)
+
+        out_rows = out_0.rearrange("(p t) j -> p t j", t=PLANES)
         out_words = out_1[0].rearrange("p c r -> p (c r)").bitcast(I32)
         res = {}
         banks = {}
 
-        z_ring = keep.tile([P, 8 * SLOT], F32)
-        for t in range(PACK - 1):
-            take_first(t, 0, V, "first%d" % (t % 2))
-            open_sums(t)
-            take_second(t, 0, V, "second%d" % (t % 2))
-            mixed = keep.tile([P, V], F32, name="mixed", tag="mixed%d" % (t % 2))
-            homes = [mixed[:, b * P : (b + 1) * P] for b in range(V // P)]
-            if t == 1:
-                homes[3] = z_ring[:, 0:P]
-            if t == 2:
-                homes[2] = z_ring[:, 4 * SLOT : 4 * SLOT + P]
-                homes[3] = z_ring[:, SLOT : SLOT + P]
-            mix(t, homes)
-        take_first(PACK - 1, 0, V, "first1")
-        take_second(PACK - 1, 0, V, "mixed1")
-        mix_on_vector(PACK - 1, 0, V, z_ring[:, 4 * SLOT : 6 * SLOT])
-
-
-        def woven(tile_bf):
-            return tile_bf.rearrange("p (c i t) -> p c t i", i=4, t=PACK)
-
-        def planes(tile_f32):
-            return tile_f32.rearrange("p t (c i) -> p c t i", i=4)
-
-        def z_home(col0, width, step=SLOT):
-            rows = z_ring[:, col0 : col0 + PACK * step].rearrange("p (t j) -> p t j", t=PACK)
+        def staged(col0, width):
+            rows = z_stage[:, col0 : col0 + PLANES * CHUNK].rearrange("p (t j) -> p t j", t=PLANES)
             return rows[:, :, 0:width]
 
-        def unmerge(home, j0, ts):
+        def unmerge(home, j0, planes):
             width = home.shape[2]
-            for t in ts:
+            for t in planes:
                 nc.vector.tensor_tensor(
                     home[:, t, :],
                     mg[t][:].indirect(back_sb[:, j0 // 16 : (j0 + width) // 16]),
@@ -235,17 +214,20 @@ def tile_picked_tome8_silu_po_kernel(
                 )
 
         def weave(engine_copy, source, target):
-            engine_copy(out=woven(target), in_=planes(source))
+            engine_copy(
+                out=target.rearrange("p (c i t) -> p c t i", i=4, t=PLANES),
+                in_=source.rearrange("p t (c i) -> p c t i", i=4),
+            )
 
-        def bf_tile(width, tag):
-            return keep.tile([P, width * PACK], BF16, name="bf", tag=tag, align_bytes=64)
+        def woven_tile(width, tag):
+            return keep.tile([P, width * PLANES], BF16, name="woven", tag=tag, align_bytes=64)
 
-        def multiply(z_bf, j0, width, per_bank=2):
+        def multiply(z_woven, j0, width, per_bank=2):
             cols = slice(j0, j0 + width)
-            nc.vector.quantize_mx(out=z_codes[:, cols].bitcast(FP8X4), scales=z_scales[:, cols], in_=z_bf)
+            nc.vector.quantize_mx(out=z_codes[:, cols].bitcast(FP8X4), scales=z_scales[:, cols], in_=z_woven)
             span = min(width, BANK // per_bank)
             for s0 in range(j0, j0 + width, span):
-                for t0 in range(0, PACK, per_bank):
+                for t0 in range(0, PLANES, per_bank):
                     acc = psum.tile([P, per_bank, span], F32, name="acc%d" % (len(banks) % 4))
                     banks[s0, t0] = acc
                     for i in range(per_bank):
@@ -260,79 +242,85 @@ def tile_picked_tome8_silu_po_kernel(
                             stop=True,
                         )
 
-        def store(j0, width, per_bank=2, copies=None, joined=False):
-            res[j0] = keep.tile([P, PACK, width], F32, name="res%d" % j0)
+        def store(j0, width, per_bank=2, joined=False):
+            res[j0] = keep.tile([P, PLANES, width], F32, name="res%d" % j0)
             span = min(width, BANK // per_bank)
-            parts = [(s0, t0) for s0 in range(0, width, span) for t0 in range(0, PACK, per_bank)]
-            for (s0, t0), engine_copy in zip(parts, copies or (on_scalar, on_scalar)):
-                held = res[j0][:, t0 : t0 + per_bank, s0 : s0 + span]
-                engine_copy(out=held, in_=banks[j0 + s0, t0][:])
-                if not joined:
-                    nc.sync.dma_start(out=out_rows[:, t0 : t0 + per_bank, j0 + s0 : j0 + s0 + span], in_=held)
+            for s0 in range(0, width, span):
+                for t0 in range(0, PLANES, per_bank):
+                    held = res[j0][:, t0 : t0 + per_bank, s0 : s0 + span]
+                    on_scalar(out=held, in_=banks[j0 + s0, t0][:])
+                    if not joined:
+                        nc.sync.dma_start(out=out_rows[:, t0 : t0 + per_bank, j0 + s0 : j0 + s0 + span], in_=held)
             if joined:
                 nc.sync.dma_start(out=out_rows[:, :, j0 : j0 + width], in_=res[j0][:])
 
         def code_tile(width, tag):
             return keep.tile([P, width], I32, name="o_codes", tag=tag, align_bytes=64)
 
-        def hand_on(codes, piece, j0, width):
-            nc.vector.quantize_mx(out=codes.bitcast(FP8X4), scales=o_scales[:, j0 : j0 + width], in_=piece)
+        def hand_on(codes, woven, j0):
+            nc.vector.quantize_mx(out=codes.bitcast(FP8X4), scales=o_scales[:, j0 : j0 + CHUNK], in_=woven)
 
-        def store_words(codes, j0, width):
-            nc.sync.dma_start(out=out_words[:, j0 : j0 + width], in_=codes)
+        def store_words(codes, j0):
+            nc.sync.dma_start(out=out_words[:, j0 : j0 + codes.shape[1]], in_=codes)
 
-        on_scalar, on_vector = nc.scalar.copy, nc.vector.tensor_copy
-        homes = [z_home(0, SLOT), z_home(3 * SLOT, SLOT), z_home(0, SLOT)]
-        home_a, home_b = z_home(3 * SLOT, P), z_home(SLOT + P, P)
-        zb = [bf_tile(SLOT, "zb%d" % c) for c in range(3)]
-        zb_a, zb_b = bf_tile(P, "zb_a"), bf_tile(P, "zb_b")
-        unmerge(homes[0], 0, (0, 1, 2, 3))
-        weave(on_scalar, homes[0], zb[0][:])
-        unmerge(homes[1], 256, (1, 2, 3))
-        multiply(zb[0][:], 0, 256, PACK)
-        unmerge(homes[1], 256, (0,))
-        weave(on_scalar, homes[1], zb[1][:])
-        store(0, 256, PACK, joined=True)
-        unmerge(homes[2], 512, (0, 1, 2))
-        multiply(zb[1][:], 256, 256)
-        unmerge(homes[2], 512, (3,))
-        o0 = bf_tile(256, "zb1")
-        weave(on_scalar, res[0][:, :, 0:P], o0[:, 0:512])
-        weave(on_scalar, homes[2], zb[2][:])
-        store(256, 256)
-        unmerge(home_a, 768, (1, 2, 3))
-        unmerge(home_b, 896, (3,))
-        weave(on_vector, res[0][:, :, P:256], o0[:, 512:1024])
-        multiply(zb[2][:], 512, 256)
-        unmerge(home_a, 768, (0,))
-        weave(on_scalar, home_a, zb_a[:])
-        unmerge(home_b, 896, (0, 1, 2))
-        multiply(zb_a[:], 768, P)
-        weave(on_vector, home_b, zb_b[:])
-        codes0 = code_tile(256, "mg0")
-        hand_on(codes0[:], o0[:], 0, 256)
-        store_words(codes0[:], 0, 256)
-        store(512, 256)
-        multiply(zb_b[:], 896, P)
-        o1 = bf_tile(256, "zb_a")
-        weave(on_scalar, res[256][:, :, 0:P], o1[:, 0:512])
-        weave(on_vector, res[256][:, :, P:256], o1[:, 512:1024])
-        store(768, P)
-        o2 = bf_tile(256, "o2")
-        weave(on_vector, res[512][:], o2[:])
-        codes12 = code_tile(512, "codes12")
-        hand_on(codes12[:, 0:256], o1[:], 256, 256)
-        hand_on(codes12[:, 256:512], o2[:], 512, 256)
-        store_words(codes12[:], 256, 512)
-        store(896, P, joined=True)
-        o3 = bf_tile(256, "o3")
-        weave(on_vector, res[768][:], o3[:, 0:512])
-        weave(on_vector, res[896][:], o3[:, 512:1024])
-        codes3 = code_tile(256, "codes3")
-        hand_on(codes3[:], o3[:], 768, 256)
-        store_words(codes3[:], 768, 256)
+        c0, c1, c2, c3 = (c * CHUNK for c in range(S // CHUNK))
+        c3b = c3 + STRIP
+        low, high = staged(0, CHUNK), staged(3 * CHUNK, CHUNK)
+        strip_a, strip_b = staged(3 * CHUNK, STRIP), staged(CHUNK + STRIP, STRIP)
+        zw = [woven_tile(CHUNK, "zw%d" % c) for c in range(3)]
+        zw_a, zw_b = woven_tile(STRIP, "zw_a"), woven_tile(STRIP, "zw_b")
+        half = STRIP * PLANES
+
+        unmerge(low, c0, (0, 1, 2, 3))
+        weave(on_scalar, low, zw[0][:])
+
+        unmerge(high, c1, (1, 2, 3))
+        multiply(zw[0][:], c0, CHUNK, PLANES)
+        unmerge(high, c1, (0,))
+        weave(on_scalar, high, zw[1][:])
+        store(c0, CHUNK, PLANES, joined=True)
+
+        unmerge(low, c2, (0, 1, 2))
+        multiply(zw[1][:], c1, CHUNK)
+        unmerge(low, c2, (3,))
+        ow0 = woven_tile(CHUNK, "zw1")
+        weave(on_scalar, res[c0][:, :, 0:STRIP], ow0[:, 0:half])
+        weave(on_scalar, low, zw[2][:])
+        store(c1, CHUNK)
+
+        unmerge(strip_a, c3, (1, 2, 3))
+        unmerge(strip_b, c3b, (3,))
+        weave(on_vector, res[c0][:, :, STRIP:CHUNK], ow0[:, half : 2 * half])
+        multiply(zw[2][:], c2, CHUNK)
+        unmerge(strip_a, c3, (0,))
+        weave(on_scalar, strip_a, zw_a[:])
+        unmerge(strip_b, c3b, (0, 1, 2))
+        multiply(zw_a[:], c3, STRIP)
+        weave(on_vector, strip_b, zw_b[:])
+        codes0 = code_tile(CHUNK, "mg0")
+        hand_on(codes0[:], ow0[:], c0)
+        store_words(codes0[:], c0)
+        store(c2, CHUNK)
+        multiply(zw_b[:], c3b, STRIP)
+
+        ow1 = woven_tile(CHUNK, "zw_a")
+        weave(on_scalar, res[c1][:, :, 0:STRIP], ow1[:, 0:half])
+        weave(on_vector, res[c1][:, :, STRIP:CHUNK], ow1[:, half : 2 * half])
+        store(c3, STRIP)
+        ow2 = woven_tile(CHUNK, "ow2")
+        weave(on_vector, res[c2][:], ow2[:])
+        codes12 = code_tile(2 * CHUNK, "codes12")
+        hand_on(codes12[:, 0:CHUNK], ow1[:], c1)
+        hand_on(codes12[:, CHUNK : 2 * CHUNK], ow2[:], c2)
+        store_words(codes12[:], c1)
+        store(c3b, STRIP, joined=True)
+        ow3 = woven_tile(CHUNK, "ow3")
+        weave(on_vector, res[c3][:], ow3[:, 0:half])
+        weave(on_vector, res[c3b][:], ow3[:, half : 2 * half])
+        codes3 = code_tile(CHUNK, "codes3")
+        hand_on(codes3[:], ow3[:], c3)
+        store_words(codes3[:], c3)
 
         for r in range(4):
-            (nc.scalar if r % 2 else nc.sync).dma_start(
-                out=out_2[0, r:16:4, :].bitcast(I32), in_=o_scales[r:P:32, :].bitcast(I32)
-            )
+            in_sbuf, in_hbm = scale_rows(o_scales, out_2, r)
+            (nc.scalar if r % 2 else nc.sync).dma_start(out=in_hbm, in_=in_sbuf)

@@ -138,80 +138,107 @@ def tile_picked_tome8_silu_po_kernel(
                 engine_copy(out=y[t][:, picked], in_=acc[:, 0:width])
                 j0 = j0 + width
 
-        w2_codes = keep.tile([P, N], U32, align_bytes=64)
-        on_vector(
-            out=w2_codes[:].rearrange("p (t m) -> p m t", t=PLANES),
-            in_=w2w_raw[:].bitcast(U32).rearrange("p (m t) -> p m t", t=PLANES),
+        y_all = keep.tile([P, PLANES, S], F32)
+        for t in range(PLANES):
+            nc.sync.dma_start(out=y_all[:, t, :], in_=y[t][:])
+
+        fetched = [keep.tile([P, PLANES, V], F32, name="fetched%d" % h) for h in range(2)]
+        home = [keep.tile([P, 2 * V], F32, name="home%d" % t) for t in range(PLANES)]
+
+        def fetch(on_act, t, j0, width):
+            target = fetched[j0 // V][:, t, j0 % V : j0 % V + width]
+            source = home[t][:].indirect(back_sb[:, j0 // 16 : (j0 + width) // 16])
+            if on_act:
+                nc.scalar.activation(target, source, ACT.Copy)
+            else:
+                nc.vector.tensor_copy(target, source)
+
+        def take_part(t, which, part):
+            offsets, weight = ((a1_sb, wa_sb), (a2_sb, wb_sb))[which]
+            nc.vector.tensor_tensor(part, y[t][:].indirect(offsets[:]), weight[:], ALU.mult)
+
+        turned0 = keep.tile([P, V], F32)
+        late = (fetched[1][:, 1, 0:CHUNK], fetched[1][:, 2, 0:CHUNK])
+        turned_halves = (
+            (turned0[:, 0:CHUNK], turned0[:, CHUNK:V]),
+            (fetched[1][:, 0, 0:CHUNK], fetched[1][:, 0, CHUNK:V]),
+            late,
         )
-        w2_sc = keep.tile([P, N], U8, align_bytes=64)
+        for t in range(LAST):
+            first = home[t][:, V : 2 * V]
+            take_part(t, 0, first)
+            summed = [psum_mix.tile([P, 2, P], F32, name="summed%d" % (2 * (t % 2) + h)) for h in range(2)]
+            for b in range(BLOCKS):
+                nc.tensor.matmul(
+                    summed[b // 2][:, b % 2, :],
+                    first[:, b * P : (b + 1) * P],
+                    ident[:],
+                    start=b % 2 == 0,
+                    stop=False,
+                    is_transpose=True,
+                )
+            second = keep.tile([P, V], F32, name="second%d" % t, align_bytes=64)
+            take_part(t, 1, second[:])
+            turned = [turned_halves[t][b // 2][:, b % 2 * P : (b % 2 + 1) * P] for b in range(BLOCKS)]
+            for b in range(BLOCKS):
+                nc.tensor.matmul(
+                    summed[b // 2][:, b % 2, :],
+                    second[:, b * P : (b + 1) * P],
+                    ident[:],
+                    start=False,
+                    stop=b % 2 == 1,
+                    is_transpose=True,
+                )
+                if b % 2 == 1:
+                    nc.scalar.activation(
+                        turned_halves[t][b // 2], summed[b // 2][:].rearrange("p i v -> p (i v)"), ACT.Silu
+                    )
+            if t == 0:
+                w2_codes = keep.tile([P, N], U32, tag="second0", align_bytes=64)
+                on_scalar(
+                    out=w2_codes[:].rearrange("p (t m) -> p m t", t=PLANES),
+                    in_=w2w_raw[:].bitcast(U32).rearrange("p (m t) -> p m t", t=PLANES),
+                )
+            else:
+                fetch(True, 0, (t - 1) * V, V // t)
+            for h in range(2):
+                back_turned = psum.tile([P, 2 * P], F32, name="acc%d" % (2 + h))
+                for i in range(2):
+                    nc.tensor.transpose(back_turned[:, i * P : (i + 1) * P], turned[2 * h + i], ident[:])
+                on_scalar(out=home[t][:, 2 * h * P : 2 * (h + 1) * P], in_=back_turned[:])
+
+        first, second = fetched[0][:, 1, :], home[LAST][:, V : 2 * V]
+        take_part(LAST, 0, first)
+        take_part(LAST, 1, second)
+        w2_sc = keep.tile([P, N], U8, tag="second2", align_bytes=64)
         on_vector(
             out=w2_sc[:].rearrange("p (t m) -> p t m", t=PLANES),
             in_=w2s_raw[:].rearrange("p (m t) -> p t m", t=PLANES),
         )
-
-        mg = [keep.tile([P, V], F32, name="mg%d" % t, align_bytes=64) for t in range(PLANES)]
-        parts = keep.tile([P, 4 * V - P], F32)
-
-        def take_part(t, which):
-            part = parts[:, PART_AT[t][which] : PART_AT[t][which] + V]
-            offsets, weight = ((a1_sb, wa_sb), (a2_sb, wb_sb))[which]
-            nc.vector.tensor_tensor(part, y[t][:].indirect(offsets[:]), weight[:], ALU.mult)
-            return part
+        for h in range(2):
+            cols = slice((1 - h) * CHUNK, (2 - h) * CHUNK)
+            nc.vector.tensor_tensor(late[h], first[:, cols], second[:, cols], ALU.add)
+            nc.scalar.activation(home[LAST][:, cols], late[h], ACT.Silu)
 
         z_codes = keep.tile([P, S], U32, align_bytes=64)
         z_scales = keep.tile([P, S], U8, align_bytes=64)
         o_scales = keep.tile([P, S], U8, align_bytes=64)
-        z_stage = keep.tile([P, 8 * CHUNK], F32)
-
-        def slot(s, width=CHUNK):
-            return z_stage[:, s * CHUNK : s * CHUNK + width]
-
-        turned_homes = {(1, 3): slot(0, P), (2, 2): slot(4, P), (2, 3): slot(1, P)}
-        for t in range(LAST):
-            first = take_part(t, 0)
-            summed = [psum_mix.tile([P, P], F32, name="summed%d" % b) for b in range(BLOCKS)]
-            for b in range(BLOCKS):
-                nc.tensor.matmul(
-                    summed[b][:], first[:, b * P : (b + 1) * P], ident[:], start=True, stop=False, is_transpose=True
-                )
-            second = take_part(t, 1)
-            mixed = keep.tile([P, V], F32, name="mixed", tag="mixed%d" % (t % 2))
-            silu_t = [turned_homes.get((t, b), mixed[:, b * P : (b + 1) * P]) for b in range(BLOCKS)]
-            for b in range(BLOCKS):
-                nc.tensor.matmul(
-                    summed[b][:], second[:, b * P : (b + 1) * P], ident[:], start=False, stop=True, is_transpose=True
-                )
-                nc.scalar.activation(silu_t[b], summed[b][:], ACT.Silu)
-            for h in range(2):
-                back_turned = psum.tile([P, 2 * P], F32, name="acc%d" % (2 + h))
-                for i in range(2):
-                    nc.tensor.transpose(back_turned[:, i * P : (i + 1) * P], silu_t[2 * h + i], ident[:])
-                on_scalar(out=mg[t][:, 2 * h * P : 2 * (h + 1) * P], in_=back_turned[:])
-
-        first = take_part(LAST, 0)
-        second = take_part(LAST, 1)
-        total = slot(4, V)
-        nc.vector.tensor_tensor(total, first, second, ALU.add)
-        nc.scalar.activation(mg[LAST][:], total, ACT.Silu)
-
         out_rows = out_0.rearrange("(p t) j -> p t j", t=PLANES)
         out_words = out_1[0].rearrange("p c r -> p (c r)").bitcast(I32)
         res = {}
         banks = {}
+        o_codes = keep.tile([P, S], I32, align_bytes=64)
 
-        def staged(col0, width):
-            rows = z_stage[:, col0 : col0 + PLANES * CHUNK].rearrange("p (t j) -> p t j", t=PLANES)
-            return rows[:, :, 0:width]
+        def woven_tile(width, tag):
+            return keep.tile([P, width * PLANES], BF16, name="woven", tag=tag, align_bytes=64)
 
-        def unmerge(home, j0, planes):
-            width = home.shape[2]
-            for t in planes:
-                nc.vector.tensor_tensor(
-                    home[:, t, :],
-                    mg[t][:].indirect(back_sb[:, j0 // 16 : (j0 + width) // 16]),
-                    y[t][:, j0 : j0 + width],
-                    ALU.add,
-                )
+        def add_weave(zw, j0, width):
+            nc.vector.tensor_tensor(
+                zw.rearrange("p (c i t) -> p c t i", i=2, t=PLANES),
+                fetched[j0 // V][:, :, j0 % V : j0 % V + width].rearrange("p t (c i) -> p c t i", i=2),
+                y_all[:, :, j0 : j0 + width].rearrange("p t (c i) -> p c t i", i=2),
+                ALU.add,
+            )
 
         def weave(engine_copy, source, target):
             engine_copy(
@@ -219,107 +246,93 @@ def tile_picked_tome8_silu_po_kernel(
                 in_=source.rearrange("p t (c i) -> p c t i", i=4),
             )
 
-        def woven_tile(width, tag):
-            return keep.tile([P, width * PLANES], BF16, name="woven", tag=tag, align_bytes=64)
-
-        def multiply(z_woven, j0, width, per_bank=2):
+        def multiply(z_woven, j0, width):
             cols = slice(j0, j0 + width)
             nc.vector.quantize_mx(out=z_codes[:, cols].bitcast(FP8X4), scales=z_scales[:, cols], in_=z_woven)
-            span = min(width, BANK // per_bank)
-            for s0 in range(j0, j0 + width, span):
-                for t0 in range(0, PLANES, per_bank):
-                    acc = psum.tile([P, per_bank, span], F32, name="acc%d" % (len(banks) % 4))
-                    banks[s0, t0] = acc
-                    for i in range(per_bank):
-                        rows = slice((t0 + i) * P, (t0 + i + 1) * P)
-                        nc.tensor.matmul_mx(
-                            out=acc[:, i, :],
-                            lhsT=w2_codes[:, rows].bitcast(FP8X4),
-                            lhsT_scale=w2_sc[:, rows],
-                            rhs=z_codes[:, s0 : s0 + span].bitcast(FP8X4),
-                            rhs_scale=z_scales[:, s0 : s0 + span],
-                            start=True,
-                            stop=True,
-                        )
+            per_bank = BANK // width
+            for t0 in range(0, PLANES, per_bank):
+                acc = psum.tile([P, per_bank, width], F32, name="acc%d" % (len(banks) % 4))
+                banks[j0, t0] = acc
+                for i in range(per_bank):
+                    rows = slice((t0 + i) * P, (t0 + i + 1) * P)
+                    nc.tensor.matmul_mx(
+                        out=acc[:, i, :],
+                        lhsT=w2_codes[:, rows].bitcast(FP8X4),
+                        lhsT_scale=w2_sc[:, rows],
+                        rhs=z_codes[:, cols].bitcast(FP8X4),
+                        rhs_scale=z_scales[:, cols],
+                        start=True,
+                        stop=True,
+                    )
 
-        def store(j0, width, per_bank=2, joined=False):
-            res[j0] = keep.tile([P, PLANES, width], F32, name="res%d" % j0)
-            span = min(width, BANK // per_bank)
-            for s0 in range(0, width, span):
-                for t0 in range(0, PLANES, per_bank):
-                    held = res[j0][:, t0 : t0 + per_bank, s0 : s0 + span]
-                    on_scalar(out=held, in_=banks[j0 + s0, t0][:])
-                    if not joined:
-                        nc.sync.dma_start(out=out_rows[:, t0 : t0 + per_bank, j0 + s0 : j0 + s0 + span], in_=held)
-            if joined:
-                nc.sync.dma_start(out=out_rows[:, :, j0 : j0 + width], in_=res[j0][:])
+        def store(j0, width, place=None):
+            if place is None:
+                place = keep.tile([P, PLANES * width], F32, name="res%d" % j0)[:]
+            res[j0] = place.rearrange("p (t j) -> p t j", t=PLANES)
+            per_bank = BANK // width
+            for t0 in range(0, PLANES, per_bank):
+                held = res[j0][:, t0 : t0 + per_bank, :]
+                on_scalar(out=held, in_=banks[j0, t0][:])
+                nc.sync.dma_start(out=out_rows[:, t0 : t0 + per_bank, j0 : j0 + width], in_=held)
 
-        def code_tile(width, tag):
-            return keep.tile([P, width], I32, name="o_codes", tag=tag, align_bytes=64)
+        def round_result(engine_copy, j0, width):
+            weave(engine_copy, res[j0], ow[:, j0 * PLANES : (j0 + width) * PLANES])
 
-        def hand_on(codes, woven, j0):
-            nc.vector.quantize_mx(out=codes.bitcast(FP8X4), scales=o_scales[:, j0 : j0 + CHUNK], in_=woven)
+        def hand_on(j0, width):
+            nc.vector.quantize_mx(
+                out=o_codes[:, j0 : j0 + width].bitcast(FP8X4),
+                scales=o_scales[:, j0 : j0 + width],
+                in_=ow[:, j0 * PLANES : (j0 + width) * PLANES],
+            )
 
-        def store_words(codes, j0):
-            nc.sync.dma_start(out=out_words[:, j0 : j0 + codes.shape[1]], in_=codes)
+        def store_words(j0, width):
+            nc.sync.dma_start(out=out_words[:, j0 : j0 + width], in_=o_codes[:, j0 : j0 + width])
 
         c0, c1, c2, c3 = (c * CHUNK for c in range(S // CHUNK))
-        c3b = c3 + STRIP
-        low, high = staged(0, CHUNK), staged(3 * CHUNK, CHUNK)
-        strip_a, strip_b = staged(3 * CHUNK, STRIP), staged(CHUNK + STRIP, STRIP)
-        zw = [woven_tile(CHUNK, "zw%d" % c) for c in range(3)]
-        zw_a, zw_b = woven_tile(STRIP, "zw_a"), woven_tile(STRIP, "zw_b")
-        half = STRIP * PLANES
+        c1b, c3b = c1 + STRIP, c3 + STRIP
+        zw = woven_tile(S, "zw")
+        ow = woven_tile(S, "ow")
 
-        unmerge(low, c0, (0, 1, 2, 3))
-        weave(on_scalar, low, zw[0][:])
+        def z_cols(j0, width):
+            return zw[:, j0 * PLANES : (j0 + width) * PLANES]
 
-        unmerge(high, c1, (1, 2, 3))
-        multiply(zw[0][:], c0, CHUNK, PLANES)
-        unmerge(high, c1, (0,))
-        weave(on_scalar, high, zw[1][:])
-        store(c0, CHUNK, PLANES, joined=True)
-
-        unmerge(low, c2, (0, 1, 2))
-        multiply(zw[1][:], c1, CHUNK)
-        unmerge(low, c2, (3,))
-        ow0 = woven_tile(CHUNK, "zw1")
-        weave(on_scalar, res[c0][:, :, 0:STRIP], ow0[:, 0:half])
-        weave(on_scalar, low, zw[2][:])
+        for t in (1, 2, 3):
+            fetch(False, t, c0, CHUNK)
+        for t in (1, 2, 3):
+            fetch(True, t, c1, CHUNK)
+        add_weave(z_cols(c0, CHUNK), c0, CHUNK)
+        add_weave(z_cols(c1, STRIP), c1, STRIP)
+        multiply(z_cols(c0, CHUNK), c0, CHUNK)
+        fetch(True, 1, c2, V)
+        fetch(True, 2, c2, CHUNK)
+        fetch(True, 3, c2, CHUNK)
+        fetch(True, 0, c3, CHUNK)
+        add_weave(z_cols(c1b, STRIP), c1b, STRIP)
+        multiply(z_cols(c1, CHUNK), c1, CHUNK)
+        store(c0, CHUNK)
+        fetch(True, 2, c3, CHUNK)
+        fetch(True, 3, c3, CHUNK)
+        add_weave(z_cols(c2, CHUNK), c2, CHUNK)
+        multiply(z_cols(c2, CHUNK), c2, CHUNK)
+        round_result(on_vector, c0, CHUNK)
         store(c1, CHUNK)
-
-        unmerge(strip_a, c3, (1, 2, 3))
-        unmerge(strip_b, c3b, (3,))
-        weave(on_vector, res[c0][:, :, STRIP:CHUNK], ow0[:, half : 2 * half])
-        multiply(zw[2][:], c2, CHUNK)
-        unmerge(strip_a, c3, (0,))
-        weave(on_scalar, strip_a, zw_a[:])
-        unmerge(strip_b, c3b, (0, 1, 2))
-        multiply(zw_a[:], c3, STRIP)
-        weave(on_vector, strip_b, zw_b[:])
-        codes0 = code_tile(CHUNK, "mg0")
-        hand_on(codes0[:], ow0[:], c0)
-        store_words(codes0[:], c0)
+        hand_on(c0, CHUNK)
+        add_weave(z_cols(c3, STRIP), c3, STRIP)
+        add_weave(z_cols(c3b, STRIP), c3b, STRIP)
+        multiply(z_cols(c3, STRIP), c3, STRIP)
+        multiply(z_cols(c3b, STRIP), c3b, STRIP)
         store(c2, CHUNK)
-        multiply(zw_b[:], c3b, STRIP)
-
-        ow1 = woven_tile(CHUNK, "zw_a")
-        weave(on_scalar, res[c1][:, :, 0:STRIP], ow1[:, 0:half])
-        weave(on_vector, res[c1][:, :, STRIP:CHUNK], ow1[:, half : 2 * half])
+        round_result(on_vector, c1, CHUNK)
         store(c3, STRIP)
-        ow2 = woven_tile(CHUNK, "ow2")
-        weave(on_vector, res[c2][:], ow2[:])
-        codes12 = code_tile(2 * CHUNK, "codes12")
-        hand_on(codes12[:, 0:CHUNK], ow1[:], c1)
-        hand_on(codes12[:, CHUNK : 2 * CHUNK], ow2[:], c2)
-        store_words(codes12[:], c1)
-        store(c3b, STRIP, joined=True)
-        ow3 = woven_tile(CHUNK, "ow3")
-        weave(on_vector, res[c3][:], ow3[:, 0:half])
-        weave(on_vector, res[c3b][:], ow3[:, half : 2 * half])
-        codes3 = code_tile(CHUNK, "codes3")
-        hand_on(codes3[:], ow3[:], c3)
-        store_words(codes3[:], c3)
+        store(c3b, STRIP)
+        round_result(on_vector, c2, CHUNK)
+        hand_on(c1, CHUNK)
+        store_words(c0, V)
+        hand_on(c2, CHUNK)
+        round_result(on_vector, c3, STRIP)
+        round_result(on_vector, c3b, STRIP)
+        hand_on(c3, CHUNK)
+        store_words(c2, V)
 
         for r in range(4):
             in_sbuf, in_hbm = scale_rows(o_scales, out_2, r)

@@ -138,87 +138,76 @@ def tile_picked_tome8_silu_po_kernel(
                 engine_copy(out=y[t][:, picked], in_=acc[:, 0:width])
                 j0 = j0 + width
 
-        y_all = keep.tile([P, PLANES, S], F32)
-        for t in range(PLANES):
-            nc.sync.dma_start(out=y_all[:, t, :], in_=y[t][:])
+        w2_codes = keep.tile([P, N], U32, align_bytes=64)
+        on_vector(
+            out=w2_codes[:].rearrange("p (t m) -> p m t", t=PLANES),
+            in_=w2w_raw[:].bitcast(U32).rearrange("p (m t) -> p m t", t=PLANES),
+        )
+        w2_sc = keep.tile([P, N], U8, align_bytes=64)
+        on_vector(
+            out=w2_sc[:].rearrange("p (t m) -> p t m", t=PLANES),
+            in_=w2s_raw[:].rearrange("p (m t) -> p t m", t=PLANES),
+        )
 
-        fetched = [keep.tile([P, PLANES, V], F32, name="fetched%d" % h) for h in range(2)]
+        y_late = keep.tile([P, PLANES, S - CHUNK], F32)
+        for t in range(PLANES):
+            nc.sync.dma_start(out=y_late[:, t, :], in_=y[t][:, CHUNK:S])
+
+        fetched = keep.tile([P, PLANES * (S - CHUNK)], F32)
+        fetched_rows = fetched[:].rearrange("p (t j) -> p t j", t=PLANES)
+        z_first = keep.tile([P, PLANES, CHUNK], F32)
         home = [keep.tile([P, 2 * V], F32, name="home%d" % t) for t in range(PLANES)]
 
-        def fetch(on_act, t, j0, width):
-            target = fetched[j0 // V][:, t, j0 % V : j0 % V + width]
-            source = home[t][:].indirect(back_sb[:, j0 // 16 : (j0 + width) // 16])
-            if on_act:
-                nc.scalar.activation(target, source, ACT.Copy)
-            else:
-                nc.vector.tensor_copy(target, source)
+        def looked_up(t, j0, width):
+            return home[t][:].indirect(back_sb[:, j0 // 16 : (j0 + width) // 16])
+
+        def place(t, j0, width):
+            return fetched_rows[:, t, j0 - CHUNK : j0 - CHUNK + width]
+
+        def fetch(t, j0, width):
+            nc.scalar.activation(place(t, j0, width), looked_up(t, j0, width), ACT.Copy)
 
         def take_part(t, which, part):
             offsets, weight = ((a1_sb, wa_sb), (a2_sb, wb_sb))[which]
             nc.vector.tensor_tensor(part, y[t][:].indirect(offsets[:]), weight[:], ALU.mult)
 
-        turned0 = keep.tile([P, V], F32)
-        late = (fetched[1][:, 1, 0:CHUNK], fetched[1][:, 2, 0:CHUNK])
-        turned_halves = (
-            (turned0[:, 0:CHUNK], turned0[:, CHUNK:V]),
-            (fetched[1][:, 0, 0:CHUNK], fetched[1][:, 0, CHUNK:V]),
-            late,
-        )
+        second0 = keep.tile([P, V], F32)
+        seconds = (second0[:], place(0, CHUNK, V), place(1, CHUNK, V))
+        turned01 = keep.tile([P, V], F32)
         for t in range(LAST):
             first = home[t][:, V : 2 * V]
             take_part(t, 0, first)
-            summed = [psum_mix.tile([P, 2, P], F32, name="summed%d" % (2 * (t % 2) + h)) for h in range(2)]
+            summed = [psum_mix.tile([P, P], F32, name="summed%d" % b) for b in range(BLOCKS)]
             for b in range(BLOCKS):
                 nc.tensor.matmul(
-                    summed[b // 2][:, b % 2, :],
-                    first[:, b * P : (b + 1) * P],
-                    ident[:],
-                    start=b % 2 == 0,
-                    stop=False,
-                    is_transpose=True,
+                    summed[b][:], first[:, b * P : (b + 1) * P], ident[:], start=True, stop=False, is_transpose=True
                 )
-            second = keep.tile([P, V], F32, name="second%d" % t, align_bytes=64)
-            take_part(t, 1, second[:])
-            turned = [turned_halves[t][b // 2][:, b % 2 * P : (b % 2 + 1) * P] for b in range(BLOCKS)]
+            second = seconds[t]
+            take_part(t, 1, second)
+            turned = turned01[:] if t < 2 else home[LAST][:, 0:V]
             for b in range(BLOCKS):
                 nc.tensor.matmul(
-                    summed[b // 2][:, b % 2, :],
-                    second[:, b * P : (b + 1) * P],
-                    ident[:],
-                    start=False,
-                    stop=b % 2 == 1,
-                    is_transpose=True,
+                    summed[b][:], second[:, b * P : (b + 1) * P], ident[:], start=False, stop=True, is_transpose=True
                 )
-                if b % 2 == 1:
-                    nc.scalar.activation(
-                        turned_halves[t][b // 2], summed[b // 2][:].rearrange("p i v -> p (i v)"), ACT.Silu
-                    )
-            if t == 0:
-                w2_codes = keep.tile([P, N], U32, tag="second0", align_bytes=64)
-                on_scalar(
-                    out=w2_codes[:].rearrange("p (t m) -> p m t", t=PLANES),
-                    in_=w2w_raw[:].bitcast(U32).rearrange("p (m t) -> p m t", t=PLANES),
-                )
-            else:
-                fetch(True, 0, (t - 1) * V, V // t)
+                nc.scalar.activation(turned[:, b * P : (b + 1) * P], summed[b][:], ACT.Silu)
+            if t > 0:
+                fetch(t - 1, CHUNK, V)
             for h in range(2):
                 back_turned = psum.tile([P, 2 * P], F32, name="acc%d" % (2 + h))
                 for i in range(2):
-                    nc.tensor.transpose(back_turned[:, i * P : (i + 1) * P], turned[2 * h + i], ident[:])
+                    b = 2 * h + i
+                    nc.tensor.transpose(back_turned[:, i * P : (i + 1) * P], turned[:, b * P : (b + 1) * P], ident[:])
                 on_scalar(out=home[t][:, 2 * h * P : 2 * (h + 1) * P], in_=back_turned[:])
 
-        first, second = fetched[0][:, 1, :], home[LAST][:, V : 2 * V]
+        first3 = keep.tile([P, V], F32)
+        first, second = first3[:], home[LAST][:, V : 2 * V]
         take_part(LAST, 0, first)
         take_part(LAST, 1, second)
-        w2_sc = keep.tile([P, N], U8, tag="second2", align_bytes=64)
-        on_vector(
-            out=w2_sc[:].rearrange("p (t m) -> p t m", t=PLANES),
-            in_=w2s_raw[:].rearrange("p (m t) -> p t m", t=PLANES),
-        )
         for h in range(2):
-            cols = slice((1 - h) * CHUNK, (2 - h) * CHUNK)
-            nc.vector.tensor_tensor(late[h], first[:, cols], second[:, cols], ALU.add)
-            nc.scalar.activation(home[LAST][:, cols], late[h], ACT.Silu)
+            cols = slice(h * CHUNK, (h + 1) * CHUNK)
+            total = place(h, S - CHUNK, CHUNK)
+            nc.vector.tensor_tensor(total, first[:, cols], second[:, cols], ALU.add)
+            nc.scalar.activation(home[LAST][:, cols], total, ACT.Silu)
 
         z_codes = keep.tile([P, S], U32, align_bytes=64)
         z_scales = keep.tile([P, S], U8, align_bytes=64)
@@ -235,8 +224,8 @@ def tile_picked_tome8_silu_po_kernel(
         def add_weave(zw, j0, width):
             nc.vector.tensor_tensor(
                 zw.rearrange("p (c i t) -> p c t i", i=2, t=PLANES),
-                fetched[j0 // V][:, :, j0 % V : j0 % V + width].rearrange("p t (c i) -> p c t i", i=2),
-                y_all[:, :, j0 : j0 + width].rearrange("p t (c i) -> p c t i", i=2),
+                fetched_rows[:, :, j0 - CHUNK : j0 - CHUNK + width].rearrange("p t (c i) -> p c t i", i=2),
+                y_late[:, :, j0 - CHUNK : j0 - CHUNK + width].rearrange("p t (c i) -> p c t i", i=2),
                 ALU.add,
             )
 
@@ -289,39 +278,37 @@ def tile_picked_tome8_silu_po_kernel(
             nc.sync.dma_start(out=out_words[:, j0 : j0 + width], in_=o_codes[:, j0 : j0 + width])
 
         c0, c1, c2, c3 = (c * CHUNK for c in range(S // CHUNK))
-        c1b, c3b = c1 + STRIP, c3 + STRIP
+        c1b, c2b, c3b = c1 + STRIP, c2 + STRIP, c3 + STRIP
         zw = woven_tile(S, "zw")
         ow = woven_tile(S, "ow")
 
         def z_cols(j0, width):
             return zw[:, j0 * PLANES : (j0 + width) * PLANES]
 
-        for t in (1, 2, 3):
-            fetch(False, t, c0, CHUNK)
-        for t in (1, 2, 3):
-            fetch(True, t, c1, CHUNK)
-        add_weave(z_cols(c0, CHUNK), c0, CHUNK)
+        for t in range(PLANES):
+            nc.vector.tensor_tensor(z_first[:, t, :], looked_up(t, c0, CHUNK), y[t][:, c0 : c0 + CHUNK], ALU.add)
+        for j0 in (c1, c2):
+            fetch(2, j0, CHUNK)
+            fetch(3, j0, CHUNK)
+        for t in range(PLANES):
+            fetch(t, c3, CHUNK)
+        weave(on_vector, z_first[:], z_cols(c0, CHUNK))
         add_weave(z_cols(c1, STRIP), c1, STRIP)
         multiply(z_cols(c0, CHUNK), c0, CHUNK)
-        fetch(True, 1, c2, V)
-        fetch(True, 2, c2, CHUNK)
-        fetch(True, 3, c2, CHUNK)
-        fetch(True, 0, c3, CHUNK)
         add_weave(z_cols(c1b, STRIP), c1b, STRIP)
+        add_weave(z_cols(c2, STRIP), c2, STRIP)
         multiply(z_cols(c1, CHUNK), c1, CHUNK)
         store(c0, CHUNK)
-        fetch(True, 2, c3, CHUNK)
-        fetch(True, 3, c3, CHUNK)
-        add_weave(z_cols(c2, CHUNK), c2, CHUNK)
-        multiply(z_cols(c2, CHUNK), c2, CHUNK)
-        round_result(on_vector, c0, CHUNK)
-        store(c1, CHUNK)
-        hand_on(c0, CHUNK)
+        add_weave(z_cols(c2b, STRIP), c2b, STRIP)
         add_weave(z_cols(c3, STRIP), c3, STRIP)
+        multiply(z_cols(c2, CHUNK), c2, CHUNK)
+        store(c1, CHUNK)
         add_weave(z_cols(c3b, STRIP), c3b, STRIP)
         multiply(z_cols(c3, STRIP), c3, STRIP)
+        round_result(on_vector, c0, CHUNK)
         multiply(z_cols(c3b, STRIP), c3b, STRIP)
         store(c2, CHUNK)
+        hand_on(c0, CHUNK)
         round_result(on_vector, c1, CHUNK)
         store(c3, STRIP)
         store(c3b, STRIP)
@@ -329,10 +316,11 @@ def tile_picked_tome8_silu_po_kernel(
         hand_on(c1, CHUNK)
         store_words(c0, V)
         hand_on(c2, CHUNK)
+        store_words(c2, CHUNK)
         round_result(on_vector, c3, STRIP)
         round_result(on_vector, c3b, STRIP)
         hand_on(c3, CHUNK)
-        store_words(c2, V)
+        store_words(c3, CHUNK)
 
         for r in range(4):
             in_sbuf, in_hbm = scale_rows(o_scales, out_2, r)

@@ -167,6 +167,9 @@ def tile_picked_tome8_silu_po_kernel(
         def fetch(t, j0, width):
             nc.scalar.activation(place(t, j0, width), looked_up(t, j0, width), ACT.Copy)
 
+        def fetch_on_vector(t, j0, width):
+            nc.vector.tensor_copy(place(t, j0, width), looked_up(t, j0, width))
+
         def take_part(t, which, part):
             offsets, weight = ((a1_sb, wa_sb), (a2_sb, wb_sb))[which]
             nc.vector.tensor_tensor(part, y[t][:].indirect(offsets[:]), weight[:], ALU.mult)
@@ -290,11 +293,13 @@ def tile_picked_tome8_silu_po_kernel(
         for j0 in (c1, c2):
             fetch(2, j0, CHUNK)
             fetch(3, j0, CHUNK)
-        for t in range(PLANES):
-            fetch(t, c3, CHUNK)
+        fetch(2, c3, CHUNK)
+        fetch(3, c3, CHUNK)
+        fetch_on_vector(0, c3, CHUNK)
         weave(on_vector, z_first[:], z_cols(c0, CHUNK))
-        add_weave(z_cols(c1, STRIP), c1, STRIP)
+        fetch_on_vector(1, c3, CHUNK)
         multiply(z_cols(c0, CHUNK), c0, CHUNK)
+        add_weave(z_cols(c1, STRIP), c1, STRIP)
         add_weave(z_cols(c1b, STRIP), c1b, STRIP)
         add_weave(z_cols(c2, STRIP), c2, STRIP)
         multiply(z_cols(c1, CHUNK), c1, CHUNK)

@@ -226,9 +226,9 @@ def tile_picked_tome8_silu_po_kernel(
 
         def add_weave(zw, j0, width):
             nc.vector.tensor_tensor(
-                zw.rearrange("p (c i t) -> p c t i", i=2, t=PLANES),
-                fetched_rows[:, :, j0 - CHUNK : j0 - CHUNK + width].rearrange("p t (c i) -> p c t i", i=2),
-                y_late[:, :, j0 - CHUNK : j0 - CHUNK + width].rearrange("p t (c i) -> p c t i", i=2),
+                zw.rearrange("p (c i t) -> p c t i", i=4, t=PLANES),
+                fetched_rows[:, :, j0 - CHUNK : j0 - CHUNK + width].rearrange("p t (c i) -> p c t i", i=4),
+                y_late[:, :, j0 - CHUNK : j0 - CHUNK + width].rearrange("p t (c i) -> p c t i", i=4),
                 ALU.add,
             )
 

@@ -24,11 +24,11 @@ BLOCKS = V // P
 CHUNK = 256
 STRIP = CHUNK // 2
 LAST = PLANES - 1
+FIRST = CHUNK
 
 EARLY_WORDS = T // 4
 PLANE0_PASSES = (512, 256, 128, 128)
 W1_SCALAR_COLS = (96, 80)
-PART_AT = ((V - P, 2 * V), (0, V), (3 * V - P, 0), (V, 2 * V))
 
 
 def tile_picked_tome8_silu_po_kernel(
@@ -149,88 +149,84 @@ def tile_picked_tome8_silu_po_kernel(
             in_=w2s_raw[:].rearrange("p (m t) -> p t m", t=PLANES),
         )
 
-        y_late = keep.tile([P, PLANES, S - CHUNK], F32)
+        y_late = keep.tile([P, PLANES, S - FIRST], F32)
         for t in range(PLANES):
-            nc.sync.dma_start(out=y_late[:, t, :], in_=y[t][:, CHUNK:S])
+            nc.sync.dma_start(out=y_late[:, t, :], in_=y[t][:, FIRST:S])
 
-        fetched = keep.tile([P, PLANES * (S - CHUNK)], F32)
-        fetched_rows = fetched[:].rearrange("p (t j) -> p t j", t=PLANES)
-        z_first = keep.tile([P, PLANES, CHUNK], F32)
-        home = [keep.tile([P, 2 * V], F32, name="home%d" % t) for t in range(PLANES)]
+        mg = [keep.tile([P, V], F32, name="mg%d" % t) for t in range(PLANES)]
 
-        def looked_up(t, j0, width):
-            return home[t][:].indirect(back_sb[:, j0 // 16 : (j0 + width) // 16])
-
-        def place(t, j0, width):
-            return fetched_rows[:, t, j0 - CHUNK : j0 - CHUNK + width]
-
-        def fetch(t, j0, width):
-            nc.scalar.activation(place(t, j0, width), looked_up(t, j0, width), ACT.Copy)
-
-        def fetch_on_vector(t, j0, width):
-            nc.vector.tensor_copy(place(t, j0, width), looked_up(t, j0, width))
-
-        def take_part(t, which, part):
+        def take_part(t, which):
+            part = keep.tile([P, V], F32, name="part%d%d" % (t, which))
             offsets, weight = ((a1_sb, wa_sb), (a2_sb, wb_sb))[which]
-            nc.vector.tensor_tensor(part, y[t][:].indirect(offsets[:]), weight[:], ALU.mult)
+            nc.vector.tensor_tensor(part[:], y[t][:].indirect(offsets[:]), weight[:], ALU.mult)
+            return part
 
-        second0 = keep.tile([P, V], F32)
-        seconds = (second0[:], place(0, CHUNK, V), place(1, CHUNK, V))
         turned01 = keep.tile([P, V], F32)
+        turned2 = keep.tile([P, V], F32, tag="slot0")
         for t in range(LAST):
-            first = home[t][:, V : 2 * V]
-            take_part(t, 0, first)
+            first = take_part(t, 0)
             summed = [psum_mix.tile([P, P], F32, name="summed%d" % b) for b in range(BLOCKS)]
             for b in range(BLOCKS):
                 nc.tensor.matmul(
                     summed[b][:], first[:, b * P : (b + 1) * P], ident[:], start=True, stop=False, is_transpose=True
                 )
-            second = seconds[t]
-            take_part(t, 1, second)
-            turned = turned01[:] if t < 2 else home[LAST][:, 0:V]
+            second = take_part(t, 1)
+            turned = [(turned01 if t < 2 else turned2)[:, b * P : (b + 1) * P] for b in range(BLOCKS)]
+            if t == 2:
+                turned[LAST] = mg[LAST][:, (V - P) // 2 : (V + P) // 2]
             for b in range(BLOCKS):
                 nc.tensor.matmul(
                     summed[b][:], second[:, b * P : (b + 1) * P], ident[:], start=False, stop=True, is_transpose=True
                 )
-                nc.scalar.activation(turned[:, b * P : (b + 1) * P], summed[b][:], ACT.Silu)
-            if t > 0:
-                fetch(t - 1, CHUNK, V)
+                nc.scalar.activation(turned[b], summed[b][:], ACT.Silu)
             for h in range(2):
                 back_turned = psum.tile([P, 2 * P], F32, name="acc%d" % (2 + h))
                 for i in range(2):
-                    b = 2 * h + i
-                    nc.tensor.transpose(back_turned[:, i * P : (i + 1) * P], turned[:, b * P : (b + 1) * P], ident[:])
-                on_scalar(out=home[t][:, 2 * h * P : 2 * (h + 1) * P], in_=back_turned[:])
+                    nc.tensor.transpose(back_turned[:, i * P : (i + 1) * P], turned[2 * h + i], ident[:])
+                on_scalar(out=mg[t][:, 2 * h * P : 2 * (h + 1) * P], in_=back_turned[:])
 
-        first3 = keep.tile([P, V], F32)
-        first, second = first3[:], home[LAST][:, V : 2 * V]
-        take_part(LAST, 0, first)
-        take_part(LAST, 1, second)
-        for h in range(2):
-            cols = slice(h * CHUNK, (h + 1) * CHUNK)
-            total = place(h, S - CHUNK, CHUNK)
-            nc.vector.tensor_tensor(total, first[:, cols], second[:, cols], ALU.add)
-            nc.scalar.activation(home[LAST][:, cols], total, ACT.Silu)
+        first = take_part(LAST, 0)
+        second = keep.tile([P, V], F32)
+        total = keep.tile([P, V], F32, tag="slot1")
+        halves = (slice(0, V // 2), slice(V // 2, V))
+        for h, cols in enumerate(halves):
+            offsets = a2_sb[:, h * V // 32 : (h + 1) * V // 32]
+            nc.vector.tensor_tensor(second[:, cols], y[LAST][:].indirect(offsets), wb_sb[:, cols], ALU.mult)
+        for cols in halves:
+            nc.vector.tensor_tensor(total[:, cols], first[:, cols], second[:, cols], ALU.add)
 
         z_codes = keep.tile([P, S], U32, align_bytes=64)
         z_scales = keep.tile([P, S], U8, align_bytes=64)
         o_scales = keep.tile([P, S], U8, align_bytes=64)
+        o_codes = keep.tile([P, S], I32, align_bytes=64)
+        ow = keep.tile([P, S * PLANES], BF16, align_bytes=64)
+        res = keep.tile([P, PLANES * S], F32)
         out_rows = out_0.rearrange("(p t) j -> p t j", t=PLANES)
         out_words = out_1[0].rearrange("p c r -> p (c r)").bitcast(I32)
-        res = {}
         banks = {}
-        o_codes = keep.tile([P, S], I32, align_bytes=64)
+        free_banks = [(psum, "acc0"), (psum, "acc1")] + [(psum_mix, "summed%d" % b) for b in range(4)]
+        free_banks = free_banks + [(psum, "acc2"), (psum, "acc3")]
+
+        def looked_up(t, j0, width):
+            return mg[t][:].indirect(back_sb[:, j0 // 16 : (j0 + width) // 16])
+
+        def fetch(home, j0, planes):
+            for t in planes:
+                nc.scalar.activation(home[:, t, :], looked_up(t, j0, home.shape[2]), ACT.Copy)
 
         def woven_tile(width, tag):
             return keep.tile([P, width * PLANES], BF16, name="woven", tag=tag, align_bytes=64)
 
-        def add_weave(zw, j0, width):
+        def add_weave(home, j0, tag):
+            width = home.shape[2]
+            zw = woven_tile(width, tag)
             nc.vector.tensor_tensor(
-                zw.rearrange("p (c i t) -> p c t i", i=4, t=PLANES),
-                fetched_rows[:, :, j0 - CHUNK : j0 - CHUNK + width].rearrange("p t (c i) -> p c t i", i=4),
-                y_late[:, :, j0 - CHUNK : j0 - CHUNK + width].rearrange("p t (c i) -> p c t i", i=4),
+                zw[:].rearrange("p (c i t) -> p c t i", i=4, t=PLANES),
+                home.rearrange("p t (c i) -> p c t i", i=4),
+                y_late[:, :, j0 - FIRST : j0 - FIRST + width].rearrange("p t (c i) -> p c t i", i=4),
                 ALU.add,
             )
+            return zw
 
         def weave(engine_copy, source, target):
             engine_copy(
@@ -238,37 +234,41 @@ def tile_picked_tome8_silu_po_kernel(
                 in_=source.rearrange("p t (c i) -> p c t i", i=4),
             )
 
-        def multiply(z_woven, j0, width):
+        def multiply(z_woven, j0, width, span):
             cols = slice(j0, j0 + width)
-            nc.vector.quantize_mx(out=z_codes[:, cols].bitcast(FP8X4), scales=z_scales[:, cols], in_=z_woven)
-            per_bank = BANK // width
-            for t0 in range(0, PLANES, per_bank):
-                acc = psum.tile([P, per_bank, width], F32, name="acc%d" % (len(banks) % 4))
-                banks[j0, t0] = acc
-                for i in range(per_bank):
-                    rows = slice((t0 + i) * P, (t0 + i + 1) * P)
-                    nc.tensor.matmul_mx(
-                        out=acc[:, i, :],
-                        lhsT=w2_codes[:, rows].bitcast(FP8X4),
-                        lhsT_scale=w2_sc[:, rows],
-                        rhs=z_codes[:, cols].bitcast(FP8X4),
-                        rhs_scale=z_scales[:, cols],
-                        start=True,
-                        stop=True,
-                    )
+            nc.vector.quantize_mx(out=z_codes[:, cols].bitcast(FP8X4), scales=z_scales[:, cols], in_=z_woven[:])
+            per_bank = BANK // span
+            for s0 in range(j0, j0 + width, span):
+                for t0 in range(0, PLANES, per_bank):
+                    pool, tag = free_banks[len(banks)]
+                    acc = pool.tile([P, per_bank, span], F32, name=tag)
+                    banks[s0, t0] = acc
+                    for i in range(per_bank):
+                        rows = slice((t0 + i) * P, (t0 + i + 1) * P)
+                        nc.tensor.matmul_mx(
+                            out=acc[:, i, :],
+                            lhsT=w2_codes[:, rows].bitcast(FP8X4),
+                            lhsT_scale=w2_sc[:, rows],
+                            rhs=z_codes[:, s0 : s0 + span].bitcast(FP8X4),
+                            rhs_scale=z_scales[:, s0 : s0 + span],
+                            start=True,
+                            stop=True,
+                        )
 
-        def store(j0, width, place=None):
-            if place is None:
-                place = keep.tile([P, PLANES * width], F32, name="res%d" % j0)[:]
-            res[j0] = place.rearrange("p (t j) -> p t j", t=PLANES)
-            per_bank = BANK // width
-            for t0 in range(0, PLANES, per_bank):
-                held = res[j0][:, t0 : t0 + per_bank, :]
-                on_scalar(out=held, in_=banks[j0, t0][:])
-                nc.sync.dma_start(out=out_rows[:, t0 : t0 + per_bank, j0 : j0 + width], in_=held)
+        def result(j0, span):
+            return res[:, PLANES * j0 : PLANES * (j0 + span)].rearrange("p (t j) -> p t j", t=PLANES)
 
-        def round_result(engine_copy, j0, width):
-            weave(engine_copy, res[j0], ow[:, j0 * PLANES : (j0 + width) * PLANES])
+        def store(engine_copy, j0, span, firsts=None):
+            per_bank = BANK // span
+            for t0 in firsts or range(0, PLANES, per_bank):
+                held = result(j0, span)[:, t0 : t0 + per_bank, :]
+                engine_copy(out=held, in_=banks[j0, t0][:])
+                nc.sync.dma_start(out=out_rows[:, t0 : t0 + per_bank, j0 : j0 + span], in_=held)
+
+        def round_result(engine_copy, j0, span, first=0, width=None):
+            width = width or span
+            source = result(j0, span)[:, :, first : first + width]
+            weave(engine_copy, source, ow[:, (j0 + first) * PLANES : (j0 + first + width) * PLANES])
 
         def hand_on(j0, width):
             nc.vector.quantize_mx(
@@ -280,49 +280,47 @@ def tile_picked_tome8_silu_po_kernel(
         def store_words(j0, width):
             nc.sync.dma_start(out=out_words[:, j0 : j0 + width], in_=o_codes[:, j0 : j0 + width])
 
-        c0, c1, c2, c3 = (c * CHUNK for c in range(S // CHUNK))
-        c1b, c2b, c3b = c1 + STRIP, c2 + STRIP, c3 + STRIP
-        zw = woven_tile(S, "zw")
-        ow = woven_tile(S, "ow")
+        c0, c1, c2, c3 = (c * CHUNK for c in range(4))
+        c3b = c3 + STRIP
 
-        def z_cols(j0, width):
-            return zw[:, j0 * PLANES : (j0 + width) * PLANES]
-
+        home1 = keep.tile([P, PLANES, CHUNK], F32, tag="slot0")
+        fetch(home1, c1, (0,))
+        for cols in halves:
+            nc.scalar.activation(mg[LAST][:, cols], total[:, cols], ACT.Silu)
+        fetch(home1, c1, (1, 2, 3))
+        z_first = keep.tile([P, PLANES, CHUNK], F32, tag="wb_sb")
         for t in range(PLANES):
             nc.vector.tensor_tensor(z_first[:, t, :], looked_up(t, c0, CHUNK), y[t][:, c0 : c0 + CHUNK], ALU.add)
-        for j0 in (c1, c2):
-            fetch(2, j0, CHUNK)
-            fetch(3, j0, CHUNK)
-        fetch(2, c3, CHUNK)
-        fetch(3, c3, CHUNK)
-        fetch_on_vector(0, c3, CHUNK)
-        weave(on_vector, z_first[:], z_cols(c0, CHUNK))
-        fetch_on_vector(1, c3, CHUNK)
-        multiply(z_cols(c0, CHUNK), c0, CHUNK)
-        add_weave(z_cols(c1, STRIP), c1, STRIP)
-        add_weave(z_cols(c1b, STRIP), c1b, STRIP)
-        add_weave(z_cols(c2, STRIP), c2, STRIP)
-        multiply(z_cols(c1, CHUNK), c1, CHUNK)
-        store(c0, CHUNK)
-        add_weave(z_cols(c2b, STRIP), c2b, STRIP)
-        add_weave(z_cols(c3, STRIP), c3, STRIP)
-        multiply(z_cols(c2, CHUNK), c2, CHUNK)
-        store(c1, CHUNK)
-        add_weave(z_cols(c3b, STRIP), c3b, STRIP)
-        multiply(z_cols(c3, STRIP), c3, STRIP)
+        zw0 = woven_tile(CHUNK, "zw0")
+        weave(on_vector, z_first[:], zw0[:])
+        home2 = keep.tile([P, PLANES, CHUNK], F32, tag="slot1")
+        fetch(home2, c2, range(PLANES))
+        zw1 = add_weave(home1[:], c1, "zw1")
+        multiply(zw0, c0, CHUNK, CHUNK)
+        multiply(zw1, c1, CHUNK, CHUNK)
+        home3 = keep.tile([P, PLANES, CHUNK], F32, tag="slot0")
+        fetch(home3, c3, range(PLANES))
+        zw2 = add_weave(home2[:], c2, "zw0")
+        store(on_vector, c0, CHUNK, (0,))
+        multiply(zw2, c2, CHUNK, CHUNK)
+        store(on_scalar, c0, CHUNK, (2,))
+        store(on_scalar, c1, CHUNK)
+        zw3 = add_weave(home3[:, :, 0:STRIP], c3, "zw3")
+        zw4 = add_weave(home3[:, :, STRIP:CHUNK], c3b, "zw4")
+        multiply(zw3, c3, STRIP, STRIP)
+        multiply(zw4, c3b, STRIP, STRIP)
+        store(on_scalar, c2, CHUNK)
         round_result(on_vector, c0, CHUNK)
-        multiply(z_cols(c3b, STRIP), c3b, STRIP)
-        store(c2, CHUNK)
-        hand_on(c0, CHUNK)
         round_result(on_vector, c1, CHUNK)
-        store(c3, STRIP)
-        store(c3b, STRIP)
-        round_result(on_vector, c2, CHUNK)
+        hand_on(c0, CHUNK)
+        store(on_scalar, c3, STRIP)
+        store(on_scalar, c3b, STRIP)
         hand_on(c1, CHUNK)
-        store_words(c0, V)
+        store_words(c0, 2 * CHUNK)
+        round_result(on_vector, c2, CHUNK)
+        round_result(on_vector, c3, STRIP)
         hand_on(c2, CHUNK)
         store_words(c2, CHUNK)
-        round_result(on_vector, c3, STRIP)
         round_result(on_vector, c3b, STRIP)
         hand_on(c3, CHUNK)
         store_words(c3, CHUNK)

@@ -24,7 +24,6 @@ BLOCKS = V // P
 CHUNK = 256
 STRIP = CHUNK // 2
 LAST = PLANES - 1
-FIRST = CHUNK
 
 EARLY_WORDS = T // 4
 PLANE0_PASSES = (512, 256, 128, 128)
@@ -149,63 +148,17 @@ def tile_picked_tome8_silu_po_kernel(
             in_=w2s_raw[:].rearrange("p (m t) -> p t m", t=PLANES),
         )
 
-        y_late = keep.tile([P, PLANES, S - FIRST], F32)
+        y_late = keep.tile([P, PLANES, 2 * CHUNK], F32)
         for t in range(PLANES):
-            nc.sync.dma_start(out=y_late[:, t, :], in_=y[t][:, FIRST:S])
+            nc.sync.dma_start(out=y_late[:, t, :], in_=y[t][:, CHUNK : 3 * CHUNK])
 
+        c0, c1, c2, c3 = (c * CHUNK for c in range(4))
+        c0b, c3b = c0 + STRIP, c3 + STRIP
         mg = [keep.tile([P, V], F32, name="mg%d" % t) for t in range(PLANES)]
-
-        def take_part(t, which):
-            part = keep.tile([P, V], F32, name="part%d%d" % (t, which))
-            offsets, weight = ((a1_sb, wa_sb), (a2_sb, wb_sb))[which]
-            nc.vector.tensor_tensor(part[:], y[t][:].indirect(offsets[:]), weight[:], ALU.mult)
-            return part
-
-        turned01 = keep.tile([P, V], F32)
-        turned2 = keep.tile([P, V], F32, tag="slot0")
-        for t in range(LAST):
-            first = take_part(t, 0)
-            summed = [psum_mix.tile([P, P], F32, name="summed%d" % b) for b in range(BLOCKS)]
-            for b in range(BLOCKS):
-                nc.tensor.matmul(
-                    summed[b][:], first[:, b * P : (b + 1) * P], ident[:], start=True, stop=False, is_transpose=True
-                )
-            second = take_part(t, 1)
-            turned = [(turned01 if t < 2 else turned2)[:, b * P : (b + 1) * P] for b in range(BLOCKS)]
-            if t == 2:
-                turned[LAST] = mg[LAST][:, (V - P) // 2 : (V + P) // 2]
-            for b in range(BLOCKS):
-                nc.tensor.matmul(
-                    summed[b][:], second[:, b * P : (b + 1) * P], ident[:], start=False, stop=True, is_transpose=True
-                )
-                nc.scalar.activation(turned[b], summed[b][:], ACT.Silu)
-            for h in range(2):
-                back_turned = psum.tile([P, 2 * P], F32, name="acc%d" % (2 + h))
-                for i in range(2):
-                    nc.tensor.transpose(back_turned[:, i * P : (i + 1) * P], turned[2 * h + i], ident[:])
-                on_scalar(out=mg[t][:, 2 * h * P : 2 * (h + 1) * P], in_=back_turned[:])
-
-        first = take_part(LAST, 0)
-        second = keep.tile([P, V], F32)
-        total = keep.tile([P, V], F32, tag="slot1")
-        halves = (slice(0, V // 2), slice(V // 2, V))
-        for h, cols in enumerate(halves):
-            offsets = a2_sb[:, h * V // 32 : (h + 1) * V // 32]
-            nc.vector.tensor_tensor(second[:, cols], y[LAST][:].indirect(offsets), wb_sb[:, cols], ALU.mult)
-        for cols in halves:
-            nc.vector.tensor_tensor(total[:, cols], first[:, cols], second[:, cols], ALU.add)
-
-        z_codes = keep.tile([P, S], U32, align_bytes=64)
-        z_scales = keep.tile([P, S], U8, align_bytes=64)
-        o_scales = keep.tile([P, S], U8, align_bytes=64)
-        o_codes = keep.tile([P, S], I32, align_bytes=64)
-        ow = keep.tile([P, S * PLANES], BF16, align_bytes=64)
-        res = keep.tile([P, PLANES * S], F32)
-        out_rows = out_0.rearrange("(p t) j -> p t j", t=PLANES)
-        out_words = out_1[0].rearrange("p c r -> p (c r)").bitcast(I32)
-        banks = {}
-        free_banks = [(psum, "acc0"), (psum, "acc1")] + [(psum_mix, "summed%d" % b) for b in range(4)]
-        free_banks = free_banks + [(psum, "acc2"), (psum, "acc3")]
+        stage1 = keep.tile([P, 5 * CHUNK], F32)
+        stage2 = keep.tile([P, 4 * CHUNK], F32)
+        home1 = stage1[:, CHUNK : 5 * CHUNK].rearrange("p (t j) -> p t j", t=PLANES)
+        home2 = stage2[:].rearrange("p (t j) -> p t j", t=PLANES)
 
         def looked_up(t, j0, width):
             return mg[t][:].indirect(back_sb[:, j0 // 16 : (j0 + width) // 16])
@@ -214,19 +167,92 @@ def tile_picked_tome8_silu_po_kernel(
             for t in planes:
                 nc.scalar.activation(home[:, t, :], looked_up(t, j0, home.shape[2]), ACT.Copy)
 
-        def woven_tile(width, tag):
-            return keep.tile([P, width * PLANES], BF16, name="woven", tag=tag, align_bytes=64)
+        def take_part(t, which, part):
+            offsets, weight = ((a1_sb, wa_sb), (a2_sb, wb_sb))[which]
+            nc.vector.tensor_tensor(part, y[t][:].indirect(offsets[:]), weight[:], ALU.mult)
 
-        def add_weave(home, j0, tag):
-            width = home.shape[2]
-            zw = woven_tile(width, tag)
+        HALF = V // 2
+        halves = (slice(0, HALF), slice(HALF, V))
+        second0 = keep.tile([P, V], F32)
+        seconds = (second0[:], stage1[:, 0:V], stage1[:, V : 2 * V])
+        last_turned = {1: home2[:, 0, :], 2: mg[LAST][:, P // 2 : P // 2 + HALF]}
+        sum_banks = ((psum_mix, "summed0"), (psum_mix, "summed1"), (psum_mix, "summed2"), (psum_mix, "summed3"))
+        sum_banks = sum_banks + ((psum, "acc0"), (psum, "acc1"))
+        for t in range(LAST):
+            order = (1, 0) if t == 2 else (0, 1)
+            first = keep.tile([P, V], F32, name="first%d" % t)
+            take_part(t, 0, first[:])
+            summed = {}
+            for n, h in enumerate(order):
+                pool, tag = sum_banks[2 * t + n]
+                summed[h] = pool.tile([P, HALF], F32, name=tag)
+                for i in range(2):
+                    block = first[:, (2 * h + i) * P : (2 * h + i + 1) * P]
+                    nc.tensor.matmul(
+                        summed[h][:, i * P : (i + 1) * P], block, ident[:], start=i == 0, stop=False, is_transpose=True
+                    )
+            take_part(t, 1, seconds[t])
+            turned_tile = keep.tile([P, V], F32, name="turned%d" % t)
+            turned = {h: turned_tile[:, halves[h]] for h in order}
+            turned[order[1]] = last_turned.get(t, turned[order[1]])
+            for h in order:
+                for i in range(2):
+                    block = seconds[t][:, (2 * h + i) * P : (2 * h + i + 1) * P]
+                    nc.tensor.matmul(
+                        summed[h][:, i * P : (i + 1) * P], block, ident[:], start=False, stop=i == 1, is_transpose=True
+                    )
+                nc.scalar.activation(turned[h], summed[h][:], ACT.Silu)
+            if t > 0:
+                fetch(home1, c1, (t - 1,))
+            for n, h in enumerate(order):
+                back_turned = psum.tile([P, HALF], F32, name="acc%d" % (2 + n))
+                for i in range(2):
+                    nc.tensor.transpose(back_turned[:, i * P : (i + 1) * P], turned[h][:, i * P : (i + 1) * P], ident[:])
+                on_scalar(out=mg[t][:, halves[h]], in_=back_turned[:])
+            if t == 1:
+                fetch(home2, c2, (0,))
+
+        first = keep.tile([P, V], F32)
+        take_part(LAST, 0, first[:])
+        second = keep.tile([P, V], F32)
+        total_b = keep.tile([P, HALF], F32, tag="late")
+        totals = (stage2[:, 3 * STRIP : 5 * STRIP], total_b[:])
+        for h, cols in enumerate(halves):
+            offsets = a2_sb[:, h * HALF // 16 : (h + 1) * HALF // 16]
+            nc.vector.tensor_tensor(second[:, cols], y[LAST][:].indirect(offsets), wb_sb[:, cols], ALU.mult)
+        for h, cols in enumerate(halves):
+            nc.vector.tensor_tensor(totals[h], first[:, cols], second[:, cols], ALU.add)
+        for h, cols in enumerate(halves):
+            nc.scalar.activation(mg[LAST][:, cols], totals[h], ACT.Silu)
+
+        z_codes = keep.tile([P, S], U32, align_bytes=64)
+        z_scales = keep.tile([P, S], U8, align_bytes=64)
+        o_scales = keep.tile([P, S], U8, align_bytes=64)
+        o_codes = keep.tile([P, S], I32, align_bytes=64)
+        zw = keep.tile([P, S * PLANES], BF16, align_bytes=64)
+        ow = keep.tile([P, S * PLANES], BF16, align_bytes=64)
+        res = [keep.tile([P, PLANES, CHUNK], F32, name="res%d" % c) for c in range(4)]
+        out_rows = out_0.rearrange("(p t) j -> p t j", t=PLANES)
+        out_words = out_1[0].rearrange("p c r -> p (c r)").bitcast(I32)
+        banks = {}
+        free_banks = sum_banks + ((psum, "acc2"), (psum, "acc3"))
+
+        def woven(tile, j0, width):
+            return tile[:, j0 * PLANES : (j0 + width) * PLANES]
+
+        def unmerge(home, j0, t, first=0, width=CHUNK):
+            j = j0 + first
             nc.vector.tensor_tensor(
-                zw[:].rearrange("p (c i t) -> p c t i", i=4, t=PLANES),
+                home[:, t, first : first + width], looked_up(t, j, width), y[t][:, j : j + width], ALU.add
+            )
+
+        def add_weave(home, j0):
+            nc.vector.tensor_tensor(
+                woven(zw, j0, CHUNK).rearrange("p (c i t) -> p c t i", i=4, t=PLANES),
                 home.rearrange("p t (c i) -> p c t i", i=4),
-                y_late[:, :, j0 - FIRST : j0 - FIRST + width].rearrange("p t (c i) -> p c t i", i=4),
+                y_late[:, :, j0 - c1 : j0 - c1 + CHUNK].rearrange("p t (c i) -> p c t i", i=4),
                 ALU.add,
             )
-            return zw
 
         def weave(engine_copy, source, target):
             engine_copy(
@@ -234,9 +260,11 @@ def tile_picked_tome8_silu_po_kernel(
                 in_=source.rearrange("p t (c i) -> p c t i", i=4),
             )
 
-        def multiply(z_woven, j0, width, span):
+        def multiply(j0, width, span):
             cols = slice(j0, j0 + width)
-            nc.vector.quantize_mx(out=z_codes[:, cols].bitcast(FP8X4), scales=z_scales[:, cols], in_=z_woven[:])
+            nc.vector.quantize_mx(
+                out=z_codes[:, cols].bitcast(FP8X4), scales=z_scales[:, cols], in_=woven(zw, j0, width)
+            )
             per_bank = BANK // span
             for s0 in range(j0, j0 + width, span):
                 for t0 in range(0, PLANES, per_bank):
@@ -255,73 +283,77 @@ def tile_picked_tome8_silu_po_kernel(
                             stop=True,
                         )
 
-        def result(j0, span):
-            return res[:, PLANES * j0 : PLANES * (j0 + span)].rearrange("p (t j) -> p t j", t=PLANES)
+        def result(j0, width):
+            return res[j0 // CHUNK][:, :, j0 % CHUNK : j0 % CHUNK + width]
 
-        def store(engine_copy, j0, span, firsts=None):
-            per_bank = BANK // span
-            for t0 in firsts or range(0, PLANES, per_bank):
-                held = result(j0, span)[:, t0 : t0 + per_bank, :]
-                engine_copy(out=held, in_=banks[j0, t0][:])
-                nc.sync.dma_start(out=out_rows[:, t0 : t0 + per_bank, j0 : j0 + span], in_=held)
+        def empty(j0, t0=0):
+            acc = banks[j0, t0]
+            on_scalar(out=result(j0, acc.shape[2])[:, t0 : t0 + acc.shape[1], :], in_=acc[:])
 
-        def round_result(engine_copy, j0, span, first=0, width=None):
-            width = width or span
-            source = result(j0, span)[:, :, first : first + width]
-            weave(engine_copy, source, ow[:, (j0 + first) * PLANES : (j0 + first + width) * PLANES])
+        def store(j0, width, t0=0, planes=PLANES):
+            rows = slice(t0, t0 + planes)
+            nc.sync.dma_start(out=out_rows[:, rows, j0 : j0 + width], in_=result(j0, width)[:, rows, :])
+
+        def round_result(engine_copy, j0, width):
+            weave(engine_copy, result(j0, width), woven(ow, j0, width))
 
         def hand_on(j0, width):
             nc.vector.quantize_mx(
                 out=o_codes[:, j0 : j0 + width].bitcast(FP8X4),
                 scales=o_scales[:, j0 : j0 + width],
-                in_=ow[:, j0 * PLANES : (j0 + width) * PLANES],
+                in_=woven(ow, j0, width),
             )
 
         def store_words(j0, width):
             nc.sync.dma_start(out=out_words[:, j0 : j0 + width], in_=o_codes[:, j0 : j0 + width])
 
-        c0, c1, c2, c3 = (c * CHUNK for c in range(4))
-        c3b = c3 + STRIP
-
-        home1 = keep.tile([P, PLANES, CHUNK], F32, tag="slot0")
-        fetch(home1, c1, (0,))
-        for cols in halves:
-            nc.scalar.activation(mg[LAST][:, cols], total[:, cols], ACT.Silu)
-        fetch(home1, c1, (1, 2, 3))
-        z_first = keep.tile([P, PLANES, CHUNK], F32, tag="wb_sb")
+        fetch(home1, c1, (2, 3))
+        fetch(home2, c2, (1, 2, 3))
+        home0 = keep.tile([P, PLANES, CHUNK], F32, tag="wb_sb")
+        home3 = keep.tile([P, PLANES, CHUNK], F32, tag="late")
         for t in range(PLANES):
-            nc.vector.tensor_tensor(z_first[:, t, :], looked_up(t, c0, CHUNK), y[t][:, c0 : c0 + CHUNK], ALU.add)
-        zw0 = woven_tile(CHUNK, "zw0")
-        weave(on_vector, z_first[:], zw0[:])
-        home2 = keep.tile([P, PLANES, CHUNK], F32, tag="slot1")
-        fetch(home2, c2, range(PLANES))
-        zw1 = add_weave(home1[:], c1, "zw1")
-        multiply(zw0, c0, CHUNK, CHUNK)
-        multiply(zw1, c1, CHUNK, CHUNK)
-        home3 = keep.tile([P, PLANES, CHUNK], F32, tag="slot0")
-        fetch(home3, c3, range(PLANES))
-        zw2 = add_weave(home2[:], c2, "zw0")
-        store(on_vector, c0, CHUNK, (0,))
-        multiply(zw2, c2, CHUNK, CHUNK)
-        store(on_scalar, c0, CHUNK, (2,))
-        store(on_scalar, c1, CHUNK)
-        zw3 = add_weave(home3[:, :, 0:STRIP], c3, "zw3")
-        zw4 = add_weave(home3[:, :, STRIP:CHUNK], c3b, "zw4")
-        multiply(zw3, c3, STRIP, STRIP)
-        multiply(zw4, c3b, STRIP, STRIP)
-        store(on_scalar, c2, CHUNK)
-        round_result(on_vector, c0, CHUNK)
-        round_result(on_vector, c1, CHUNK)
+            unmerge(home0, c0, t)
+        unmerge(home3, c3, 0)
+        weave(on_vector, home0[:], woven(zw, c0, CHUNK))
+        unmerge(home3, c3, 1)
+        multiply(c0, CHUNK, STRIP)
+        add_weave(home1, c1)
+        unmerge(home3, c3, 2)
+        multiply(c1, CHUNK, CHUNK)
+        add_weave(home2, c2)
+        empty(c0)
+        empty(c0b)
+        store(c0, CHUNK)
+        round_result(on_scalar, c0, STRIP)
+        round_result(on_scalar, c0b, STRIP)
+        unmerge(home3, c3, 3, 0, STRIP)
+        unmerge(home3, c3, 3, STRIP, STRIP)
+        multiply(c2, CHUNK, CHUNK)
+        empty(c1, 0)
+        store(c1, CHUNK, 0, 2)
+        empty(c1, 2)
+        store(c1, CHUNK, 2, 2)
+        weave(on_scalar, home3[:, :, 0:STRIP], woven(zw, c3, STRIP))
+        weave(on_vector, home3[:, :, STRIP:CHUNK], woven(zw, c3b, STRIP))
         hand_on(c0, CHUNK)
-        store(on_scalar, c3, STRIP)
-        store(on_scalar, c3b, STRIP)
-        hand_on(c1, CHUNK)
-        store_words(c0, 2 * CHUNK)
+        store_words(c0, CHUNK)
+        multiply(c3, STRIP, STRIP)
+        multiply(c3b, STRIP, STRIP)
+        empty(c2, 0)
+        store(c2, CHUNK, 0, 2)
+        empty(c2, 2)
+        store(c2, CHUNK, 2, 2)
+        round_result(on_vector, c1, CHUNK)
         round_result(on_vector, c2, CHUNK)
+        hand_on(c1, CHUNK)
+        empty(c3)
+        store(c3, STRIP)
         round_result(on_vector, c3, STRIP)
+        empty(c3b)
+        store(c3b, STRIP)
         hand_on(c2, CHUNK)
-        store_words(c2, CHUNK)
         round_result(on_vector, c3b, STRIP)
+        store_words(c1, 2 * CHUNK)
         hand_on(c3, CHUNK)
         store_words(c3, CHUNK)
 

@@ -153,7 +153,7 @@ def tile_picked_tome8_silu_po_kernel(
             nc.sync.dma_start(out=y_late[:, t, :], in_=y[t][:, CHUNK : 3 * CHUNK])
 
         c0, c1, c2, c3 = (c * CHUNK for c in range(4))
-        c0b, c3b = c0 + STRIP, c3 + STRIP
+        c0b, c1b, c2b, c3b = (c + STRIP for c in (c0, c1, c2, c3))
         mg = [keep.tile([P, V], F32, name="mg%d" % t) for t in range(PLANES)]
         stage1 = keep.tile([P, 5 * CHUNK], F32)
         stage2 = keep.tile([P, 4 * CHUNK], F32)
@@ -246,11 +246,12 @@ def tile_picked_tome8_silu_po_kernel(
                 home[:, t, first : first + width], looked_up(t, j, width), y[t][:, j : j + width], ALU.add
             )
 
-        def add_weave(home, j0):
+        def add_weave(home, j0, first=0, width=CHUNK):
+            j = j0 + first
             nc.vector.tensor_tensor(
-                woven(zw, j0, CHUNK).rearrange("p (c i t) -> p c t i", i=4, t=PLANES),
-                home.rearrange("p t (c i) -> p c t i", i=4),
-                y_late[:, :, j0 - c1 : j0 - c1 + CHUNK].rearrange("p t (c i) -> p c t i", i=4),
+                woven(zw, j, width).rearrange("p (c i t) -> p c t i", i=4, t=PLANES),
+                home[:, :, first : first + width].rearrange("p t (c i) -> p c t i", i=4),
+                y_late[:, :, j - c1 : j - c1 + width].rearrange("p t (c i) -> p c t i", i=4),
                 ALU.add,
             )
 
@@ -260,15 +261,15 @@ def tile_picked_tome8_silu_po_kernel(
                 in_=source.rearrange("p t (c i) -> p c t i", i=4),
             )
 
-        def multiply(j0, width, span):
+        def multiply(j0, width, span, per_bank=None):
             cols = slice(j0, j0 + width)
             nc.vector.quantize_mx(
                 out=z_codes[:, cols].bitcast(FP8X4), scales=z_scales[:, cols], in_=woven(zw, j0, width)
             )
-            per_bank = BANK // span
+            per_bank = per_bank or BANK // span
             for s0 in range(j0, j0 + width, span):
                 for t0 in range(0, PLANES, per_bank):
-                    pool, tag = free_banks[len(banks)]
+                    pool, tag = free_banks[len(banks) % len(free_banks)]
                     acc = pool.tile([P, per_bank, span], F32, name=tag)
                     banks[s0, t0] = acc
                     for i in range(per_bank):
@@ -286,9 +287,9 @@ def tile_picked_tome8_silu_po_kernel(
         def result(j0, width):
             return res[j0 // CHUNK][:, :, j0 % CHUNK : j0 % CHUNK + width]
 
-        def empty(j0, t0=0):
+        def empty(j0, t0=0, engine_copy=on_scalar):
             acc = banks[j0, t0]
-            on_scalar(out=result(j0, acc.shape[2])[:, t0 : t0 + acc.shape[1], :], in_=acc[:])
+            engine_copy(out=result(j0, acc.shape[2])[:, t0 : t0 + acc.shape[1], :], in_=acc[:])
 
         def store(j0, width, t0=0, planes=PLANES):
             rows = slice(t0, t0 + planes)
@@ -307,55 +308,66 @@ def tile_picked_tome8_silu_po_kernel(
         def store_words(j0, width):
             nc.sync.dma_start(out=out_words[:, j0 : j0 + width], in_=o_codes[:, j0 : j0 + width])
 
-        fetch(home1, c1, (2, 3))
-        fetch(home2, c2, (1, 2, 3))
         home0 = keep.tile([P, PLANES, CHUNK], F32, tag="wb_sb")
         home3 = keep.tile([P, PLANES, CHUNK], F32, tag="late")
-        for t in range(PLANES):
-            unmerge(home0, c0, t)
-        unmerge(home3, c3, 0)
-        weave(on_vector, home0[:], woven(zw, c0, CHUNK))
-        unmerge(home3, c3, 1)
-        multiply(c0, CHUNK, STRIP)
-        add_weave(home1, c1)
-        unmerge(home3, c3, 2)
-        multiply(c1, CHUNK, CHUNK)
-        add_weave(home2, c2)
-        empty(c0)
-        empty(c0b)
-        store(c0, CHUNK)
-        round_result(on_scalar, c0, STRIP)
-        round_result(on_scalar, c0b, STRIP)
+        fetch(home1, c1, (2,))
+        fetch(home1, c1, (3,))
+        fetch(home2, c2, (1,))
+        fetch(home2, c2, (2,))
+        fetch(home2, c2, (3,))
+        unmerge(home0, c0, 0)
+        unmerge(home0, c0, 1)
+        unmerge(home0, c0, 2)
+        unmerge(home0, c0, 3)
+        unmerge(home3, c3, 0, 0, STRIP)
+        unmerge(home3, c3, 1, 0, STRIP)
+        weave(on_vector, home0[:, :, 0 : 0 + CHUNK], woven(zw, c0, CHUNK))
+        add_weave(home1, c1, 0, STRIP)
+        multiply(c0, CHUNK, CHUNK)
+        add_weave(home1, c1, STRIP, STRIP)
+        unmerge(home3, c3, 2, 0, STRIP)
         unmerge(home3, c3, 3, 0, STRIP)
-        unmerge(home3, c3, 3, STRIP, STRIP)
-        multiply(c2, CHUNK, CHUNK)
-        empty(c1, 0)
-        store(c1, CHUNK, 0, 2)
-        empty(c1, 2)
-        store(c1, CHUNK, 2, 2)
-        weave(on_scalar, home3[:, :, 0:STRIP], woven(zw, c3, STRIP))
-        weave(on_vector, home3[:, :, STRIP:CHUNK], woven(zw, c3b, STRIP))
-        hand_on(c0, CHUNK)
-        store_words(c0, CHUNK)
+        multiply(c1, CHUNK, CHUNK)
+        weave(on_vector, home3[:, :, 0 : 0 + STRIP], woven(zw, c3, STRIP))
+        add_weave(home2, c2, 0, STRIP)
         multiply(c3, STRIP, STRIP)
-        multiply(c3b, STRIP, STRIP)
-        empty(c2, 0)
-        store(c2, CHUNK, 0, 2)
-        empty(c2, 2)
-        store(c2, CHUNK, 2, 2)
-        round_result(on_vector, c1, CHUNK)
-        round_result(on_vector, c2, CHUNK)
-        hand_on(c1, CHUNK)
-        empty(c3)
+        add_weave(home2, c2, STRIP, STRIP)
+        empty(c0, 0, on_scalar)
+        store(c0, CHUNK, 0, 2)
+        empty(c0, 2, on_scalar)
+        store(c0, CHUNK, 2, 2)
+        empty(c1, 0, on_scalar)
+        store(c1, CHUNK, 0, 2)
+        empty(c1, 2, on_scalar)
+        store(c1, CHUNK, 2, 2)
+        unmerge(home3, c3, 0, STRIP, STRIP)
+        unmerge(home3, c3, 1, STRIP, STRIP)
+        multiply(c2, CHUNK, CHUNK)
+        round_result(on_scalar, c0, STRIP)
+        empty(c3, 0, on_scalar)
         store(c3, STRIP)
-        round_result(on_vector, c3, STRIP)
-        empty(c3b)
+        round_result(on_scalar, c0b, STRIP)
+        unmerge(home3, c3, 2, STRIP, STRIP)
+        unmerge(home3, c3, 3, STRIP, STRIP)
+        round_result(on_vector, c1, STRIP)
+        weave(on_vector, home3[:, :, STRIP : STRIP + STRIP], woven(zw, c3b, STRIP))
+        round_result(on_vector, c1b, STRIP)
+        multiply(c3b, STRIP, STRIP)
+        empty(c2, 0, on_scalar)
+        store(c2, CHUNK, 0, 2)
+        empty(c2, 2, on_scalar)
+        store(c2, CHUNK, 2, 2)
+        hand_on(c0, 512)
+        store_words(c0, 512)
+        round_result(on_scalar, c3, STRIP)
+        empty(c3b, 0, on_scalar)
         store(c3b, STRIP)
+        round_result(on_vector, c2, CHUNK)
+        hand_on(c3, STRIP)
         hand_on(c2, CHUNK)
         round_result(on_vector, c3b, STRIP)
-        store_words(c1, 2 * CHUNK)
-        hand_on(c3, CHUNK)
-        store_words(c3, CHUNK)
+        hand_on(c3b, STRIP)
+        store_words(c2, 512)
 
         for r in range(4):
             in_sbuf, in_hbm = scale_rows(o_scales, out_2, r)

@@ -148,16 +148,18 @@ def tile_picked_tome8_silu_po_kernel(
             in_=w2s_raw[:].rearrange("p (m t) -> p t m", t=PLANES),
         )
 
-        y_late = keep.tile([P, PLANES, 2 * CHUNK], F32)
+        y_late = keep.tile([P, PLANES, 5 * STRIP], F32)
         for t in range(PLANES):
-            nc.sync.dma_start(out=y_late[:, t, :], in_=y[t][:, CHUNK : 3 * CHUNK])
+            nc.sync.dma_start(out=y_late[:, t, :], in_=y[t][:, CHUNK : S - STRIP])
 
         c0, c1, c2, c3 = (c * CHUNK for c in range(4))
         c0b, c1b, c2b, c3b = (c + STRIP for c in (c0, c1, c2, c3))
         mg = [keep.tile([P, V], F32, name="mg%d" % t) for t in range(PLANES)]
-        stage1 = keep.tile([P, 5 * CHUNK], F32)
+        stage1 = keep.tile([P, 7 * CHUNK], F32)
         stage2 = keep.tile([P, 4 * CHUNK], F32)
         home1 = stage1[:, CHUNK : 5 * CHUNK].rearrange("p (t j) -> p t j", t=PLANES)
+        home3a = stage1[:, 3 * CHUNK : 7 * CHUNK].rearrange("p (t j) -> p t j", t=PLANES)[:, :, 0:STRIP]
+        home3b = stage1[:, 5 * CHUNK : 7 * CHUNK].rearrange("p (t j) -> p t j", t=PLANES)
         home2 = stage2[:].rearrange("p (t j) -> p t j", t=PLANES)
 
         def looked_up(t, j0, width):
@@ -215,8 +217,7 @@ def tile_picked_tome8_silu_po_kernel(
         first = keep.tile([P, V], F32)
         take_part(LAST, 0, first[:])
         second = keep.tile([P, V], F32)
-        total_b = keep.tile([P, HALF], F32, tag="late")
-        totals = (stage2[:, 3 * STRIP : 5 * STRIP], total_b[:])
+        totals = (stage2[:, 3 * STRIP : 5 * STRIP], stage1[:, 5 * CHUNK + STRIP // 2 : 6 * CHUNK + STRIP // 2])
         for h, cols in enumerate(halves):
             offsets = a2_sb[:, h * HALF // 16 : (h + 1) * HALF // 16]
             nc.vector.tensor_tensor(second[:, cols], y[LAST][:].indirect(offsets), wb_sb[:, cols], ALU.mult)
@@ -309,7 +310,6 @@ def tile_picked_tome8_silu_po_kernel(
             nc.sync.dma_start(out=out_words[:, j0 : j0 + width], in_=o_codes[:, j0 : j0 + width])
 
         home0 = keep.tile([P, PLANES, CHUNK], F32, tag="wb_sb")
-        home3 = keep.tile([P, PLANES, CHUNK], F32, tag="late")
         fetch(home1, c1, (2,))
         fetch(home1, c1, (3,))
         fetch(home2, c2, (1,))
@@ -319,54 +319,53 @@ def tile_picked_tome8_silu_po_kernel(
         unmerge(home0, c0, 1)
         unmerge(home0, c0, 2)
         unmerge(home0, c0, 3)
-        unmerge(home3, c3, 0, 0, STRIP)
-        unmerge(home3, c3, 1, 0, STRIP)
+        unmerge(home3b, c3b, 0, 0, STRIP)
+        unmerge(home3b, c3b, 1, 0, STRIP)
         weave(on_vector, home0[:, :, 0 : 0 + CHUNK], woven(zw, c0, CHUNK))
         add_weave(home1, c1, 0, STRIP)
+        fetch(home3a, c3, (0, 1))
         multiply(c0, CHUNK, CHUNK)
         add_weave(home1, c1, STRIP, STRIP)
-        unmerge(home3, c3, 2, 0, STRIP)
-        unmerge(home3, c3, 3, 0, STRIP)
+        unmerge(home3b, c3b, 2, 0, STRIP)
+        unmerge(home3b, c3b, 3, 0, STRIP)
         multiply(c1, CHUNK, CHUNK)
-        weave(on_vector, home3[:, :, 0 : 0 + STRIP], woven(zw, c3, STRIP))
+        weave(on_vector, home3b, woven(zw, c3b, STRIP))
         add_weave(home2, c2, 0, STRIP)
-        multiply(c3, STRIP, STRIP)
+        multiply(c3b, STRIP, STRIP)
         add_weave(home2, c2, STRIP, STRIP)
         empty(c0, 0, on_scalar)
         store(c0, CHUNK, 0, 2)
         empty(c0, 2, on_scalar)
         store(c0, CHUNK, 2, 2)
+        fetch(home3a, c3, (2,))
         empty(c1, 0, on_scalar)
         store(c1, CHUNK, 0, 2)
+        fetch(home3a, c3, (3,))
         empty(c1, 2, on_scalar)
         store(c1, CHUNK, 2, 2)
-        unmerge(home3, c3, 0, STRIP, STRIP)
-        unmerge(home3, c3, 1, STRIP, STRIP)
+        empty(c3b, 0, on_scalar)
+        store(c3b, STRIP)
+        round_result(on_vector, c0b, STRIP)
         multiply(c2, CHUNK, CHUNK)
+        add_weave(home3a, c3, 0, STRIP)
         round_result(on_scalar, c0, STRIP)
-        empty(c3, 0, on_scalar)
-        store(c3, STRIP)
-        round_result(on_scalar, c0b, STRIP)
-        unmerge(home3, c3, 2, STRIP, STRIP)
-        unmerge(home3, c3, 3, STRIP, STRIP)
         round_result(on_vector, c1, STRIP)
-        weave(on_vector, home3[:, :, STRIP : STRIP + STRIP], woven(zw, c3b, STRIP))
-        round_result(on_vector, c1b, STRIP)
-        multiply(c3b, STRIP, STRIP)
+        multiply(c3, STRIP, STRIP)
         empty(c2, 0, on_scalar)
         store(c2, CHUNK, 0, 2)
         empty(c2, 2, on_scalar)
         store(c2, CHUNK, 2, 2)
+        round_result(on_vector, c1b, STRIP)
+        round_result(on_vector, c3b, STRIP)
+        empty(c3, 0, on_scalar)
+        store(c3, STRIP)
         hand_on(c0, 512)
         store_words(c0, 512)
-        round_result(on_scalar, c3, STRIP)
-        empty(c3b, 0, on_scalar)
-        store(c3b, STRIP)
-        round_result(on_vector, c2, CHUNK)
-        hand_on(c3, STRIP)
+        round_result(on_scalar, c2b, STRIP)
+        round_result(on_vector, c2, STRIP)
+        round_result(on_vector, c3, STRIP)
         hand_on(c2, CHUNK)
-        round_result(on_vector, c3b, STRIP)
-        hand_on(c3b, STRIP)
+        hand_on(c3, CHUNK)
         store_words(c2, 512)
 
         for r in range(4):

@@ -25,9 +25,8 @@ CHUNK = 256
 STRIP = CHUNK // 2
 LAST = PLANES - 1
 
-EARLY_WORDS = T // 4
-PLANE0_PASSES = (512, 256, 128, 128)
-W1_SCALAR_COLS = (96, 80)
+PIECES = (256, 256, 256, 128, 128)
+HALF = V // 2
 
 
 def tile_picked_tome8_silu_po_kernel(
@@ -38,7 +37,9 @@ def tile_picked_tome8_silu_po_kernel(
     with ExitStack() as ctx:
         keep = ctx.enter_context(tc.tile_pool(name="keep", bufs=1))
         psum = ctx.enter_context(tc.psum_pool(name="psum", bufs=1))
-        psum_mix = ctx.enter_context(tc.psum_pool(name="psum_mix", bufs=1))
+
+        def bank(number, *shape):
+            return psum.tile([P, *shape], F32, name="bank%d" % number)
 
         def scale_rows(tile, rows, r):
             return tile[r:P:QUADRANT, :].bitcast(I32), rows[0, r:16:4, :].bitcast(I32)
@@ -69,33 +70,27 @@ def tile_picked_tome8_silu_po_kernel(
         xw_all = keep.tile([P, T], I32, align_bytes=64)
         wa_sb = keep.tile([P, V], F32)
         w2w_raw = keep.tile([P, N], I32, align_bytes=64)
-        x_rows = x_words[0].rearrange("p c r -> p (c r)").bitcast(I32)
-        nc.sync.dma_start(out=xw_all[:, 0:EARLY_WORDS], in_=x_rows[:, 0:EARLY_WORDS])
+        w1_rows = w1.rearrange("(p j) c -> p j c", j=PLANES)
+        nc.sync.dma_start(out=w1_raw[:, 0:1, :], in_=w1_rows[:, 0:1, :])
         nc.sync.dma_start(offs_sb[:], offs)
         load_scales(xs_all, x_scales)
-        nc.sync.dma_start(out=xw_all[:, EARLY_WORDS:T], in_=x_rows[:, EARLY_WORDS:T])
-        nc.sync.dma_start(out=w1_raw[:], in_=w1.rearrange("(p j) c -> p j c", j=PLANES))
-        nc.sync.dma_start(out=wa_sb[:], in_=wa.rearrange("(p j) v -> p j v", j=PLANES)[:, 0, :])
-        nc.sync.dma_start(out=w2w_raw[:], in_=w2_words[0].rearrange("p c r -> p (c r)").bitcast(I32))
+        nc.sync.dma_start(out=w1_raw[:, 1:PLANES, :], in_=w1_rows[:, 1:PLANES, :])
+        nc.sync.dma_start(out=xw_all[:], in_=x_words[0].rearrange("p c r -> p (c r)").bitcast(I32))
         load_scales(w2s_raw, w2_scales)
         nc.sync.dma_start(a1_sb[:], a1)
         nc.sync.dma_start(a2_sb[:], a2)
+        nc.sync.dma_start(out=wa_sb[:], in_=wa.rearrange("(p j) v -> p j v", j=PLANES)[:, 0, :])
+        nc.sync.dma_start(out=w2w_raw[:], in_=w2_words[0].rearrange("p c r -> p (c r)").bitcast(I32))
         nc.sync.dma_start(back_sb[:], back)
 
         xs = keep.tile([P, S], U8, align_bytes=64)
         nc.vector.tensor_copy(xs[:], xs_all[:].indirect(offs_sb[:]))
-        xw = keep.tile([P, S], U32, align_bytes=64)
-        nc.vector.tensor_copy(xw[:], xw_all[:].bitcast(U32).indirect(offs_sb[:]))
 
         w1_bf = keep.tile([P, H * PLANES], BF16, align_bytes=64)
         w1_dealt = w1_bf[:].rearrange("p (t m j) -> p m j t", t=PLANES, j=PLANES)
         w1_cols = w1_raw[:].rearrange("p j (m t) -> p m j t", t=PLANES)
         w1_codes = keep.tile([P, H], U32, align_bytes=64)
         w1_scales = keep.tile([P, H], U8, align_bytes=64)
-
-        def round_w1(t0, t1, split):
-            on_scalar(out=w1_dealt[:, 0:split, :, t0:t1], in_=w1_cols[:, 0:split, :, t0:t1])
-            on_vector(out=w1_dealt[:, split:P, :, t0:t1], in_=w1_cols[:, split:P, :, t0:t1])
 
         def quantise_w1(t0, t1):
             nc.vector.quantize_mx(
@@ -104,63 +99,63 @@ def tile_picked_tome8_silu_po_kernel(
                 in_=w1_bf[:, t0 * P * PLANES : t1 * P * PLANES],
             )
 
-        round_w1(0, 2, W1_SCALAR_COLS[0])
-        quantise_w1(0, 1)
-        quantise_w1(1, 2)
-        round_w1(2, 4, W1_SCALAR_COLS[1])
+        on_scalar(out=w1_dealt[:, :, :, 0:2], in_=w1_cols[:, :, :, 0:2])
+        on_vector(out=w1_dealt[:, :, :, 2:4], in_=w1_cols[:, :, :, 2:4])
+        quantise_w1(0, 2)
         quantise_w1(2, 4)
 
-        wb_sb = keep.tile([P, V], F32)
-        nc.scalar.activation(wb_sb[:], wa_sb[:], ACT.Copy, bias=1.0, scale=-1.0)
-
+        xw = keep.tile([P, S], U32, align_bytes=64)
         y = [keep.tile([P, S], F32, name="y%d" % t) for t in range(PLANES)]
-        plane0_copies = (on_scalar, on_vector, on_vector, on_scalar)
-        for t in range(PLANES):
-            cols = slice(t * P, (t + 1) * P)
-            j0 = 0
-            for i, width in enumerate(PLANE0_PASSES if t == 0 else (BANK, BANK)):
-                picked = slice(j0, j0 + width)
-                if t == 0:
-                    acc = psum_mix.tile([P, BANK], F32, name="summed%d" % i)
-                else:
-                    acc = psum.tile([P, BANK], F32, name="acc%d" % (2 * (1 - t % 2) + i))
-                nc.tensor.matmul_mx(
-                    out=acc[:, 0:width],
-                    lhsT=w1_codes[:, cols].bitcast(FP8X4),
-                    lhsT_scale=w1_scales[:, cols],
-                    rhs=xw[:, picked].bitcast(FP8X4),
-                    rhs_scale=xs[:, picked],
-                    start=True,
-                    stop=True,
-                )
-                engine_copy = plane0_copies[i] if t == 0 else on_scalar
-                engine_copy(out=y[t][:, picked], in_=acc[:, 0:width])
-                j0 = j0 + width
+        passes = []
 
-        w2_codes = keep.tile([P, N], U32, align_bytes=64)
-        on_vector(
-            out=w2_codes[:].rearrange("p (t m) -> p m t", t=PLANES),
-            in_=w2w_raw[:].bitcast(U32).rearrange("p (m t) -> p m t", t=PLANES),
-        )
+        def first_product(t, j0, width):
+            acc = bank(len(passes) % 8, width)
+            passes.append(acc)
+            cols, picked = slice(t * P, (t + 1) * P), slice(j0, j0 + width)
+            nc.tensor.matmul_mx(
+                out=acc[:],
+                lhsT=w1_codes[:, cols].bitcast(FP8X4),
+                lhsT_scale=w1_scales[:, cols],
+                rhs=xw[:, picked].bitcast(FP8X4),
+                rhs_scale=xs[:, picked],
+                start=True,
+                stop=True,
+            )
+            on_scalar(out=y[t][:, picked], in_=acc[:])
+
+        j0 = 0
+        for i, width in enumerate(PIECES):
+            on_vector(xw[:, j0 : j0 + width], xw_all[:].bitcast(U32).indirect(offs_sb[:, j0 // 16 : (j0 + width) // 16]))
+            first_product(0, j0, width)
+            if i < 2:
+                first_product(1, j0, width)
+            j0 = j0 + width
+        first_product(1, 2 * CHUNK, CHUNK)
+        first_product(1, 3 * CHUNK, CHUNK)
+        for t in (2, 3):
+            first_product(t, 0, BANK)
+            first_product(t, BANK, BANK)
+
         w2_sc = keep.tile([P, N], U8, align_bytes=64)
         on_vector(
             out=w2_sc[:].rearrange("p (t m) -> p t m", t=PLANES),
             in_=w2s_raw[:].rearrange("p (m t) -> p t m", t=PLANES),
         )
+        wb_sb = keep.tile([P, V], F32)
+        nc.vector.tensor_scalar(wb_sb[:], wa_sb[:], -1.0, 1.0, ALU.mult, ALU.add)
 
-        y_late = keep.tile([P, PLANES, 5 * STRIP], F32)
+        y_late = keep.tile([P, PLANES, 2 * CHUNK], F32)
         for t in range(PLANES):
-            nc.sync.dma_start(out=y_late[:, t, :], in_=y[t][:, CHUNK : S - STRIP])
+            nc.sync.dma_start(out=y_late[:, t, :], in_=y[t][:, CHUNK : 3 * CHUNK])
 
         c0, c1, c2, c3 = (c * CHUNK for c in range(4))
         c0b, c1b, c2b, c3b = (c + STRIP for c in (c0, c1, c2, c3))
         mg = [keep.tile([P, V], F32, name="mg%d" % t) for t in range(PLANES)]
-        stage1 = keep.tile([P, 7 * CHUNK], F32)
-        stage2 = keep.tile([P, 4 * CHUNK], F32)
-        home1 = stage1[:, CHUNK : 5 * CHUNK].rearrange("p (t j) -> p t j", t=PLANES)
-        home3a = stage1[:, 3 * CHUNK : 7 * CHUNK].rearrange("p (t j) -> p t j", t=PLANES)[:, :, 0:STRIP]
-        home3b = stage1[:, 5 * CHUNK : 7 * CHUNK].rearrange("p (t j) -> p t j", t=PLANES)
-        home2 = stage2[:].rearrange("p (t j) -> p t j", t=PLANES)
+        stage = keep.tile([P, PLANES, V], F32)
+        home2, home1 = stage[:, :, 0:CHUNK], stage[:, :, CHUNK:V]
+        second0 = keep.tile([P, V], F32, align_bytes=64)
+        seconds = (second0[:], stage[:, 0, :], stage[:, 1, :])
+        halves = (slice(0, HALF), slice(HALF, V))
 
         def looked_up(t, j0, width):
             return mg[t][:].indirect(back_sb[:, j0 // 16 : (j0 + width) // 16])
@@ -169,77 +164,78 @@ def tile_picked_tome8_silu_po_kernel(
             for t in planes:
                 nc.scalar.activation(home[:, t, :], looked_up(t, j0, home.shape[2]), ACT.Copy)
 
-        def take_part(t, which, part):
-            offsets, weight = ((a1_sb, wa_sb), (a2_sb, wb_sb))[which]
-            nc.vector.tensor_tensor(part, y[t][:].indirect(offsets[:]), weight[:], ALU.mult)
+        def second_part(t, part, h):
+            offsets = a2_sb[:, h * HALF // 16 : (h + 1) * HALF // 16]
+            nc.vector.tensor_tensor(part[:, halves[h]], y[t][:].indirect(offsets), wb_sb[:, halves[h]], ALU.mult)
 
-        HALF = V // 2
-        halves = (slice(0, HALF), slice(HALF, V))
-        second0 = keep.tile([P, V], F32)
-        seconds = (second0[:], stage1[:, 0:V], stage1[:, V : 2 * V])
-        last_turned = {1: home2[:, 0, :], 2: mg[LAST][:, P // 2 : P // 2 + HALF]}
-        sum_banks = ((psum_mix, "summed0"), (psum_mix, "summed1"), (psum_mix, "summed2"), (psum_mix, "summed3"))
-        sum_banks = sum_banks + ((psum, "acc0"), (psum, "acc1"))
+        def add_turned(summed, part, h, opens):
+            for i in range(2):
+                block = part[:, h * HALF + i * P : h * HALF + (i + 1) * P]
+                nc.tensor.matmul(
+                    summed[:, i * P : (i + 1) * P],
+                    block,
+                    ident[:],
+                    start=opens and i == 0,
+                    stop=not opens and i == 1,
+                    is_transpose=True,
+                )
+
+        w2_codes = None
         for t in range(LAST):
-            order = (1, 0) if t == 2 else (0, 1)
             first = keep.tile([P, V], F32, name="first%d" % t)
-            take_part(t, 0, first[:])
-            summed = {}
-            for n, h in enumerate(order):
-                pool, tag = sum_banks[2 * t + n]
-                summed[h] = pool.tile([P, HALF], F32, name=tag)
-                for i in range(2):
-                    block = first[:, (2 * h + i) * P : (2 * h + i + 1) * P]
-                    nc.tensor.matmul(
-                        summed[h][:, i * P : (i + 1) * P], block, ident[:], start=i == 0, stop=False, is_transpose=True
-                    )
-            take_part(t, 1, seconds[t])
-            turned_tile = keep.tile([P, V], F32, name="turned%d" % t)
-            turned = {h: turned_tile[:, halves[h]] for h in order}
-            turned[order[1]] = last_turned.get(t, turned[order[1]])
-            for h in order:
-                for i in range(2):
-                    block = seconds[t][:, (2 * h + i) * P : (2 * h + i + 1) * P]
-                    nc.tensor.matmul(
-                        summed[h][:, i * P : (i + 1) * P], block, ident[:], start=False, stop=i == 1, is_transpose=True
-                    )
+            nc.vector.tensor_tensor(first[:], y[t][:].indirect(a1_sb[:]), wa_sb[:], ALU.mult)
+            summed = [bank(5 + h, HALF) for h in range(2)]
+            for h in range(2):
+                add_turned(summed[h], first, h, True)
+            second = seconds[t]
+            turned = [mg[LAST][:, halves[(h + t) % 2]] for h in range(2)]
+            for h in range(2):
+                second_part(t, second, h)
+                add_turned(summed[h], second, h, False)
                 nc.scalar.activation(turned[h], summed[h][:], ACT.Silu)
-            if t > 0:
-                fetch(home1, c1, (t - 1,))
-            for n, h in enumerate(order):
-                back_turned = psum.tile([P, HALF], F32, name="acc%d" % (2 + n))
+                if t > 0 and h == 0:
+                    fetch(home2, c2, (t - 1,))
+                if t > 0 and h == 1:
+                    fetch(home1, c1, (t - 1,))
+            if t == 0:
+                w2_codes = keep.tile([P, N], U32, tag="second0", align_bytes=64)
+                on_scalar(
+                    out=w2_codes[:].rearrange("p (t m) -> p m t", t=PLANES),
+                    in_=w2w_raw[:].bitcast(U32).rearrange("p (m t) -> p m t", t=PLANES),
+                )
+            for h in range(2):
+                back_turned = bank((7, 0)[h], HALF)
                 for i in range(2):
                     nc.tensor.transpose(back_turned[:, i * P : (i + 1) * P], turned[h][:, i * P : (i + 1) * P], ident[:])
                 on_scalar(out=mg[t][:, halves[h]], in_=back_turned[:])
-            if t == 1:
-                fetch(home2, c2, (0,))
 
         first = keep.tile([P, V], F32)
-        take_part(LAST, 0, first[:])
+        nc.vector.tensor_tensor(first[:], y[LAST][:].indirect(a1_sb[:]), wa_sb[:], ALU.mult)
         second = keep.tile([P, V], F32)
-        totals = (stage2[:, 3 * STRIP : 5 * STRIP], stage1[:, 5 * CHUNK + STRIP // 2 : 6 * CHUNK + STRIP // 2])
-        for h, cols in enumerate(halves):
-            offsets = a2_sb[:, h * HALF // 16 : (h + 1) * HALF // 16]
-            nc.vector.tensor_tensor(second[:, cols], y[LAST][:].indirect(offsets), wb_sb[:, cols], ALU.mult)
-        for h, cols in enumerate(halves):
-            nc.vector.tensor_tensor(totals[h], first[:, cols], second[:, cols], ALU.add)
-        for h, cols in enumerate(halves):
-            nc.scalar.activation(mg[LAST][:, cols], totals[h], ACT.Silu)
+        nc.vector.tensor_tensor(second[:], y[LAST][:].indirect(a2_sb[:]), wb_sb[:], ALU.mult)
+        total = keep.tile([P, V], F32)
+        nc.vector.tensor_tensor(total[:], first[:], second[:], ALU.add)
+        fetch(home1, c1, (2,))
+        nc.scalar.activation(mg[LAST][:], total[:], ACT.Silu)
+        home3a = home1[:, :, 0:STRIP]
+        home3b = total[:].rearrange("p (t j) -> p t j", t=PLANES)
+        home0 = keep.tile([P, PLANES, CHUNK], F32)
 
         z_codes = keep.tile([P, S], U32, align_bytes=64)
         z_scales = keep.tile([P, S], U8, align_bytes=64)
         o_scales = keep.tile([P, S], U8, align_bytes=64)
         o_codes = keep.tile([P, S], I32, align_bytes=64)
-        zw = keep.tile([P, S * PLANES], BF16, align_bytes=64)
-        ow = keep.tile([P, S * PLANES], BF16, align_bytes=64)
+        zw = [keep.tile([P, CHUNK * PLANES], BF16, name="zw%d" % c, align_bytes=64) for c in range(4)]
+        ow = {}
         res = [keep.tile([P, PLANES, CHUNK], F32, name="res%d" % c) for c in range(4)]
         out_rows = out_0.rearrange("(p t) j -> p t j", t=PLANES)
         out_words = out_1[0].rearrange("p c r -> p (c r)").bitcast(I32)
         banks = {}
-        free_banks = sum_banks + ((psum, "acc2"), (psum, "acc3"))
 
         def woven(tile, j0, width):
-            return tile[:, j0 * PLANES : (j0 + width) * PLANES]
+            if tile is zw:
+                return zw[j0 // CHUNK][:, j0 % CHUNK * PLANES : (j0 % CHUNK + width) * PLANES]
+            return ow[j0 // BANK][:, j0 % BANK * PLANES : (j0 % BANK + width) * PLANES]
 
         def unmerge(home, j0, t, first=0, width=CHUNK):
             j = j0 + first
@@ -270,8 +266,7 @@ def tile_picked_tome8_silu_po_kernel(
             per_bank = per_bank or BANK // span
             for s0 in range(j0, j0 + width, span):
                 for t0 in range(0, PLANES, per_bank):
-                    pool, tag = free_banks[len(banks) % len(free_banks)]
-                    acc = pool.tile([P, per_bank, span], F32, name=tag)
+                    acc = bank((1 + len(banks)) % 8, per_bank, span)
                     banks[s0, t0] = acc
                     for i in range(per_bank):
                         rows = slice((t0 + i) * P, (t0 + i + 1) * P)
@@ -309,64 +304,53 @@ def tile_picked_tome8_silu_po_kernel(
         def store_words(j0, width):
             nc.sync.dma_start(out=out_words[:, j0 : j0 + width], in_=o_codes[:, j0 : j0 + width])
 
-        home0 = keep.tile([P, PLANES, CHUNK], F32, tag="wb_sb")
-        fetch(home1, c1, (2,))
+        def leave(j0, width):
+            for t0 in range(0, PLANES, BANK // width):
+                empty(j0, t0)
+                store(j0, width, t0, BANK // width)
+
+        def round_bank(j0):
+            weave(on_scalar, banks[j0, 0][:], woven(ow, j0, STRIP))
+
         fetch(home1, c1, (3,))
-        fetch(home2, c2, (1,))
-        fetch(home2, c2, (2,))
-        fetch(home2, c2, (3,))
-        unmerge(home0, c0, 0)
-        unmerge(home0, c0, 1)
-        unmerge(home0, c0, 2)
-        unmerge(home0, c0, 3)
+        fetch(home2, c2, (2, 3))
+        for t in range(PLANES):
+            unmerge(home0, c0, t)
         unmerge(home3b, c3b, 0, 0, STRIP)
+        weave(on_vector, home0[:], woven(zw, c0, CHUNK))
         unmerge(home3b, c3b, 1, 0, STRIP)
-        weave(on_vector, home0[:, :, 0 : 0 + CHUNK], woven(zw, c0, CHUNK))
-        add_weave(home1, c1, 0, STRIP)
-        fetch(home3a, c3, (0, 1))
         multiply(c0, CHUNK, CHUNK)
-        add_weave(home1, c1, STRIP, STRIP)
+        add_weave(home1, c1, 0, CHUNK)
         unmerge(home3b, c3b, 2, 0, STRIP)
-        unmerge(home3b, c3b, 3, 0, STRIP)
         multiply(c1, CHUNK, CHUNK)
-        weave(on_vector, home3b, woven(zw, c3b, STRIP))
-        add_weave(home2, c2, 0, STRIP)
-        multiply(c3b, STRIP, STRIP)
-        add_weave(home2, c2, STRIP, STRIP)
-        empty(c0, 0, on_scalar)
-        store(c0, CHUNK, 0, 2)
-        empty(c0, 2, on_scalar)
-        store(c0, CHUNK, 2, 2)
-        fetch(home3a, c3, (2,))
-        empty(c1, 0, on_scalar)
-        store(c1, CHUNK, 0, 2)
-        fetch(home3a, c3, (3,))
-        empty(c1, 2, on_scalar)
-        store(c1, CHUNK, 2, 2)
-        empty(c3b, 0, on_scalar)
-        store(c3b, STRIP)
-        round_result(on_vector, c0b, STRIP)
+        add_weave(home2, c2, 0, CHUNK)
+        unmerge(home3b, c3b, 3, 0, STRIP)
         multiply(c2, CHUNK, CHUNK)
-        add_weave(home3a, c3, 0, STRIP)
-        round_result(on_scalar, c0, STRIP)
-        round_result(on_vector, c1, STRIP)
+        for t in range(PLANES):
+            unmerge(home3a, c3, t, 0, STRIP)
+        weave(on_vector, home3b, woven(zw, c3b, STRIP))
+        weave(on_vector, home3a, woven(zw, c3, STRIP))
+        multiply(c3b, STRIP, STRIP)
         multiply(c3, STRIP, STRIP)
-        empty(c2, 0, on_scalar)
-        store(c2, CHUNK, 0, 2)
-        empty(c2, 2, on_scalar)
-        store(c2, CHUNK, 2, 2)
-        round_result(on_vector, c1b, STRIP)
-        round_result(on_vector, c3b, STRIP)
-        empty(c3, 0, on_scalar)
-        store(c3, STRIP)
+        ow[0] = keep.tile([P, BANK * PLANES], BF16, tag="zw2", align_bytes=64, name="ow0")
+        ow[1] = keep.tile([P, BANK * PLANES], BF16, align_bytes=64, name="ow1")
+        leave(c0, CHUNK)
+        leave(c1, CHUNK)
+        round_result(on_scalar, c0, STRIP)
+        leave(c2, CHUNK)
+        round_result(on_scalar, c0b, STRIP)
+        leave(c3b, STRIP)
+        round_bank(c3)
+        leave(c3, STRIP)
+        round_result(on_vector, c1, CHUNK)
+        round_result(on_vector, c2, CHUNK)
         hand_on(c0, 512)
         store_words(c0, 512)
-        round_result(on_scalar, c2b, STRIP)
-        round_result(on_vector, c2, STRIP)
-        round_result(on_vector, c3, STRIP)
+        round_result(on_vector, c3b, STRIP)
         hand_on(c2, CHUNK)
+        store_words(c2, CHUNK)
         hand_on(c3, CHUNK)
-        store_words(c2, 512)
+        store_words(c3, CHUNK)
 
         for r in range(4):
             in_sbuf, in_hbm = scale_rows(o_scales, out_2, r)

@@ -144,9 +144,9 @@ def tile_picked_tome8_silu_po_kernel(
         wb_sb = keep.tile([P, V], F32)
         nc.vector.tensor_scalar(wb_sb[:], wa_sb[:], -1.0, 1.0, ALU.mult, ALU.add)
 
-        y_late = keep.tile([P, PLANES, 2 * CHUNK], F32)
+        y_late = keep.tile([P, PLANES, 5 * STRIP], F32)
         for t in range(PLANES):
-            nc.sync.dma_start(out=y_late[:, t, :], in_=y[t][:, CHUNK : 3 * CHUNK])
+            nc.sync.dma_start(out=y_late[:, t, :], in_=y[t][:, CHUNK : S - STRIP])
 
         c0, c1, c2, c3 = (c * CHUNK for c in range(4))
         c0b, c1b, c2b, c3b = (c + STRIP for c in (c0, c1, c2, c3))
@@ -156,6 +156,14 @@ def tile_picked_tome8_silu_po_kernel(
         second0 = keep.tile([P, V], F32, align_bytes=64)
         seconds = (second0[:], stage[:, 0, :], stage[:, 1, :])
         halves = (slice(0, HALF), slice(HALF, V))
+        early = keep.tile([P, PLANES * STRIP], F32)
+        home3a = early[:].rearrange("p (t j) -> p t j", t=PLANES)
+        late = keep.tile([P, HALF + PLANES * CHUNK], F32)
+        home3b = late[:, 0 : PLANES * STRIP].rearrange("p (t j) -> p t j", t=PLANES)
+        home0 = late[:, HALF:].rearrange("p (t j) -> p t j", t=PLANES)
+        totals = (early[:, STRIP : STRIP + HALF], late[:, 0:HALF])
+        blocks = mg[LAST][:].rearrange("p (b j) -> p b j", j=P)
+        parked = (blocks[:, 0:BLOCKS:LAST, :], blocks[:, 1:LAST, :])
 
         def looked_up(t, j0, width):
             return mg[t][:].indirect(back_sb[:, j0 // 16 : (j0 + width) // 16])
@@ -188,11 +196,11 @@ def tile_picked_tome8_silu_po_kernel(
             for h in range(2):
                 add_turned(summed[h], first, h, True)
             second = seconds[t]
-            turned = [mg[LAST][:, halves[(h + t) % 2]] for h in range(2)]
+            turned = [parked[(h + t) % 2] for h in range(2)]
             for h in range(2):
                 second_part(t, second, h)
                 add_turned(summed[h], second, h, False)
-                nc.scalar.activation(turned[h], summed[h][:], ACT.Silu)
+                nc.scalar.activation(turned[h], summed[h][:].rearrange("p (b j) -> p b j", j=P), ACT.Silu)
                 if t > 0 and h == 0:
                     fetch(home2, c2, (t - 1,))
                 if t > 0 and h == 1:
@@ -206,20 +214,20 @@ def tile_picked_tome8_silu_po_kernel(
             for h in range(2):
                 back_turned = bank((7, 0)[h], HALF)
                 for i in range(2):
-                    nc.tensor.transpose(back_turned[:, i * P : (i + 1) * P], turned[h][:, i * P : (i + 1) * P], ident[:])
+                    nc.tensor.transpose(back_turned[:, i * P : (i + 1) * P], turned[h][:, i, :], ident[:])
                 on_scalar(out=mg[t][:, halves[h]], in_=back_turned[:])
+            if t == 0:
+                fetch(home3a, c3, (0,))
 
         first = keep.tile([P, V], F32)
         nc.vector.tensor_tensor(first[:], y[LAST][:].indirect(a1_sb[:]), wa_sb[:], ALU.mult)
         second = keep.tile([P, V], F32)
-        nc.vector.tensor_tensor(second[:], y[LAST][:].indirect(a2_sb[:]), wb_sb[:], ALU.mult)
-        total = keep.tile([P, V], F32)
-        nc.vector.tensor_tensor(total[:], first[:], second[:], ALU.add)
-        fetch(home1, c1, (2,))
-        nc.scalar.activation(mg[LAST][:], total[:], ACT.Silu)
-        home3a = home1[:, :, 0:STRIP]
-        home3b = total[:].rearrange("p (t j) -> p t j", t=PLANES)
-        home0 = keep.tile([P, PLANES, CHUNK], F32)
+        for h in range(2):
+            second_part(LAST, second, h)
+        for h in range(2):
+            nc.vector.tensor_tensor(totals[h], first[:, halves[h]], second[:, halves[h]], ALU.add)
+        for h in range(2):
+            nc.scalar.activation(mg[LAST][:, halves[h]], totals[h], ACT.Silu)
 
         z_codes = keep.tile([P, S], U32, align_bytes=64)
         z_scales = keep.tile([P, S], U8, align_bytes=64)
@@ -312,12 +320,13 @@ def tile_picked_tome8_silu_po_kernel(
         def round_bank(j0):
             weave(on_scalar, banks[j0, 0][:], woven(ow, j0, STRIP))
 
-        fetch(home1, c1, (3,))
+        fetch(home1, c1, (2, 3))
         fetch(home2, c2, (2, 3))
+        fetch(home3a, c3, (1, 2, 3))
         for t in range(PLANES):
             unmerge(home0, c0, t)
         unmerge(home3b, c3b, 0, 0, STRIP)
-        weave(on_vector, home0[:], woven(zw, c0, CHUNK))
+        weave(on_vector, home0, woven(zw, c0, CHUNK))
         unmerge(home3b, c3b, 1, 0, STRIP)
         multiply(c0, CHUNK, CHUNK)
         add_weave(home1, c1, 0, CHUNK)
@@ -326,26 +335,24 @@ def tile_picked_tome8_silu_po_kernel(
         add_weave(home2, c2, 0, CHUNK)
         unmerge(home3b, c3b, 3, 0, STRIP)
         multiply(c2, CHUNK, CHUNK)
-        for t in range(PLANES):
-            unmerge(home3a, c3, t, 0, STRIP)
         weave(on_vector, home3b, woven(zw, c3b, STRIP))
-        weave(on_vector, home3a, woven(zw, c3, STRIP))
+        add_weave(home3a, c3, 0, STRIP)
         multiply(c3b, STRIP, STRIP)
         multiply(c3, STRIP, STRIP)
-        ow[0] = keep.tile([P, BANK * PLANES], BF16, tag="zw2", align_bytes=64, name="ow0")
+        ow[0] = keep.tile([P, BANK * PLANES], BF16, align_bytes=64, name="ow0")
         ow[1] = keep.tile([P, BANK * PLANES], BF16, align_bytes=64, name="ow1")
         leave(c0, CHUNK)
-        leave(c1, CHUNK)
         round_result(on_scalar, c0, STRIP)
-        leave(c2, CHUNK)
+        leave(c1, CHUNK)
         round_result(on_scalar, c0b, STRIP)
+        leave(c2, CHUNK)
         leave(c3b, STRIP)
         round_bank(c3)
         leave(c3, STRIP)
         round_result(on_vector, c1, CHUNK)
-        round_result(on_vector, c2, CHUNK)
         hand_on(c0, 512)
         store_words(c0, 512)
+        round_result(on_vector, c2, CHUNK)
         round_result(on_vector, c3b, STRIP)
         hand_on(c2, CHUNK)
         store_words(c2, CHUNK)

@@ -144,24 +144,22 @@ def tile_picked_tome8_silu_po_kernel(
         wb_sb = keep.tile([P, V], F32)
         nc.vector.tensor_scalar(wb_sb[:], wa_sb[:], -1.0, 1.0, ALU.mult, ALU.add)
 
-        y_late = keep.tile([P, PLANES, 5 * STRIP], F32)
-        for t in range(PLANES):
-            nc.sync.dma_start(out=y_late[:, t, :], in_=y[t][:, CHUNK : S - STRIP])
-
         c0, c1, c2, c3 = (c * CHUNK for c in range(4))
-        c0b, c1b, c2b, c3b = (c + STRIP for c in (c0, c1, c2, c3))
+        b1 = c1
+        widths = {c: CHUNK for c in (c0, c1, c2, c3)}
+        y_late = keep.tile([P, PLANES, S - c1], F32)
+        home3 = keep.tile([P, PLANES, CHUNK], F32)
+        totals = (home3[:, 2, :], home3[:, 1, :])
+        for t in range(PLANES):
+            nc.sync.dma_start(out=y_late[:, t, :], in_=y[t][:, c1:S])
+
         mg = [keep.tile([P, V], F32, name="mg%d" % t) for t in range(PLANES)]
         stage = keep.tile([P, PLANES, V], F32)
         home2, home1 = stage[:, :, 0:CHUNK], stage[:, :, CHUNK:V]
         second0 = keep.tile([P, V], F32, align_bytes=64)
         seconds = (second0[:], stage[:, 0, :], stage[:, 1, :])
         halves = (slice(0, HALF), slice(HALF, V))
-        early = keep.tile([P, PLANES * STRIP], F32)
-        home3a = early[:].rearrange("p (t j) -> p t j", t=PLANES)
-        late = keep.tile([P, HALF + PLANES * CHUNK], F32)
-        home3b = late[:, 0 : PLANES * STRIP].rearrange("p (t j) -> p t j", t=PLANES)
-        home0 = late[:, HALF:].rearrange("p (t j) -> p t j", t=PLANES)
-        totals = (early[:, STRIP : STRIP + HALF], late[:, 0:HALF])
+        home0 = keep.tile([P, PLANES, CHUNK], F32)
         blocks = mg[LAST][:].rearrange("p (b j) -> p b j", j=P)
         parked = (blocks[:, 0:BLOCKS:LAST, :], blocks[:, 1:LAST, :])
 
@@ -217,7 +215,7 @@ def tile_picked_tome8_silu_po_kernel(
                     nc.tensor.transpose(back_turned[:, i * P : (i + 1) * P], turned[h][:, i, :], ident[:])
                 on_scalar(out=mg[t][:, halves[h]], in_=back_turned[:])
             if t == 0:
-                fetch(home3a, c3, (0,))
+                fetch(home3, c3, (0,))
 
         first = keep.tile([P, V], F32)
         nc.vector.tensor_tensor(first[:], y[LAST][:].indirect(a1_sb[:]), wa_sb[:], ALU.mult)
@@ -233,17 +231,15 @@ def tile_picked_tome8_silu_po_kernel(
         z_scales = keep.tile([P, S], U8, align_bytes=64)
         o_scales = keep.tile([P, S], U8, align_bytes=64)
         o_codes = keep.tile([P, S], I32, align_bytes=64)
-        zw = [keep.tile([P, CHUNK * PLANES], BF16, name="zw%d" % c, align_bytes=64) for c in range(4)]
-        ow = {}
-        res = [keep.tile([P, PLANES, CHUNK], F32, name="res%d" % c) for c in range(4)]
+        zw = keep.tile([P, S * PLANES], BF16, align_bytes=64)
+        ow = keep.tile([P, S * PLANES], BF16, align_bytes=64)
+        res = {j0: keep.tile([P, PLANES, w], F32, name="res%d" % j0) for j0, w in widths.items()}
         out_rows = out_0.rearrange("(p t) j -> p t j", t=PLANES)
         out_words = out_1[0].rearrange("p c r -> p (c r)").bitcast(I32)
         banks = {}
 
         def woven(tile, j0, width):
-            if tile is zw:
-                return zw[j0 // CHUNK][:, j0 % CHUNK * PLANES : (j0 % CHUNK + width) * PLANES]
-            return ow[j0 // BANK][:, j0 % BANK * PLANES : (j0 % BANK + width) * PLANES]
+            return tile[:, j0 * PLANES : (j0 + width) * PLANES]
 
         def unmerge(home, j0, t, first=0, width=CHUNK):
             j = j0 + first
@@ -256,7 +252,7 @@ def tile_picked_tome8_silu_po_kernel(
             nc.vector.tensor_tensor(
                 woven(zw, j, width).rearrange("p (c i t) -> p c t i", i=4, t=PLANES),
                 home[:, :, first : first + width].rearrange("p t (c i) -> p c t i", i=4),
-                y_late[:, :, j - c1 : j - c1 + width].rearrange("p t (c i) -> p c t i", i=4),
+                y_late[:, :, j - b1 : j - b1 + width].rearrange("p t (c i) -> p c t i", i=4),
                 ALU.add,
             )
 
@@ -289,7 +285,8 @@ def tile_picked_tome8_silu_po_kernel(
                         )
 
         def result(j0, width):
-            return res[j0 // CHUNK][:, :, j0 % CHUNK : j0 % CHUNK + width]
+            piece = max(j for j in widths if j <= j0)
+            return res[piece][:, :, j0 - piece : j0 - piece + width]
 
         def empty(j0, t0=0, engine_copy=on_scalar):
             acc = banks[j0, t0]
@@ -322,42 +319,43 @@ def tile_picked_tome8_silu_po_kernel(
 
         fetch(home1, c1, (2, 3))
         fetch(home2, c2, (2, 3))
-        fetch(home3a, c3, (1, 2, 3))
-        for t in range(PLANES):
+        fetch(home3, c3, (1, 2, 3))
+        for t in range(LAST):
             unmerge(home0, c0, t)
-        unmerge(home3b, c3b, 0, 0, STRIP)
-        weave(on_vector, home0, woven(zw, c0, CHUNK))
-        unmerge(home3b, c3b, 1, 0, STRIP)
+        unmerge(home0, c0, LAST, 0, STRIP)
+        unmerge(home0, c0, LAST, STRIP, STRIP)
+        weave(on_vector, home0[:, :, 0:STRIP], woven(zw, c0, STRIP))
+        weave(on_vector, home0[:, :, STRIP:CHUNK], woven(zw, c0 + STRIP, STRIP))
+        add_weave(home1, c1, 0, STRIP)
         multiply(c0, CHUNK, CHUNK)
-        add_weave(home1, c1, 0, CHUNK)
-        unmerge(home3b, c3b, 2, 0, STRIP)
+        add_weave(home1, c1, STRIP, STRIP)
+        add_weave(home2, c2, 0, STRIP)
         multiply(c1, CHUNK, CHUNK)
-        add_weave(home2, c2, 0, CHUNK)
-        unmerge(home3b, c3b, 3, 0, STRIP)
+        add_weave(home2, c2, STRIP, STRIP)
+        add_weave(home3, c3, 0, STRIP)
         multiply(c2, CHUNK, CHUNK)
-        weave(on_vector, home3b, woven(zw, c3b, STRIP))
-        add_weave(home3a, c3, 0, STRIP)
-        multiply(c3b, STRIP, STRIP)
+        add_weave(home3, c3, STRIP, STRIP)
         multiply(c3, STRIP, STRIP)
-        ow[0] = keep.tile([P, BANK * PLANES], BF16, align_bytes=64, name="ow0")
-        ow[1] = keep.tile([P, BANK * PLANES], BF16, align_bytes=64, name="ow1")
         leave(c0, CHUNK)
-        round_result(on_scalar, c0, STRIP)
+        round_result(on_vector, c0, STRIP)
+        multiply(c3 + STRIP, STRIP, STRIP)
         leave(c1, CHUNK)
-        round_result(on_scalar, c0b, STRIP)
         leave(c2, CHUNK)
-        leave(c3b, STRIP)
-        round_bank(c3)
-        leave(c3, STRIP)
+        empty(c3)
+        empty(c3 + STRIP)
+        store(c3, CHUNK, 0, 2)
+        store(c3, CHUNK, 2, 2)
+        round_bank(c3 + STRIP)
+        round_result(on_vector, c0 + STRIP, STRIP)
         round_result(on_vector, c1, CHUNK)
+        round_result(on_vector, c2, STRIP)
         hand_on(c0, 512)
         store_words(c0, 512)
-        round_result(on_vector, c2, CHUNK)
-        round_result(on_vector, c3b, STRIP)
+        round_result(on_vector, c2 + STRIP, STRIP)
+        round_result(on_vector, c3, STRIP)
         hand_on(c2, CHUNK)
-        store_words(c2, CHUNK)
         hand_on(c3, CHUNK)
-        store_words(c3, CHUNK)
+        store_words(c2, 512)
 
         for r in range(4):
             in_sbuf, in_hbm = scale_rows(o_scales, out_2, r)

@@ -27,6 +27,7 @@ LAST = PLANES - 1
 
 PIECES = (256, 256, 256, 128, 128)
 HALF = V // 2
+EARLY_GROUPS = ((0, 1), (1, 1), (2, 2))
 
 
 def tile_picked_tome8_silu_po_kernel(
@@ -148,13 +149,14 @@ def tile_picked_tome8_silu_po_kernel(
         b1 = c1
         widths = {c: CHUNK for c in (c0, c1, c2, c3)}
         y_late = keep.tile([P, PLANES, S - c1], F32)
-        home3 = keep.tile([P, PLANES, CHUNK], F32)
-        totals = (home3[:, 2, :], home3[:, 1, :])
         for t in range(PLANES):
             nc.sync.dma_start(out=y_late[:, t, :], in_=y[t][:, c1:S])
 
         mg = [keep.tile([P, V], F32, name="mg%d" % t) for t in range(PLANES)]
-        stage = keep.tile([P, PLANES, V], F32)
+        staging = keep.tile([P, PLANES * CHUNK + PLANES * V], F32)
+        stage = staging[:, PLANES * CHUNK :].rearrange("p (t j) -> p t j", t=PLANES)
+        home3 = staging[:, 0 : PLANES * CHUNK].rearrange("p (t j) -> p t j", t=PLANES)
+        totals = (home3[:, 2, :], home3[:, 1, :])
         home2, home1 = stage[:, :, 0:CHUNK], stage[:, :, CHUNK:V]
         second0 = keep.tile([P, V], F32, align_bytes=64)
         seconds = (second0[:], stage[:, 0, :], stage[:, 1, :])
@@ -262,14 +264,17 @@ def tile_picked_tome8_silu_po_kernel(
                 in_=source.rearrange("p t (c i) -> p c t i", i=4),
             )
 
-        def multiply(j0, width, span, per_bank=None):
+        def quantise_z(j0, width):
             cols = slice(j0, j0 + width)
             nc.vector.quantize_mx(
                 out=z_codes[:, cols].bitcast(FP8X4), scales=z_scales[:, cols], in_=woven(zw, j0, width)
             )
-            per_bank = per_bank or BANK // span
+
+        def multiply(j0, width, span, groups=None, quantised=0):
+            quantise_z(j0 + quantised, width - quantised)
+            groups = groups or [(t0, BANK // span) for t0 in range(0, PLANES, BANK // span)]
             for s0 in range(j0, j0 + width, span):
-                for t0 in range(0, PLANES, per_bank):
+                for t0, per_bank in groups:
                     acc = bank((1 + len(banks)) % 8, per_bank, span)
                     banks[s0, t0] = acc
                     for i in range(per_bank):
@@ -310,9 +315,10 @@ def tile_picked_tome8_silu_po_kernel(
             nc.sync.dma_start(out=out_words[:, j0 : j0 + width], in_=o_codes[:, j0 : j0 + width])
 
         def leave(j0, width):
-            for t0 in range(0, PLANES, BANK // width):
-                empty(j0, t0)
-                store(j0, width, t0, BANK // width)
+            for t0 in range(PLANES):
+                if (j0, t0) in banks:
+                    empty(j0, t0)
+                    store(j0, width, t0, banks[j0, t0].shape[1])
 
         def round_bank(j0):
             weave(on_scalar, banks[j0, 0][:], woven(ow, j0, STRIP))
@@ -326,8 +332,9 @@ def tile_picked_tome8_silu_po_kernel(
         unmerge(home0, c0, LAST, STRIP, STRIP)
         weave(on_vector, home0[:, :, 0:STRIP], woven(zw, c0, STRIP))
         weave(on_vector, home0[:, :, STRIP:CHUNK], woven(zw, c0 + STRIP, STRIP))
+        quantise_z(c0, STRIP)
+        multiply(c0, CHUNK, CHUNK, EARLY_GROUPS, STRIP)
         add_weave(home1, c1, 0, STRIP)
-        multiply(c0, CHUNK, CHUNK)
         add_weave(home1, c1, STRIP, STRIP)
         add_weave(home2, c2, 0, STRIP)
         multiply(c1, CHUNK, CHUNK)
@@ -336,17 +343,14 @@ def tile_picked_tome8_silu_po_kernel(
         multiply(c2, CHUNK, CHUNK)
         add_weave(home3, c3, STRIP, STRIP)
         multiply(c3, STRIP, STRIP)
-        leave(c0, CHUNK)
-        round_result(on_vector, c0, STRIP)
         multiply(c3 + STRIP, STRIP, STRIP)
+        leave(c0, CHUNK)
         leave(c1, CHUNK)
         leave(c2, CHUNK)
-        empty(c3)
-        empty(c3 + STRIP)
-        store(c3, CHUNK, 0, 2)
-        store(c3, CHUNK, 2, 2)
+        leave(c3, STRIP)
         round_bank(c3 + STRIP)
-        round_result(on_vector, c0 + STRIP, STRIP)
+        leave(c3 + STRIP, STRIP)
+        round_result(on_vector, c0, CHUNK)
         round_result(on_vector, c1, CHUNK)
         round_result(on_vector, c2, STRIP)
         hand_on(c0, 512)
@@ -354,8 +358,9 @@ def tile_picked_tome8_silu_po_kernel(
         round_result(on_vector, c2 + STRIP, STRIP)
         round_result(on_vector, c3, STRIP)
         hand_on(c2, CHUNK)
+        store_words(c2, CHUNK)
         hand_on(c3, CHUNK)
-        store_words(c2, 512)
+        store_words(c3, CHUNK)
 
         for r in range(4):
             in_sbuf, in_hbm = scale_rows(o_scales, out_2, r)

@@ -90,20 +90,19 @@ def tile_picked_tome8_silu_po_kernel(
         w1_bf = keep.tile([P, H * PLANES], BF16, align_bytes=64)
         w1_dealt = w1_bf[:].rearrange("p (t m j) -> p m j t", t=PLANES, j=PLANES)
         w1_cols = w1_raw[:].rearrange("p j (m t) -> p m j t", t=PLANES)
-        w1_codes = keep.tile([P, H], U32, align_bytes=64)
+        w1_codes = {0: keep.tile([P, H // 2], U32, name="w1_codes0", align_bytes=64)}
         w1_scales = keep.tile([P, H], U8, align_bytes=64)
 
         def quantise_w1(t0, t1):
             nc.vector.quantize_mx(
-                out=w1_codes[:, t0 * P : t1 * P].bitcast(FP8X4),
+                out=w1_codes[t0 // 2][:].bitcast(FP8X4),
                 scales=w1_scales[:, t0 * P : t1 * P],
                 in_=w1_bf[:, t0 * P * PLANES : t1 * P * PLANES],
             )
 
         on_scalar(out=w1_dealt[:, :, :, 0:2], in_=w1_cols[:, :, :, 0:2])
-        on_vector(out=w1_dealt[:, :, :, 2:4], in_=w1_cols[:, :, :, 2:4])
+        on_scalar(out=w1_dealt[:, :, :, 2:4], in_=w1_cols[:, :, :, 2:4])
         quantise_w1(0, 2)
-        quantise_w1(2, 4)
 
         xw = keep.tile([P, S], U32, align_bytes=64)
         y = [keep.tile([P, S], F32, name="y%d" % t) for t in range(PLANES)]
@@ -115,7 +114,7 @@ def tile_picked_tome8_silu_po_kernel(
             cols, picked = slice(t * P, (t + 1) * P), slice(j0, j0 + width)
             nc.tensor.matmul_mx(
                 out=acc[:],
-                lhsT=w1_codes[:, cols].bitcast(FP8X4),
+                lhsT=w1_codes[t // 2][:, t % 2 * P : (t % 2 + 1) * P].bitcast(FP8X4),
                 lhsT_scale=w1_scales[:, cols],
                 rhs=xw[:, picked].bitcast(FP8X4),
                 rhs_scale=xs[:, picked],
@@ -133,6 +132,8 @@ def tile_picked_tome8_silu_po_kernel(
             j0 = j0 + width
         first_product(1, 2 * CHUNK, CHUNK)
         first_product(1, 3 * CHUNK, CHUNK)
+        w1_codes[1] = keep.tile([P, H // 2], U32, name="w1_codes1", tag="xw_all", align_bytes=64)
+        quantise_w1(2, 4)
         for t in (2, 3):
             first_product(t, 0, BANK)
             first_product(t, BANK, BANK)
@@ -332,9 +333,8 @@ def tile_picked_tome8_silu_po_kernel(
         unmerge(home0, c0, LAST, STRIP, STRIP)
         weave(on_vector, home0[:, :, 0:STRIP], woven(zw, c0, STRIP))
         weave(on_vector, home0[:, :, STRIP:CHUNK], woven(zw, c0 + STRIP, STRIP))
-        quantise_z(c0, STRIP)
-        multiply(c0, CHUNK, CHUNK, EARLY_GROUPS, STRIP)
         add_weave(home1, c1, 0, STRIP)
+        multiply(c0, CHUNK, CHUNK, EARLY_GROUPS)
         add_weave(home1, c1, STRIP, STRIP)
         add_weave(home2, c2, 0, STRIP)
         multiply(c1, CHUNK, CHUNK)
@@ -343,14 +343,15 @@ def tile_picked_tome8_silu_po_kernel(
         multiply(c2, CHUNK, CHUNK)
         add_weave(home3, c3, STRIP, STRIP)
         multiply(c3, STRIP, STRIP)
-        multiply(c3 + STRIP, STRIP, STRIP)
         leave(c0, CHUNK)
+        round_result(on_vector, c0, STRIP)
+        multiply(c3 + STRIP, STRIP, STRIP)
         leave(c1, CHUNK)
         leave(c2, CHUNK)
         leave(c3, STRIP)
         round_bank(c3 + STRIP)
         leave(c3 + STRIP, STRIP)
-        round_result(on_vector, c0, CHUNK)
+        round_result(on_vector, c0 + STRIP, STRIP)
         round_result(on_vector, c1, CHUNK)
         round_result(on_vector, c2, STRIP)
         hand_on(c0, 512)

from contextlib import ExitStack

import concourse.mybir as mybir
from concourse.masks import make_identity

K, T, S, V, H, N = 512, 2048, 1024, 512, 512, 512
FLOPS = 2 * K * H * S + 2 * H * N * S

F32 = mybir.dt.float32
BF16 = mybir.dt.bfloat16
I32 = mybir.dt.int32
U32 = mybir.dt.uint32
U16 = mybir.dt.uint16
U8 = mybir.dt.uint8
FP8X4 = mybir.dt.float8_e4m3fn_x4
ALU = mybir.AluOpType
ACT = mybir.ActivationFunctionType

P = 128
PLANES = 4
QUADRANT = 32
BANK = 512
BLOCKS = V // P
CHUNK = 256
STRIP = CHUNK // 2
LAST = PLANES - 1

PIECES = (256, 256, 256, 128, 128)
HALF = V // 2
EARLY_GROUPS = ((0, 1), (1, 1), (2, 2))


def tile_picked_tome8_silu_po_kernel(
    tc, x_words, x_scales, w1, wa, w2_words, w2_scales, offs, a1, a2, back, out_0, out_1, out_2
):
    nc = tc.nc
    on_scalar, on_vector = nc.scalar.copy, nc.vector.tensor_copy
    with ExitStack() as ctx:
        keep = ctx.enter_context(tc.tile_pool(name="keep", bufs=1))
        psum = ctx.enter_context(tc.psum_pool(name="psum", bufs=1))

        def bank(number, *shape):
            return psum.tile([P, *shape], F32, name="bank%d" % number)

        def scale_rows(tile, rows, r):
            return tile[r:P:QUADRANT, :].bitcast(I32), rows[0, r:16:4, :].bitcast(I32)

        def load_scales(tile, rows):
            for r in range(4):
                in_sbuf, in_hbm = scale_rows(tile, rows, r)
                nc.sync.dma_start(out=in_sbuf, in_=in_hbm)

        offs_sb = keep.tile([P, S // 16], U16)
        a1_sb = keep.tile([P, V // 16], U16)
        a2_sb = keep.tile([P, V // 16], U16)
        back_sb = keep.tile([P, S // 16], U16)

        xs_all = keep.tile([P, T], U8, align_bytes=64)
        nc.vector.memset(xs_all[:].bitcast(I32), 0)
        w2s_raw = keep.tile([P, N], U8, align_bytes=64)
        nc.vector.memset(w2s_raw[:].bitcast(I32), 0)
        warm = keep.tile([P, 2], F32)
        nc.vector.memset(warm[:, 0:1], 0.0)
        nc.scalar.activation(warm[:, 1:2], warm[:, 0:1], ACT.Silu)

        ident = keep.tile([P, P], F32)
        nc.vector.memset(ident[:], 0.0)
        make_identity(nc, ident[:], nomemset=True)

        w1_raw = keep.tile([P, PLANES, H], F32)
        xw_all = keep.tile([P, T], I32, align_bytes=64)
        wa_sb = keep.tile([P, V], F32)
        w2w_raw = keep.tile([P, N], I32, align_bytes=64)
        w1_rows = w1.rearrange("(p j) c -> p j c", j=PLANES)
        nc.sync.dma_start(out=w1_raw[:, 0:1, :], in_=w1_rows[:, 0:1, :])
        nc.sync.dma_start(offs_sb[:], offs)
        load_scales(xs_all, x_scales)
        nc.sync.dma_start(out=w1_raw[:, 1:PLANES, :], in_=w1_rows[:, 1:PLANES, :])
        nc.sync.dma_start(out=xw_all[:], in_=x_words[0].rearrange("p c r -> p (c r)").bitcast(I32))
        load_scales(w2s_raw, w2_scales)
        nc.sync.dma_start(a1_sb[:], a1)
        nc.sync.dma_start(a2_sb[:], a2)
        nc.sync.dma_start(out=wa_sb[:], in_=wa.rearrange("(p j) v -> p j v", j=PLANES)[:, 0, :])
        nc.sync.dma_start(out=w2w_raw[:], in_=w2_words[0].rearrange("p c r -> p (c r)").bitcast(I32))
        nc.sync.dma_start(back_sb[:], back)

        xs = keep.tile([P, S], U8, align_bytes=64)
        nc.vector.tensor_copy(xs[:], xs_all[:].indirect(offs_sb[:]))

        w1_bf = keep.tile([P, H * PLANES], BF16, align_bytes=64)
        w1_dealt = w1_bf[:].rearrange("p (t m j) -> p m j t", t=PLANES, j=PLANES)
        w1_cols = w1_raw[:].rearrange("p j (m t) -> p m j t", t=PLANES)
        w1_codes = {0: keep.tile([P, H // 2], U32, name="w1_codes0", align_bytes=64)}
        w1_scales = keep.tile([P, H], U8, align_bytes=64)

        def quantise_w1(t0, t1):
            nc.vector.quantize_mx(
                out=w1_codes[t0 // 2][:].bitcast(FP8X4),
                scales=w1_scales[:, t0 * P : t1 * P],
                in_=w1_bf[:, t0 * P * PLANES : t1 * P * PLANES],
            )

        on_scalar(out=w1_dealt[:, :, :, 0:2], in_=w1_cols[:, :, :, 0:2])
        on_scalar(out=w1_dealt[:, :, :, 2:4], in_=w1_cols[:, :, :, 2:4])
        quantise_w1(0, 2)

        xw = keep.tile([P, S], U32, align_bytes=64)
        y = [keep.tile([P, S], F32, name="y%d" % t) for t in range(PLANES)]
        passes = []

        def first_product(t, j0, width):
            acc = bank(len(passes) % 8, width)
            passes.append(acc)
            cols, picked = slice(t * P, (t + 1) * P), slice(j0, j0 + width)
            nc.tensor.matmul_mx(
                out=acc[:],
                lhsT=w1_codes[t // 2][:, t % 2 * P : (t % 2 + 1) * P].bitcast(FP8X4),
                lhsT_scale=w1_scales[:, cols],
                rhs=xw[:, picked].bitcast(FP8X4),
                rhs_scale=xs[:, picked],
                start=True,
                stop=True,
            )
            on_scalar(out=y[t][:, picked], in_=acc[:])

        j0 = 0
        for i, width in enumerate(PIECES):
            on_vector(xw[:, j0 : j0 + width], xw_all[:].bitcast(U32).indirect(offs_sb[:, j0 // 16 : (j0 + width) // 16]))
            first_product(0, j0, width)
            if i < 2:
                first_product(1, j0, width)
            j0 = j0 + width
        first_product(1, 2 * CHUNK, CHUNK)
        first_product(1, 3 * CHUNK, CHUNK)
        w1_codes[1] = keep.tile([P, H // 2], U32, name="w1_codes1", tag="xw_all", align_bytes=64)
        quantise_w1(2, 4)
        for t in (2, 3):
            first_product(t, 0, BANK)
            first_product(t, BANK, BANK)

        w2_sc = keep.tile([P, N], U8, align_bytes=64)
        on_vector(
            out=w2_sc[:].rearrange("p (t m) -> p t m", t=PLANES),
            in_=w2s_raw[:].rearrange("p (m t) -> p t m", t=PLANES),
        )
        wb_sb = keep.tile([P, V], F32)
        nc.vector.tensor_scalar(wb_sb[:], wa_sb[:], -1.0, 1.0, ALU.mult, ALU.add)

        c0, c1, c2, c3 = (c * CHUNK for c in range(4))
        b1 = c1
        widths = {c: CHUNK for c in (c0, c1, c2, c3)}
        y_late = keep.tile([P, PLANES, S - c1], F32)
        for t in range(PLANES):
            nc.sync.dma_start(out=y_late[:, t, :], in_=y[t][:, c1:S])

        mg = [keep.tile([P, V], F32, name="mg%d" % t) for t in range(PLANES)]
        staging = keep.tile([P, PLANES * CHUNK + PLANES * V], F32)
        stage = staging[:, PLANES * CHUNK :].rearrange("p (t j) -> p t j", t=PLANES)
        home3 = staging[:, 0 : PLANES * CHUNK].rearrange("p (t j) -> p t j", t=PLANES)
        totals = (home3[:, 2, :], home3[:, 1, :])
        home2, home1 = stage[:, :, 0:CHUNK], stage[:, :, CHUNK:V]
        second0 = keep.tile([P, V], F32, align_bytes=64)
        seconds = (second0[:], stage[:, 0, :], stage[:, 1, :])
        halves = (slice(0, HALF), slice(HALF, V))
        home0 = keep.tile([P, PLANES, CHUNK], F32)
        blocks = mg[LAST][:].rearrange("p (b j) -> p b j", j=P)
        parked = (blocks[:, 0:BLOCKS:LAST, :], blocks[:, 1:LAST, :])

        def looked_up(t, j0, width):
            return mg[t][:].indirect(back_sb[:, j0 // 16 : (j0 + width) // 16])

        def fetch(home, j0, planes):
            for t in planes:
                nc.scalar.activation(home[:, t, :], looked_up(t, j0, home.shape[2]), ACT.Copy)

        def second_part(t, part, h):
            offsets = a2_sb[:, h * HALF // 16 : (h + 1) * HALF // 16]
            nc.vector.tensor_tensor(part[:, halves[h]], y[t][:].indirect(offsets), wb_sb[:, halves[h]], ALU.mult)

        def add_turned(summed, part, h, opens):
            for i in range(2):
                block = part[:, h * HALF + i * P : h * HALF + (i + 1) * P]
                nc.tensor.matmul(
                    summed[:, i * P : (i + 1) * P],
                    block,
                    ident[:],
                    start=opens and i == 0,
                    stop=not opens and i == 1,
                    is_transpose=True,
                )

        w2_codes = None
        for t in range(LAST):
            first = keep.tile([P, V], F32, name="first%d" % t)
            nc.vector.tensor_tensor(first[:], y[t][:].indirect(a1_sb[:]), wa_sb[:], ALU.mult)
            summed = [bank(5 + h, HALF) for h in range(2)]
            for h in range(2):
                add_turned(summed[h], first, h, True)
            second = seconds[t]
            turned = [parked[(h + t) % 2] for h in range(2)]
            for h in range(2):
                second_part(t, second, h)
                add_turned(summed[h], second, h, False)
                nc.scalar.activation(turned[h], summed[h][:].rearrange("p (b j) -> p b j", j=P), ACT.Silu)
                if t > 0 and h == 0:
                    fetch(home2, c2, (t - 1,))
                if t > 0 and h == 1:
                    fetch(home1, c1, (t - 1,))
            if t == 0:
                w2_codes = keep.tile([P, N], U32, tag="second0", align_bytes=64)
                on_scalar(
                    out=w2_codes[:].rearrange("p (t m) -> p m t", t=PLANES),
                    in_=w2w_raw[:].bitcast(U32).rearrange("p (m t) -> p m t", t=PLANES),
                )
            for h in range(2):
                back_turned = bank((7, 0)[h], HALF)
                for i in range(2):
                    nc.tensor.transpose(back_turned[:, i * P : (i + 1) * P], turned[h][:, i, :], ident[:])
                on_scalar(out=mg[t][:, halves[h]], in_=back_turned[:])
            if t == 0:
                fetch(home3, c3, (0,))

        first = keep.tile([P, V], F32)
        nc.vector.tensor_tensor(first[:], y[LAST][:].indirect(a1_sb[:]), wa_sb[:], ALU.mult)
        second = keep.tile([P, V], F32)
        for h in range(2):
            second_part(LAST, second, h)
        for h in range(2):
            nc.vector.tensor_tensor(totals[h], first[:, halves[h]], second[:, halves[h]], ALU.add)
        for h in range(2):
            nc.scalar.activation(mg[LAST][:, halves[h]], totals[h], ACT.Silu)

        z_codes = keep.tile([P, S], U32, align_bytes=64)
        z_scales = keep.tile([P, S], U8, align_bytes=64)
        o_scales = keep.tile([P, S], U8, align_bytes=64)
        o_codes = keep.tile([P, S], I32, align_bytes=64)
        zw = keep.tile([P, S * PLANES], BF16, align_bytes=64)
        ow = keep.tile([P, S * PLANES], BF16, align_bytes=64)
        res = {j0: keep.tile([P, PLANES, w], F32, name="res%d" % j0) for j0, w in widths.items()}
        out_rows = out_0.rearrange("(p t) j -> p t j", t=PLANES)
        out_words = out_1[0].rearrange("p c r -> p (c r)").bitcast(I32)
        banks = {}

        def woven(tile, j0, width):
            return tile[:, j0 * PLANES : (j0 + width) * PLANES]

        def unmerge(home, j0, t, first=0, width=CHUNK):
            j = j0 + first
            nc.vector.tensor_tensor(
                home[:, t, first : first + width], looked_up(t, j, width), y[t][:, j : j + width], ALU.add
            )

        def add_weave(home, j0, first=0, width=CHUNK):
            j = j0 + first
            nc.vector.tensor_tensor(
                woven(zw, j, width).rearrange("p (c i t) -> p c t i", i=4, t=PLANES),
                home[:, :, first : first + width].rearrange("p t (c i) -> p c t i", i=4),
                y_late[:, :, j - b1 : j - b1 + width].rearrange("p t (c i) -> p c t i", i=4),
                ALU.add,
            )

        def weave(engine_copy, source, target):
            engine_copy(
                out=target.rearrange("p (c i t) -> p c t i", i=4, t=PLANES),
                in_=source.rearrange("p t (c i) -> p c t i", i=4),
            )

        def quantise_z(j0, width):
            cols = slice(j0, j0 + width)
            nc.vector.quantize_mx(
                out=z_codes[:, cols].bitcast(FP8X4), scales=z_scales[:, cols], in_=woven(zw, j0, width)
            )

        def multiply(j0, width, span, groups=None, quantised=0):
            quantise_z(j0 + quantised, width - quantised)
            groups = groups or [(t0, BANK // span) for t0 in range(0, PLANES, BANK // span)]
            for s0 in range(j0, j0 + width, span):
                for t0, per_bank in groups:
                    acc = bank((1 + len(banks)) % 8, per_bank, span)
                    banks[s0, t0] = acc
                    for i in range(per_bank):
                        rows = slice((t0 + i) * P, (t0 + i + 1) * P)
                        nc.tensor.matmul_mx(
                            out=acc[:, i, :],
                            lhsT=w2_codes[:, rows].bitcast(FP8X4),
                            lhsT_scale=w2_sc[:, rows],
                            rhs=z_codes[:, s0 : s0 + span].bitcast(FP8X4),
                            rhs_scale=z_scales[:, s0 : s0 + span],
                            start=True,
                            stop=True,
                        )

        def result(j0, width):
            piece = max(j for j in widths if j <= j0)
            return res[piece][:, :, j0 - piece : j0 - piece + width]

        def empty(j0, t0=0, engine_copy=on_scalar):
            acc = banks[j0, t0]
            engine_copy(out=result(j0, acc.shape[2])[:, t0 : t0 + acc.shape[1], :], in_=acc[:])

        def store(j0, width, t0=0, planes=PLANES):
            rows = slice(t0, t0 + planes)
            nc.sync.dma_start(out=out_rows[:, rows, j0 : j0 + width], in_=result(j0, width)[:, rows, :])

        def round_result(engine_copy, j0, width):
            weave(engine_copy, result(j0, width), woven(ow, j0, width))

        def hand_on(j0, width):
            nc.vector.quantize_mx(
                out=o_codes[:, j0 : j0 + width].bitcast(FP8X4),
                scales=o_scales[:, j0 : j0 + width],
                in_=woven(ow, j0, width),
            )

        def store_words(j0, width):
            nc.sync.dma_start(out=out_words[:, j0 : j0 + width], in_=o_codes[:, j0 : j0 + width])

        def leave(j0, width):
            for t0 in range(PLANES):
                if (j0, t0) in banks:
                    empty(j0, t0)
                    store(j0, width, t0, banks[j0, t0].shape[1])

        def round_bank(j0):
            weave(on_scalar, banks[j0, 0][:], woven(ow, j0, STRIP))

        fetch(home1, c1, (2, 3))
        fetch(home2, c2, (2, 3))
        fetch(home3, c3, (1, 2, 3))
        for t in range(LAST):
            unmerge(home0, c0, t)
        unmerge(home0, c0, LAST, 0, STRIP)
        unmerge(home0, c0, LAST, STRIP, STRIP)
        weave(on_vector, home0[:, :, 0:STRIP], woven(zw, c0, STRIP))
        weave(on_vector, home0[:, :, STRIP:CHUNK], woven(zw, c0 + STRIP, STRIP))
        add_weave(home1, c1, 0, STRIP)
        multiply(c0, CHUNK, CHUNK, EARLY_GROUPS)
        add_weave(home1, c1, STRIP, STRIP)
        add_weave(home2, c2, 0, STRIP)
        multiply(c1, CHUNK, CHUNK)
        add_weave(home2, c2, STRIP, STRIP)
        add_weave(home3, c3, 0, STRIP)
        multiply(c2, CHUNK, CHUNK)
        add_weave(home3, c3, STRIP, STRIP)
        multiply(c3, STRIP, STRIP)
        leave(c0, CHUNK)
        round_result(on_vector, c0, STRIP)
        multiply(c3 + STRIP, STRIP, STRIP)
        leave(c1, CHUNK)
        leave(c2, CHUNK)
        leave(c3, STRIP)
        round_bank(c3 + STRIP)
        leave(c3 + STRIP, STRIP)
        round_result(on_vector, c0 + STRIP, STRIP)
        round_result(on_vector, c1, CHUNK)
        round_result(on_vector, c2, STRIP)
        hand_on(c0, 512)
        store_words(c0, 512)
        round_result(on_vector, c2 + STRIP, STRIP)
        round_result(on_vector, c3, STRIP)
        hand_on(c2, CHUNK)
        store_words(c2, CHUNK)
        hand_on(c3, CHUNK)
        store_words(c3, CHUNK)

        for r in range(4):
            in_sbuf, in_hbm = scale_rows(o_scales, out_2, r)
            (nc.scalar if r % 2 else nc.sync).dma_start(out=in_hbm, in_=in_sbuf)
